import numpy as np, ml_dtypes
CORES = [113,118,241,246]
N = 4
BF = ml_dtypes.bfloat16
W, L, S, T, F = 2048, 256, 1, 5, 256
C = W >> S
LEVELS = np.array([800, 900, 1000, 1050, 1100, 1150, 1250, 1400])
def parts(rng):
    d = {"key": rng.integers(0, 256, (N, 8, 16, W)), "em": rng.integers(0, 256, (N, 8, 16, W)), "cl": rng.integers(0, W, (N, 8, 16, C)), "pl": rng.integers(0, W, (N, 8, 16, L)),
         "q": rng.integers(0, 256, (N, 8, 16, L)), "emb": rng.integers(0, 256, (N, 8, 16, 16)), "w": rng.integers(0, 256, (N, 8, 16, 1))}
    base = np.stack([rng.permutation(LEVELS) for r in range(N)]).reshape(N, 8, 1, 1)
    d["th"] = base + rng.integers(-100, 101, (N, 8, 16, 1))
    return d
def pack(d):
    kinds = {"key": BF, "em": BF, "cl": np.int32, "pl": np.int32, "q": BF, "emb": BF, "w": BF, "th": np.float32}
    return {k: np.ascontiguousarray(d[k].reshape(N, 128, -1)).astype(np.float32).astype(t) for k, t in kinds.items()}
def setup_inputs(rng):
    return pack(parts(rng))
def setup_inputs_ties(rng):
    d = parts(rng); o = rng.permutation(8)
    for k in ("key", "q", "emb"): d[k] = 64 * rng.integers(0, 4, d[k].shape)
    d["th"] = 64 * rng.integers(16, 23, (N, 8, 16, 1)) + rng.integers(0, 2, (N, 8, 16, 1))
    d["em"] = rng.integers(0, 2, (N, 8, 16, W)) * rng.choice(np.array([1, 3, 255]), (N, 8, 1, 1))
    d["em"][:, o[0]] = 7; d["em"][:, o[1]] = 0
    for k in ("key", "q", "emb"):
        d[k][:, o[2]] = 0
        d[k][:, o[3]] = rng.integers(0, 32, d[k][:, o[3]].shape)
    d["th"][:, o[2], :, 0] = rng.permutation(np.arange(16) % 3)
    d["th"][:, o[3]] = rng.integers(1, 256, (N, 16, 1))
    return pack(d)
def setup_inputs_ends(rng):
    d = parts(rng); o = rng.permutation(8); ends = np.array([0, 1, W - 2, W - 1])
    d["pl"][:, o[0]] = rng.choice(ends, (N, 16, L)); d["th"][:, o[0]] = 4096
    d["th"][:, o[1]] = 0
    d["pl"][:, o[2]] = rng.integers(0, W, (N, 1, L))
    d["cl"][:, o[3]] = rng.choice(ends, (N, 16, C)); d["th"][:, o[3]] = 1000
    d["cl"][:, o[4]] = rng.integers(0, W, (N, 1, C))
    d["key"][:, o[5]] = d["key"][:, o[5]][:, :, :1]
    d["pl"][:, o[6]] = rng.choice(ends, (N, 16, L))
    d["th"][:, o[7]] = 0; d["w"][:, o[7]] = 0
    return pack(d)
def setup_inputs_lone(rng):
    d = parts(rng); d["th"] = np.zeros((N, 8, 16, 1), np.int64)
    for r in range(N):
        o = rng.permutation(8)
        d["th"][r, o[1], 0] = 4096; d["th"][r, o[2], 15] = 4096; d["th"][r, o[3], 14:] = 4096
        for g in o[4:]: d["th"][r, g, rng.integers(1, 15)] = 4096
    d["th"][rng.integers(0, N)] = 0
    return pack(d)
def setup_inputs_big(rng):
    d = parts(rng); o = rng.permutation(8)
    for k in ("key", "em", "q", "emb"): d[k] = 255 * rng.integers(0, 2, d[k].shape)
    d["w"] = rng.integers(254, 256, d["w"].shape)
    d["th"] = rng.choice(np.array([1785, 1786, 2040, 2041, 2295, 1020, 4080, 4081]), (N, 8, 16, 1))
    d["key"][:, o[0]] = 0; d["q"][:, o[0]] = 255; d["emb"][:, o[0]] = 255; d["w"][:, o[0]] = 255
    d["th"][:, o[0], :, 0] = 4080 + np.arange(16) % 2
    d["em"][:, o[1]] = 255
    d["th"][:, o[2]] = 0
    d["th"][:, o[3]] = 0; d["q"][:, o[3]] = 255; d["emb"][:, o[3]] = 255; d["w"][:, o[3]] = 255
    d["em"][:, o[4]] = 255 - (rng.random((N, 16, W)) < 0.0625)
    return pack(d)
def setup_inputs_spread(rng):
    d = parts(rng)
    for k in ("key", "em", "q", "emb"):
        s = d[k].shape
        d[k] = np.minimum((np.exp2(10 * rng.random(s[:2] + (1, s[3]))) * rng.random(s)).astype(np.int64), 255)
    d["w"] = np.minimum(np.exp2(8 * rng.random(d["w"].shape)).astype(np.int64), 255)
    d["th"] = np.minimum(np.exp2(8 + 4 * rng.random((N, 8, 16, 1))).astype(np.int64), 4096)
    for k in ("pl", "cl"): d[k] = np.minimum((W * rng.random(d[k].shape) ** 3).astype(np.int64), W - 1)
    return pack(d)
def check_inputs(d):
    bad = []
    for k, hi in (("key", 255), ("em", 255), ("cl", W - 1), ("pl", W - 1), ("q", 255), ("emb", 255), ("w", 255), ("th", 4096)):
        a = np.asarray(d[k]).astype(np.float64)
        if not np.all((a >= 0) & (a <= hi) & (a == np.floor(a))): bad.append("whole numbers and range of " + k)
    return bad
def reference(key, em, cl, pl, q, emb, w, th):
    def ints(a): return a.astype(np.float32).astype(np.int32).reshape(N, 8, 16, -1)
    K, E, CL, B, H, TH = ints(key), ints(em), ints(cl), ints(emb), ints(w), ints(th)
    p, x = ints(pl), ints(q)
    toks = [[] for r in range(N)]
    for t in range(T):
        pn, xn = [], []
        for r in range(N):
            at = np.take_along_axis(K[r], p[r].reshape(8, 1, 16 * L), 2).reshape(8, 16, 16, L)
            dist = np.add.reduce(np.abs(at - x[r][:, :, None, :]), axis=1)
            near = dist < TH[r]
            first = np.argmax(near, axis=1)
            lead = np.take_along_axis(p[r], first[:, None, :], 1)[:, 0]
            h = np.add.reduce(H[r] * x[r], axis=1)
            c = np.where(np.any(near, axis=1), lead >> S, h & (C - 1))
            pr = np.where(near, p[r], np.take_along_axis(CL[r], c[:, None, :], 2))
            v = np.add.reduce(np.take_along_axis(E[r], pr.reshape(8, 1, 16 * L), 2).reshape(8, 16, 16, L), axis=2)
            tok = np.argmax(v, axis=1)
            toks[r].append(tok)
            xn.append((x[r] + np.take_along_axis(B[r], tok[:, :, None], 1).transpose(0, 2, 1)) >> 1); pn.append(pr)
        p = np.stack([np.concatenate([(pn[(r - 1) % N][..., :F] + (1 if r == 0 else 0)) & (W - 1), (pn[(r + 1) % N][..., F:] - (1 if r == N - 1 else 0)) & (W - 1)], axis=2) for r in range(N)])
        x = np.stack([np.concatenate([xn[(r - 1) % N][..., :F], xn[(r + 1) % N][..., F:]], axis=2) for r in range(N)])
    yt = np.stack([np.concatenate(a, axis=1) for a in toks])
    return {"yp": p.reshape(N, 128, L).astype(np.float32), "yq": x.reshape(N, 128, L).astype(np.float32).astype(BF), "yt": yt.astype(np.float32)}

@@ -1,0 +1,435 @@
+from concourse.mybir import AluOpType, ActivationFunctionType
+from concourse.bass import DstId, RemoteDMATransfer
+
+NR, NB, LB, NT = 4, 4, 64, 5
+NC = 2
+GW = 1024 // NC
+HOP = 40
+LINK = 3200
+
+SCRATCH = {
+    "keyb": ("sbuf", [128, 2064], "bfloat16"), "keys": ("sbuf", [128, 2048], "bfloat16"),
+    "emt": ("sbuf", [128, 2064], "bfloat16"), "clb": ("sbuf", [128, 1032], "int32"),
+    "plb": ("sbuf", [128, 256], "int32"), "qb": ("sbuf", [128, 256], "bfloat16"),
+    "wb": ("sbuf", [128, 1], "bfloat16"), "thf": ("sbuf", [128, 1], "float32"), "eb": ("sbuf", [128, 16], "bfloat16"),
+    "LU": ("sbuf", [128, 1280], "uint16"), "LP": ("sbuf", [128, 1280], "float16"), "LX": ("sbuf", [128, 1280], "float16"),
+    "SU": ("sbuf", [128, 1280], "uint16"), "SP": ("sbuf", [128, 1280], "float16"), "SX": ("sbuf", [128, 1280], "float16"),
+    "SYP": ("sbuf", [128, 256], "float32"), "SYQ": ("sbuf", [128, 256], "bfloat16"),
+    "FYP": ("sbuf", [128, 256], "float32"), "FYQ": ("sbuf", [128, 256], "bfloat16"),
+    "ip": ("sbuf", [128, 256], "int32"), "iq": ("sbuf", [128, 256], "int32"),
+    "ob": ("sbuf", [128, 128], "bfloat16"), "oh": ("sbuf", [128, 64], "float16"), "idb": ("sbuf", [128, 128], "bfloat16"),
+    "idh": ("sbuf", [128, 128], "float16"), "bm": ("sbuf", [128, 128], "bfloat16"), "bm0": ("sbuf", [128, 128], "bfloat16"),
+    "wd": ("sbuf", [128, 144], "bfloat16"), "ub": ("sbuf", [128, 128], "bfloat16"), "u2": ("sbuf", [128, 128], "bfloat16"),
+    "q2": ("sbuf", [128, 128], "bfloat16"), "cnt": ("sbuf", [128, 128], "bfloat16"), "bn": ("sbuf", [128, 128], "bfloat16"),
+    "nk": ("sbuf", [128, 128], "float16"), "n4": ("sbuf", [128, 128], "bfloat16"), "db": ("sbuf", [128, 128], "bfloat16"),
+    "ii": ("sbuf", [128, 1], "int32"), "ik": ("sbuf", [128, 1], "int32"), "io16": ("sbuf", [128, 1], "int32"),
+    "kc": ("sbuf", [128, 1], "float32"), "odd": ("sbuf", [128, 1], "float32"), "even": ("sbuf", [128, 1], "float32"),
+    "vb": ("sbuf", [128, 1], "float32"), "ca0": ("sbuf", [128, 1], "float32"), "ca1": ("sbuf", [128, 1], "float32"),
+    "m0": ("sbuf", [128, 1], "float32"), "thb": ("sbuf", [128, 1], "float32"), "ck": ("sbuf", [128, 1], "float32"),
+    "cn": ("sbuf", [128, 1], "float32"),
+    "zb": ("sbuf", [128, 512], "bfloat16"), "zm": ("sbuf", [128, 512], "float16"),
+    "f10r": ("sbuf", [128, 128], "bfloat16"), "f01r": ("sbuf", [128, 128], "bfloat16"), "fx": ("sbuf", [128, 512], "bfloat16"),
+    "sl": ("sbuf", [128, 128], "bfloat16"), "mk": ("sbuf", [128, 64], "float32"), "wt": ("sbuf", [128, 640], "float16"),
+    "m2": ("sbuf", [128, 32], "float32"), "t2": ("sbuf", [128, 32], "float32"), "et": ("sbuf", [128, 16], "float32"),
+    "tab": ("sbuf", [128, 80], "float32"),
+    "toku": ("sbuf", [128, 80], "uint16"), "tokb": ("sbuf", [128, 80], "bfloat16"), "ytb": ("sbuf", [128, 1280], "float32"),
+}
+for _n, _s, _d in (("kk", [128, 256], "float16"), ("sg", [128, 256], "bfloat16"), ("nn", [128, 256], "bfloat16"),
+                   ("y", [128, 16, 16], "float16"), ("zh", [128, 16, 16], "float16"), ("zt", [128, 16, 32], "float32"),
+                   ("cc", [128, 16], "uint16"), ("cm", [128, 256], "float16"), ("vt", [128, 256], "float32"),
+                   ("sc", [128, 256], "float32"), ("ti", [128, 16], "int32"), ("tv", [128, 16], "bfloat16")):
+    SCRATCH[_n] = ("sbuf", _s, _d)
+for _b in range(NB):
+    SCRATCH.update({
+        "xr%d" % _b: ("sbuf", [128, 1024], "float16"), "df%d" % _b: ("sbuf", [128, 1024], "bfloat16"),
+        "ad%d" % _b: ("sbuf", [128, 1024], "bfloat16"), "eg%d" % _b: ("sbuf", [128, 1024], "bfloat16"),
+        "pa%d" % _b: ("psum", [128, 16, 32], "float32"), "pb%d" % _b: ("psum", [128, 512], "float32"),
+    })
+LOADS = ["pl", "q", "key", "w", "th", "cl", "emb", "em", "keys"]
+SEMAPHORES = (["cv", "cs", "ct", "cg", "sent"] + ["ld_" + n for n in LOADS]
+              + ["ar%d_%d" % (t, b) for t in range(1, NT) for b in range(NB)]
+              + ["ap%d" % b for b in range(NB)] + ["aq%d" % b for b in range(NB)]
+              + ["op%d" % b for b in range(NB)] + ["oq%d" % b for b in range(NB)] + ["oy%d" % k for k in range(3)])
+
+
+def rank_program(g, core, T, topo):
+    rank = T.rank_of(core)
+    if rank is None:
+        return
+    A, F = AluOpType, ActivationFunctionType
+    V, S, P, Y = g.vector, g.scalar, g.tensor, g.sync
+    nxt = T.cores[(rank + 1) % NR]
+    rid, pid = topo.addr(nxt, core)
+    eng = topo.engines(core, nxt)[:8]
+
+    def mask(es):
+        return sum(1 << e for e in es)
+
+    o1 = 1 if rank == 0 else 0
+    ops, seq = [], [0]
+
+    def op(q, dur, emit, R=(), W=(), banks=(), sem=None, val=1, lat=0, skip=False, bias=0):
+        ops.append({"q": q, "dur": dur, "emit": emit, "R": list(R), "W": list(W), "banks": list(banks), "sem": sem, "val": val,
+                    "lat": lat, "skip": skip, "i": len(ops), "bias": bias - 4000 * seq[0]})
+
+    def cyc(n):
+        return max(64, n) + 4
+
+    def load(q, name, fn, W, done, skip=False, bias=0):
+        op(q, 80, fn, (), W, sem="ld_" + name, val=16, lat=done, skip=skip, bias=bias)
+
+    load("Y", "pl", lambda: Y.dma_start(T.plb[:], T.pl[:]), ["plb"], 2300, bias=9e6)
+    load("S", "q", lambda: S.dma_start(T.qb[:], T.q[:]), ["qb"], 2300, bias=9e6)
+    load("Y", "key", lambda: Y.dma_start(T.keyb[:, 0:2048], T.key[:]), ["key"], 4600, bias=8e6)
+    load("S", "w", lambda: S.dma_start(T.wb[:], T.w[:]), ["wb"], 2300, bias=8e6)
+    load("S", "th", lambda: S.dma_start(T.thf[:], T.th[:]), ["thf"], 2300, bias=7e6)
+    load("S", "emb", lambda: S.dma_start(T.eb[:], T.emb[:]), ["eb"], 2300, bias=6e6)
+    load("Y", "cl", lambda: Y.dma_start(T.clb[:, 0:1024], T.cl[:]), ["cl"], 6900, bias=7e6)
+    load("Y", "em", lambda: Y.dma_start(T.emt[:, 0:2048], T.em[:]), ["em"], 9000, bias=6e6)
+    load("Y", "keys", lambda: Y.dma_start(T.keys[:, 0:2047], T.key[:, 1:2048]), ["keys"], 11000, skip=rank != 0, bias=5e6)
+
+    op("V", cyc(256), lambda: V.tensor_copy(T.LU[:, 0:256], T.plb[:]), ["plb"], [("LU", 0, b) for b in range(NB)])
+    op("V", cyc(128), lambda: V.tensor_copy(T.LX[:, 0:256], T.qb[:]), ["qb"], [("LX", 0, b) for b in range(NB)])
+    op("V", cyc(256), lambda: V.tensor_copy(T.LP[:, 0:256], T.plb[:]), ["plb"], [("LP", 0, b) for b in range(NB)])
+    op("V", 68, lambda: V.memset(T.ob[:], 1.0), (), ["ob"])
+
+    def aff(out, src, pat, cmp, base, cm, n):
+        op("G", 180 + 2 * n, lambda: g.affine_select(T[out][:], T[src][:], pat, cmp, 0.0, base, cm), [src], [out])
+
+    aff("bm0", "ob", [[-16, 8], [0, 16]], A.is_ge, 0, 1, 128)
+    aff("bm", "bm0", [[16, 8], [0, 16]], A.is_ge, 15, -1, 128)
+    aff("idb", "ob", [[-1, 128]], A.is_equal, 0, 1, 128)
+    op("G", 140, lambda: g.iota(T.ii[:], [[0, 1]], 0, 1), (), ["ii"])
+    aff("ub", "bm", [[1, 128]], A.is_ge, -1, -1, 128)
+    aff("f10r", "ob", [[1, 128]], A.is_equal, -16, -1, 128)
+    aff("f01r", "ob", [[1, 128]], A.is_equal, 16, -1, 128)
+    aff("sl", "ob", [[-1, 16], [-16, 8]], A.is_equal, 0, 1, 128)
+
+    def ts(out, i, s1, s2, a, b, R, W, n=1):
+        if b is None:
+            op("V", cyc(n), lambda: V.tensor_scalar(out, i, s1, None, a), R, W)
+        else:
+            op("V", cyc(n), lambda: V.tensor_scalar(out, i, s1, s2, a, b), R, W)
+
+    def cp(out, i, R, W, n=1):
+        op("V", cyc(n), lambda: V.tensor_copy(out, i), R, W)
+
+    op("V", 76, lambda: V.memset(T.wd[:], 0.0), (), ["wd"])
+    cp(T.wd[:, 15:128:16], T.bm[:, 0::16], ["bm"], ["wd"])
+    ts(T.ik[:], T.ii[:], 15, None, A.bitwise_and, None, ["ii"], ["ik"])
+    ts(T.io16[:], T.ii[:], 16, None, A.bitwise_and, None, ["ii"], ["io16"])
+    cp(T.kc[:], T.ik[:], ["ik"], ["kc"])
+    ts(T.odd[:], T.io16[:], 0.0625, None, A.mult, None, ["io16"], ["odd"])
+    ts(T.even[:], T.odd[:], -1.0, 1.0, A.mult, A.add, ["odd"], ["even"])
+    ts(T.thb[:], T.thf[:], -0.5, None, A.add, None, ["thf"], ["thb"])
+    cp(T.idh[:], T.idb[:], ["idb"], ["idh"], 64)
+    ts(T.u2[:], T.ub[:], -2048.0, None, A.mult, None, ["ub"], ["u2"], 64)
+    ts(T.q2[:], T.idb[:], 2048.0, None, A.mult, None, ["idb"], ["q2"], 64)
+    op("V", 260, lambda: V.tensor_tensor(T.cnt[:], T.u2[:], T.q2[:], A.add), ["u2", "q2"], ["cnt"])
+    ts(T.bn[:], T.bm[:], -2048.0, None, A.mult, None, ["bm"], ["bn"], 64)
+    ts(T.nk[:], T.idb[:], -2048.0, None, A.mult, None, ["idb"], ["nk"], 64)
+    ts(T.n4[:], T.idb[:], -4096.0, None, A.mult, None, ["idb"], ["n4"], 64)
+    for t in range(NT):
+        ts(T.wt[:, 128 * t:128 * t + 128], T.bm[:], T.wb[:], 2.0 ** (1 - t), A.mult, A.mult, ["bm", "wb"], [("wt", t)], 64)
+    op("P", 64, lambda: P.matmul(T.pb0[:, 511:512], T.bm[:], T.wb[:], True, True), ["bm", "wb"], ["sw"], banks=["b0"])
+    op("V", 68, lambda: V.tensor_scalar(T.ck[:], T.pb0[:, 511:512], -1.0, 1025.0 - 511.5 / 1024, A.mult, A.add), ["sw"], ["ck"],
+       banks=["b0"])
+    op("V", 68, lambda: V.tensor_scalar(T.cn[:], T.pb0[:, 511:512], -2048.0, float(2048 * 1025 + 2 - 32768), A.mult, A.add),
+       ["sw"], ["cn"], banks=["b0"])
+    ts(T.ca0[:], T.kc[:], -2048.0, -2046.0, A.mult, A.add, ["kc"], ["ca0"])
+    op("V", 68, lambda: V.memset(T.zb[:], 0.0), (), ["zb"])
+    cp(T.zb[:, 0:128:32], T.bm[:, 0::32], ["bm"], ["zb"])
+    cp(T.zb[:, 128:256:32], T.bm[:, 16::32], ["bm"], ["zb"])
+    ts(T.m0[:], T.kc[:], 0.0, None, A.is_equal, None, ["kc"], ["m0"])
+    ts(T.zb[:, 256:384:32], T.bm[:, 0::32], T.m0[:], None, A.mult, None, ["bm", "m0"], ["zb"])
+    ts(T.zb[:, 384:512:32], T.bm[:, 16::32], T.m0[:], None, A.mult, None, ["bm", "m0"], ["zb"])
+    cp(T.zm[:], T.zb[:], ["zb"], ["zm"], 256)
+    cp(T.oh[:], T.ob[:, 0:64], ["ob"], ["oh"])
+    ts(T.vb[:], T.kc[:], -0.0625, 0.46875, A.mult, A.add, ["kc"], ["vb"])
+    ts(T.db[:], T.idb[:], T.vb[:], None, A.mult, None, ["idb", "vb"], ["db"], 64)
+    op("V", 68, lambda: V.memset(T.mk[:], 1.0), (), ["mk"])
+    op("V", 68, lambda: V.memset(T.mk[:, 0::16], 0.0), (), ["mk"])
+    fsrc = [("idb", "even"), ("f01r", "odd"), ("f10r", "even"), ("idb", "odd")]
+    for j, (m, c) in enumerate(fsrc):
+        ts(T.fx[:, 128 * j:128 * j + 128], T[m][:], T[c][:], None, A.mult, None, [m, c], [("fx", j)], 64)
+    ts(T.m2[:, 0:16], T.eb[:], T.even[:], None, A.mult, None, ["eb", "even"], ["m2"])
+    ts(T.m2[:, 16:32], T.eb[:], T.odd[:], None, A.mult, None, ["eb", "odd"], ["m2b"])
+    op("V", 68, lambda: V.transpose(T.t2[:], T.m2[:]), ["m2", "m2b"], ["t2"])
+    op("V", 68, lambda: V.tensor_tensor(T.et[:], T.t2[:, 0:16], T.t2[:, 16:32], A.add), ["t2"], ["et"])
+    for t in range(NT):
+        ts(T.tab[:, 16 * t:16 * t + 16], T.et[:], 2047.5 if t == 0 else 1023.5, 2.0 ** t, A.add, A.mult, ["et"], [("tab", t)])
+    ts(T.ca1[:], T.kc[:], -2048.0, -2046.0 + o1, A.mult, A.add, ["kc"], ["ca1"])
+    cp(T.clb[:, 1024:1025], T.clb[:, 0:1], ["cl"], ["clx"])
+    op("S", 80, lambda: S.activation(T.emt[:, 2048:2049], T.emt[:, 0:1], F.Copy), ["em"], ["emx"])
+    op("S", 80, lambda: S.activation(T.keyb[:, 2048:2049], T.keyb[:, 0:1], F.Copy), ["key"], ["keyx"])
+    op("S", 80, lambda: S.activation(T.keys[:, 2047:2048], T.keyb[:, 0:1], F.Copy), ["key", "keys"], ["keysx"], skip=rank != 0)
+
+    def group(ms):
+        def f():
+            last = None
+            for m in ms:
+                last = P.matmul(*m)
+            return last
+        return f
+
+    def arrive(t, b):
+        return "ar%d_%d" % (t, b)
+
+    def yt_out(k, ts_):
+        n = len(ts_)
+        lo, hi = ts_[0], ts_[-1] + 1
+        cp(T.tokb[:, 16 * lo:16 * hi], T.toku[:, 16 * lo:16 * hi], [("tok", t, b) for t in ts_ for b in range(NB)], [("tokb", k)])
+        bk, lastb = T["pa%d" % (NB - 1)], NB - 1
+        op("P", 16 * 64, group([(bk[0:8, 0:8 * n, j::16], T.sl[:, 8 * j:8 * j + 8], T.tokb[:, 16 * lo:16 * hi], True, True)
+                                for j in range(16)]), ["sl", ("tokb", k)], ["ytp"] + [(x, lastb) for x in ("D", "Q", "Z", "TK")],
+           banks=["a%d" % lastb])
+        op("S", 80 + 256 * n, lambda: S.activation(T.ytb[0:8, 256 * lo:256 * hi], bk[0:8, 0:8 * n, :], F.Copy), ["ytp"],
+           [("ytb", k)], banks=["a%d" % lastb])
+        op("Y", 80, lambda: Y.dma_start(T.yt[:, 256 * lo:256 * hi], T.ytb[0:8, 256 * lo:256 * hi]), [("ytb", k)], (),
+           sem="oy%d" % k, val=16, lat=2200)
+
+    for t in range(NT):
+        for b in range(NB):
+            c0 = 256 * t + LB * b
+            seq[0] = t * NB + b
+            cs = slice(c0, c0 + LB)
+            bA, bB = "a%d" % b, "b%d" % b
+            pa, pb = T["pa%d" % b], T["pb%d" % b]
+            D, Q, Z, TK = pa[:, 4:6, :], pa[:, 6:8, :], pa[:, 0:4, :], pa[:, 8, 0:4]
+            H, PA, PN, VT = pb[:, 0:64], pb[:, 64:128], pb[:, 128:192], pb[:, 192:256]
+            xr, df, ad, eg = T["xr%d" % b], T["df%d" % b], T["ad%d" % b], T["eg%d" % b]
+            bl, b4 = slice(LB * b, LB * b + LB), slice(4 * b, 4 * b + 4)
+            kk, sg, nn, cm, vt, sc = [T[n][:, bl] for n in ("kk", "sg", "nn", "cm", "vt", "sc")]
+            y, zh, zt = [T[n][:, b4, :] for n in ("y", "zh", "zt")]
+            cc, ti, tv = [T[n][:, b4] for n in ("cc", "ti", "tv")]
+            shifted = rank == 0 and t > 0
+            if t:
+                op("N", 0, None, [("snd", t - 1, b)], [(n, t, b) for n in ("LU", "LP", "LX")], sem=arrive(t, b), val=8)
+            LU, LP, LX = T.LU[:, cs], T.LP[:, cs], T.LX[:, cs]
+            wt = T.wt[:, 128 * t:128 * t + 128]
+            if t:
+                op("V", cyc(32), lambda xr=xr, LX=LX, t=t: V.tensor_scalar(xr[:, 0::16], LX, 2.0 ** -t, -1024.0, A.mult, A.add),
+                   [("LX", t, b)], [("xr", b, j) for j in range(2)])
+            else:
+                op("V", cyc(32), lambda xr=xr, LX=LX: V.tensor_copy(xr[:, 0::16], LX), [("LX", t, b)],
+                   [("xr", b, j) for j in range(2)])
+            for st in (8, 4, 2):
+                op("V", cyc(256 // st), lambda xr=xr, st=st: V.tensor_copy(xr[:, st::2 * st], xr[:, 0::2 * st]), [("xr", b, 0)],
+                   [("xr", b, 0)])
+            op("V", cyc(256), lambda xr=xr: V.tensor_copy(xr[:, 1::2], xr[:, 0::2]), [("xr", b, 0)], [("xr", b, 1)])
+            for h in range(NC):
+                e = slice(GW * h, GW * h + GW)
+                win = T.keys[:, 0:2048] if shifted else T.keyb[:, 0:2049] if t else T.keyb[:, 0:2048]
+                off = T.LU[:, c0 + GW // 16 * h:c0 + GW // 16 * (h + 1)]
+                op("V", 60 + 1.6 * GW, lambda df=df, xr=xr, e=e, win=win, off=off: V.tensor_tensor(df[:, e], win.indirect(off),
+                                                                                                   xr[:, e], A.subtract),
+                   (["keys", "keysx"] if shifted else ["key", "keyx"] if t else ["key"])
+                   + [("LU", t, b), ("xr", b, 0), ("xr", b, 1)], [("df", b, h)])
+                op("S", 70 + GW, lambda df=df, ad=ad, e=e: S.activation(ad[:, e], df[:, e], F.Abs), [("df", b, h)], [("ad", b, h)])
+                if h == 0:
+                    op("P", 64, group([(H, wt, LX, True, True)]), [("LX", t, b), ("wt", t)], [("H", b)], banks=[bB])
+                    op("V", 68, lambda kk=kk, H=H, t=t: V.tensor_scalar(kk, H, 2.0 ** -11, T.ck[:] if t else 1025.0 - 511.5 / 1024,
+                                                                        A.mult, A.add), [("H", b), "ck"], [("kk", b)], banks=[bB])
+            op("P", 1024, group([(D, T.wd[:, 15 - i:143 - i], ad[:, i::16], i == 0, i == 15) for i in range(16)]),
+               [("ad", b, h) for h in range(NC)] + ["wd"], [("D", b)], banks=[bA])
+            op("S", 140, lambda sg=sg, D=D: S.activation(sg, D, F.Sign, bias=T.thb[:], scale=-1.0), [("D", b), "thb"],
+               [("sg", b)], banks=[bA])
+            op("P", 320, group([(PA, T.idh[:], LP, True, False), (PA, T.cnt[:], sg, False, True),
+                                (PN, wt, LX, True, False), (PN, T.nk[:], kk, False, False), (PN, T.bn[:], sg, False, True)]),
+               [("LP", t, b), ("LX", t, b), ("wt", t), ("kk", b), ("sg", b), "idh", "cnt", "nk", "bn"], [("AN", b)], banks=[bB])
+            op("S", 140, lambda sg=sg, nn=nn: S.activation(nn, sg, F.Relu, scale=-1.0), [("sg", b)], [("nn", b)])
+            op("V", 68, lambda y=y, PA=PA, t=t: V.tensor_scalar(y, PA, T.ca1[:] if t else T.ca0[:], 0.0, A.add, A.max),
+               [("AN", b), "ca1", "ca0"], [("y", b)], banks=[bB])
+            op("V", 68, lambda zh=zh, PN=PN, t=t: V.tensor_scalar(zh, PN, T.cn[:] if t else float(2048 * 1025 + 2 - 32768), 0.0,
+                                                                  A.add, A.max), [("AN", b), "cn"], [("zh", b)], banks=[bB])
+            zm = T.zm
+            op("P", 256, group([(Z[:, :, 0:16], zm[:, 0:128], y, True, False), (Z[:, :, 0:16], zm[:, 256:384], zh, False, True),
+                                (Z[:, :, 16:32], zm[:, 128:256], y, True, False),
+                                (Z[:, :, 16:32], zm[:, 384:512], zh, False, True)]),
+               [("y", b), ("zh", b), "zm"], [("Z", b)], banks=[bA])
+            op("V", cyc(128), lambda zt=zt, Z=Z: V.transpose(zt, Z), [("Z", b)], [("zt", b)], banks=[bA])
+            op("P", 128 + 64 * (t > 0), group([(Q, T.idh[:], LP, True, False)]
+                                              + ([(Q, T.idh[:], T.oh[:], False, False)] if shifted else [])
+                                              + [(Q, T.n4[:], nn, False, True)]),
+               [("LP", t, b), ("nn", b), "idh", "oh", "n4"], [("Q", b)], banks=[bA])
+            op("V", 68, lambda cc=cc, zt=zt: V.tensor_scalar(cc, zt[:, :, 0], 0.5, -1.25, A.mult, A.add), [("zt", b)], [("cc", b)])
+            clw = T.clb[:, 0:1025] if t else T.clb[:, 0:1024]
+            op("V", 170, lambda cm=cm, cc=cc, nn=nn, clw=clw: V.tensor_tensor(cm, clw.indirect(cc), nn, A.mult),
+               [("cc", b), ("nn", b), "cl"] + (["clx"] if t else []), [("cm", b)])
+            SP, SU, SX = T.SP[:, cs], T.SU[:, cs], T.SX[:, cs]
+            op("V", 68, lambda SP=SP, cm=cm, Q=Q: V.tensor_tensor(SP, cm, Q, A.max), [("cm", b), ("Q", b)], [("SP", t, b)],
+               banks=[bA])
+            op("V", 68, lambda SU=SU, SP=SP: V.tensor_copy(SU, SP), [("SP", t, b)], [("SU", t, b)])
+            emw = T.emt[:, 0:2049] if t else T.emt[:, 0:2048]
+            for h in range(NC):
+                e = slice(GW * h, GW * h + GW)
+                off = T.SU[:, c0 + GW // 16 * h:c0 + GW // 16 * (h + 1)]
+                op("S", 80 + 1.6 * GW, lambda eg=eg, e=e, emw=emw, off=off: S.activation(eg[:, e], emw.indirect(off), F.Copy),
+                   [("SU", t, b), "em"] + (["emx"] if t else []), [("eg", b, h)])
+            if t == NT - 1:
+                ts(T.ip[:, bl], SP, 1.0 if rank == NR - 1 else 0.0, None, A.add, None, [("SP", t, b)], [("ip", b)], 64)
+                ts(T.iq[:, bl], T.ip[:, bl], 2047, None, A.bitwise_and, None, [("ip", b)], [("iq", b)], 64)
+                cp(T.SYP[:, bl], T.iq[:, bl], [("iq", b)], [("SYP", b)], 64)
+                op("G", 900, lambda b=b, bl=bl: g.remote_dma(T.FYP[:, bl], T.SYP[:, bl], T.sem["ap%d" % b], T.sem.sent, pid, rid,
+                                                             mask(eng)), [("SYP", b)], [("fp", b)], sem="sent", val=len(eng))
+                op("N", 0, None, [("fp", b)], [("FYP", b)], sem="ap%d" % b, val=8)
+                op("Y", 80, lambda b=b, bl=bl: Y.dma_start(T.yp[:, bl], T.FYP[:, bl]), [("FYP", b)], (), sem="op%d" % b, val=16,
+                   lat=2200)
+            op("P", 17 * 64, group([(VT, T.db[:], T.ob[:, 0:64], True, False)]
+                                   + [(VT, T.idb[:], eg[:, i::16], False, i == 15) for i in range(16)]),
+               [("eg", b, h) for h in range(NC)] + ["db", "ob", "idb"], [("VT", b)], banks=[bB])
+            op("V", 68, lambda vt=vt, VT=VT: V.transpose(vt, VT), [("VT", b)], [("vt", b)], banks=[bB])
+            op("V", 68, lambda vt=vt, sc=sc: V.tensor_tensor_scan(sc, T.mk[:], vt, 0.0, A.mult, A.max), [("vt", b), "mk"],
+               [("sc", b)])
+            op("V", 68, lambda ti=ti, sc=sc: V.tensor_copy(ti, sc[:, 15::16]), [("sc", b)], [("ti", b)])
+            op("V", 68, lambda tv=tv, ti=ti, sc=sc: V.tensor_tensor(tv, sc[:, 15::16], ti, A.subtract), [("sc", b), ("ti", b)],
+               [("tv", b)])
+            op("P", 256, group([(TK[:, hf::2], T.fx[:, 256 * e + 128 * hf:256 * e + 128 * hf + 128], tv[:, e::2], e == 0, e == 1)
+                                for hf in range(2) for e in range(2)]), [("tv", b)] + [("fx", j) for j in range(4)], [("TK", b)],
+               banks=[bA])
+            tok = T.toku[:, 16 * t + 4 * b:16 * t + 4 * b + 4]
+            op("V", 68, lambda tok=tok, TK=TK: V.tensor_scalar(tok, TK, -16.0, 7.5, A.mult, A.add), [("TK", b)], [("tok", t, b)],
+               banks=[bA])
+            op("V", 170, lambda SX=SX, tok=tok, LX=LX, t=t: V.tensor_tensor(SX, T.tab[:, 16 * t:16 * t + 16].indirect(tok), LX, A.add),
+               [("tok", t, b), ("LX", t, b), ("tab", t)], [("SX", t, b)])
+            if t < NT - 1:
+                d0 = 256 * (t + 1) + LB * b
+                ds = slice(d0, d0 + LB)
+
+                def send(ds=ds, SU=SU, SP=SP, SX=SX, t=t, b=b):
+                    dst, sem = [DstId(rid=rid, pnc=pid)], T.sem[arrive(t + 1, b)]
+                    return g.remote_dma_fused([
+                        RemoteDMATransfer(dst_ids=dst, dma_engine_mask=mask(es), remote_sem=sem, src=a, dst=d)
+                        for es, a, d in ((eng[0:2], SU, T.LU[:, ds]), (eng[2:4], SP, T.LP[:, ds]), (eng[4:8], SX, T.LX[:, ds]))],
+                        local_sem=T.sem.sent)
+                op("G", 900, send, [("SU", t, b), ("SP", t, b), ("SX", t, b)], [("snd", t, b)], sem="sent", val=len(eng))
+            else:
+                ts(T.SYQ[:, bl], SX, 2.0 ** -NT, -1024.0, A.mult, A.add, [("SX", t, b)], [("SYQ", b)], 32)
+                op("G", 900, lambda b=b, bl=bl: g.remote_dma(T.FYQ[:, bl], T.SYQ[:, bl], T.sem["aq%d" % b], T.sem.sent, pid, rid,
+                                                             mask(eng)), [("SYQ", b)], [("fq", b)], sem="sent", val=len(eng))
+                op("N", 0, None, [("fq", b)], [("FYQ", b)], sem="aq%d" % b, val=8)
+                op("Y", 80, lambda b=b, bl=bl: Y.dma_start(T.yq[:, bl], T.FYQ[:, bl]), [("FYQ", b)], (), sem="oq%d" % b, val=16,
+                   lat=2200)
+        if t == 1:
+            yt_out(0, [0, 1])
+        if t == 3:
+            yt_out(1, [2, 3])
+    yt_out(2, [4])
+
+    schedule(ops)
+    emit_all(ops, {"V": V, "S": S, "P": P, "G": g, "Y": Y}, T, g)
+
+
+CNT_SEM = {"V": "cv", "S": "cs", "P": "ct", "G": "cg"}
+
+
+def schedule(ops):
+    lastw, readers, bank = {}, {}, {}
+    for o in ops:
+        d = set()
+        for k in o["R"]:
+            if k in lastw:
+                d.add(lastw[k])
+            readers.setdefault(k, []).append(o["i"])
+        for k in o["W"]:
+            if k in lastw:
+                d.add(lastw[k])
+            d.update(readers.get(k, []))
+            lastw[k], readers[k] = o["i"], []
+        for k in o["banks"]:
+            for q, i in bank.setdefault(k, [])[-40:]:
+                if q != o["q"]:
+                    d.add(i)
+            bank[k].append((o["q"], o["i"]))
+        d.discard(o["i"])
+        o["D"] = d
+    n = len(ops)
+    succ = [[] for _ in range(n)]
+    for o in ops:
+        for d in o["D"]:
+            succ[d].append(o["i"])
+    tail = [0.0] * n
+    for o in reversed(ops):
+        w = max([tail[s] for s in succ[o["i"]]] + [0])
+        tail[o["i"]] = w + o["dur"] + o["lat"] + (LINK if o["q"] == "N" else HOP)
+    free = {q: 0.0 for q in "VSPGYN"}
+    left = [len(o["D"]) for o in ops]
+    ready = {q: [] for q in "VSPGYN"}
+    avail = [0.0] * n
+    for o in ops:
+        if not left[o["i"]]:
+            ready[o["q"]].append(o["i"])
+    done = 0
+    while done < n:
+        best = None
+        for q in "VSPGYN":
+            if not ready[q]:
+                continue
+            if q == "N":
+                i = min(ready[q], key=lambda j: avail[j])
+                st = avail[i]
+            else:
+                st = max(free[q], min(avail[j] for j in ready[q]))
+                i = max((j for j in ready[q] if avail[j] <= st + 1e-9), key=lambda j: tail[j] + ops[j]["bias"])
+            if best is None or st < best[0]:
+                best = (st, q, i)
+        st, q, i = best
+        o = ops[i]
+        ready[q].remove(i)
+        o["st"] = st
+        end = st + o["dur"]
+        if q != "N":
+            free[q] = end
+        fin = end + o["lat"] + (LINK if q == "N" else HOP)
+        o["end"] = fin
+        done += 1
+        for s in succ[i]:
+            avail[s] = max(avail[s], fin)
+            left[s] -= 1
+            if not left[s]:
+                ready[ops[s]["q"]].append(s)
+
+
+def emit_all(ops, queues, T, g):
+    order = sorted((o for o in ops if not o["skip"]), key=lambda o: (o["st"], o["i"]))
+    count, known, total, clock = {}, {q: {} for q in "VSPGYN"}, {}, {}
+    for o in order:
+        q = o["q"]
+        kn = known[q]
+        if q == "N":
+            clock[o["i"]] = {o["sem"]: o["val"]}
+            total[o["sem"]] = o["val"]
+            o["tok"] = (o["sem"], o["val"])
+            continue
+        eng = queues[q]
+        for d in sorted((ops[i] for i in o["D"]), key=lambda x: -x["end"]):
+            if d["skip"]:
+                continue
+            s, v = d["tok"]
+            if kn.get(s, 0) >= v:
+                continue
+            eng.wait_ge(T.sem[s], v)
+            for a, w in clock[d["i"]].items():
+                if kn.get(a, 0) < w:
+                    kn[a] = w
+        ins = o["emit"]()
+        if o["sem"] == "sent":
+            total["sent"] = total.get("sent", 0) + o["val"]
+            o["tok"] = ("sent", 0)
+            clock[o["i"]] = {}
+            continue
+        if o["sem"] is not None:
+            ins.then_inc(T.sem[o["sem"]], o["val"])
+            s, v = o["sem"], o["val"]
+        else:
+            s = CNT_SEM[q]
+            count[s] = count.get(s, 0) + 1
+            v = count[s]
+            ins.then_inc(T.sem[s], 1)
+        total[s] = v
+        o["tok"] = (s, v)
+        ck = dict(kn)
+        ck[s] = v
+        clock[o["i"]] = ck
+    for s, v in sorted(total.items()):
+        g.wait_ge(T.sem[s], v)

@@ -1,55 +1,55 @@
 from concourse.mybir import AluOpType, ActivationFunctionType
-from concourse.bass import DstId, RemoteDMATransfer
 
 NR, NB, LB, NT = 4, 4, 64, 5
-NC = 2
-GW = 1024 // NC
-HOP = 40
-LINK = 3200
+XO = 1536.0
+CFG = {"nk": 2, "ne": 2, "nx": 2, "np": 4,
+       "f": 1.2, "gam": 1.56, "hop": 180, "link": 2600, "iss": 700, "rounds": 1, "per": 3260,
+       "off": {'xr0': 6740, 'xr1': 3850, 'df0': -550, 'ad0': 8500, 'df1': 950, 'ad1': 11080, 'H0': 5470, 'kk0': -900, 'PA0': 2010,
+               'PA1': 4680, 'D0': 4940, 'D1': 1530, 'D2': 3930, 'D3': 3070, 'sg0': 3590, 'PA2': 2330, 'Q0': 7000, 'at0': 13380,
+               'am0': 3490, 'cc0': 5260, 'cm0': 16090, 'SP0': 6270, 'SU0': 11280, 'VT0': 9880, 'E0': 10450, 'eg0': 6070, 'eg1': 5330,
+               'VT1': 7500, 'VT2': 12480, 'VT3': 7550, 'VT4': 17950, 'vt0': 9450, 'sc0': 11360, 'SC0': 9810, 'eq0': 11530,
+               'oh0': 13080, 'E1': 14810, 'SX0': 10410},
+       "tab": [27000, 42000, 57000], "piece": 2000, "due": 70000, "ahead": ["key"],
+       "eng": {"lu": "V", "xs": "S", "kk": "S", "cc": "V", "su": "S", "sx": "S"}}
 
 SCRATCH = {
-    "keyb": ("sbuf", [128, 2064], "bfloat16"), "keys": ("sbuf", [128, 2048], "bfloat16"),
-    "emt": ("sbuf", [128, 2064], "bfloat16"), "clb": ("sbuf", [128, 1032], "int32"),
     "plb": ("sbuf", [128, 256], "int32"), "qb": ("sbuf", [128, 256], "bfloat16"),
-    "wb": ("sbuf", [128, 1], "bfloat16"), "thf": ("sbuf", [128, 1], "float32"), "eb": ("sbuf", [128, 16], "bfloat16"),
-    "LU": ("sbuf", [128, 1280], "uint16"), "LP": ("sbuf", [128, 1280], "float16"), "LX": ("sbuf", [128, 1280], "float16"),
-    "SU": ("sbuf", [128, 1280], "uint16"), "SP": ("sbuf", [128, 1280], "float16"), "SX": ("sbuf", [128, 1280], "float16"),
+    "wb": ("sbuf", [128, 1], "bfloat16"), "thf": ("sbuf", [128, 1], "float32"), "eb": ("sbuf", [128, 128], "bfloat16"),
+    "LU": ("sbuf", [128, 256], "uint16"), "SU": ("sbuf", [128, 256], "uint16"),
+    "LA": ("sbuf", [128, 4, 128], "float16"), "P0": ("sbuf", [128, 256], "float16"), "SA": ("sbuf", [128, 20, 128], "float16"),
     "SYP": ("sbuf", [128, 256], "float32"), "SYQ": ("sbuf", [128, 256], "bfloat16"),
-    "FYP": ("sbuf", [128, 256], "float32"), "FYQ": ("sbuf", [128, 256], "bfloat16"),
     "ip": ("sbuf", [128, 256], "int32"), "iq": ("sbuf", [128, 256], "int32"),
-    "ob": ("sbuf", [128, 128], "bfloat16"), "oh": ("sbuf", [128, 64], "float16"), "idb": ("sbuf", [128, 128], "bfloat16"),
-    "idh": ("sbuf", [128, 128], "float16"), "bm": ("sbuf", [128, 128], "bfloat16"), "bm0": ("sbuf", [128, 128], "bfloat16"),
-    "wd": ("sbuf", [128, 144], "bfloat16"), "ub": ("sbuf", [128, 128], "bfloat16"), "u2": ("sbuf", [128, 128], "bfloat16"),
-    "q2": ("sbuf", [128, 128], "bfloat16"), "cnt": ("sbuf", [128, 128], "bfloat16"), "bn": ("sbuf", [128, 128], "bfloat16"),
-    "nk": ("sbuf", [128, 128], "float16"), "n4": ("sbuf", [128, 128], "bfloat16"), "db": ("sbuf", [128, 128], "bfloat16"),
-    "ii": ("sbuf", [128, 1], "int32"), "ik": ("sbuf", [128, 1], "int32"), "io16": ("sbuf", [128, 1], "int32"),
-    "kc": ("sbuf", [128, 1], "float32"), "odd": ("sbuf", [128, 1], "float32"), "even": ("sbuf", [128, 1], "float32"),
-    "vb": ("sbuf", [128, 1], "float32"), "ca0": ("sbuf", [128, 1], "float32"), "ca1": ("sbuf", [128, 1], "float32"),
-    "m0": ("sbuf", [128, 1], "float32"), "thb": ("sbuf", [128, 1], "float32"), "ck": ("sbuf", [128, 1], "float32"),
-    "cn": ("sbuf", [128, 1], "float32"),
-    "zb": ("sbuf", [128, 512], "bfloat16"), "zm": ("sbuf", [128, 512], "float16"),
-    "f10r": ("sbuf", [128, 128], "bfloat16"), "f01r": ("sbuf", [128, 128], "bfloat16"), "fx": ("sbuf", [128, 512], "bfloat16"),
-    "sl": ("sbuf", [128, 128], "bfloat16"), "mk": ("sbuf", [128, 64], "float32"), "wt": ("sbuf", [128, 640], "float16"),
-    "m2": ("sbuf", [128, 32], "float32"), "t2": ("sbuf", [128, 32], "float32"), "et": ("sbuf", [128, 16], "float32"),
-    "tab": ("sbuf", [128, 80], "float32"),
-    "toku": ("sbuf", [128, 80], "uint16"), "tokb": ("sbuf", [128, 80], "bfloat16"), "ytb": ("sbuf", [128, 1280], "float32"),
+    "m16": ("sbuf", [128, 1024], "bfloat16"), "m32": ("sbuf", [128, 128], "float32"),
+    "wd": ("sbuf", [128, 144], "bfloat16"), "wk": ("sbuf", [128, 132], "bfloat16"),
+    "ii": ("sbuf", [128, 1], "int32"), "ik": ("sbuf", [128, 1], "int32"), "i16": ("sbuf", [128, 1], "int32"),
+    "oh": ("sbuf", [128, 1280], "bfloat16"), "ytb": ("sbuf", [128, 320], "float32"), "ytl": ("sbuf", [128, 320], "float32"),
 }
-for _n, _s, _d in (("kk", [128, 256], "float16"), ("sg", [128, 256], "bfloat16"), ("nn", [128, 256], "bfloat16"),
-                   ("y", [128, 16, 16], "float16"), ("zh", [128, 16, 16], "float16"), ("zt", [128, 16, 32], "float32"),
-                   ("cc", [128, 16], "uint16"), ("cm", [128, 256], "float16"), ("vt", [128, 256], "float32"),
-                   ("sc", [128, 256], "float32"), ("ti", [128, 16], "int32"), ("tv", [128, 16], "bfloat16")):
+for _k in range(NR):
+    SCRATCH.update({"key%d" % _k: ("sbuf", [128, 2064], "bfloat16"), "em%d" % _k: ("sbuf", [128, 2064], "bfloat16"),
+                    "cl%d" % _k: ("sbuf", [128, 1032], "int32"), "cs%d" % _k: ("sbuf", [128, 512], "bfloat16"),
+                    "th%d" % _k: ("sbuf", [128, 1], "float32")})
+for _n in ("ob", "bm0", "bm", "idb", "ub", "xc", "ci", "t1", "t2", "sm0", "sm1", "n2"):
+    SCRATCH[_n] = ("sbuf", [128, 128], "bfloat16")
+for _n in ("idh", "ih0", "ih1", "k1", "k2", "k3", "k4", "k5", "km0", "km1", "cq", "cv"):
+    SCRATCH[_n] = ("sbuf", [128, 128], "float16")
+for _n in ("kc", "odd", "even", "r0", "r1", "r2", "r3", "ksc", "kb", "kb0", "kb1", "xk", "xk1", "rq", "we", "wo"):
+    SCRATCH[_n] = ("sbuf", [128, 1], "float32")
+for _n, _s, _d in (("kk", [128, 256], "float16"), ("sg", [128, 256], "bfloat16"), ("at", [128, 512], "float32"),
+                   ("am", [128, 512], "float32"), ("cc", [128, 16], "uint16"), ("cm", [128, 256], "float16"),
+                   ("vt", [128, 256], "float32"), ("sc", [128, 256], "float32"), ("eq", [128, 256], "bfloat16")):
     SCRATCH[_n] = ("sbuf", _s, _d)
 for _b in range(NB):
     SCRATCH.update({
-        "xr%d" % _b: ("sbuf", [128, 1024], "float16"), "df%d" % _b: ("sbuf", [128, 1024], "bfloat16"),
+        "xs%d" % _b: ("sbuf", [128, 1024], "uint16"),
+        "xr%d" % _b: ("sbuf", [128, 1024], "bfloat16"), "df%d" % _b: ("sbuf", [128, 1024], "bfloat16"),
         "ad%d" % _b: ("sbuf", [128, 1024], "bfloat16"), "eg%d" % _b: ("sbuf", [128, 1024], "bfloat16"),
-        "pa%d" % _b: ("psum", [128, 16, 32], "float32"), "pb%d" % _b: ("psum", [128, 512], "float32"),
+        "pa%d" % _b: ("psum", [128, 512], "float32"), "pb%d" % _b: ("psum", [128, 16, 32], "float32"),
     })
-LOADS = ["pl", "q", "key", "w", "th", "cl", "emb", "em", "keys"]
+PIECES = {"key": 2049, "cs": 512, "cl": 1026, "em": 2049}
+LOADS = ["pl", "q", "key", "w", "th", "cl", "emb", "em"]
 SEMAPHORES = (["cv", "cs", "ct", "cg", "sent"] + ["ld_" + n for n in LOADS]
-              + ["ar%d_%d" % (t, b) for t in range(1, NT) for b in range(NB)]
-              + ["ap%d" % b for b in range(NB)] + ["aq%d" % b for b in range(NB)]
-              + ["op%d" % b for b in range(NB)] + ["oq%d" % b for b in range(NB)] + ["oy%d" % k for k in range(3)])
+              + ["ar%d" % b for b in range(NB)] + ["a%s%d" % (n, k) for n in PIECES for k in range(1, NR)]
+              + ["op", "oq0", "oq1"] + ["oy%d" % t for t in range(NT)] + ["ay%d" % t for t in range(2, NT)])
 
 
 def rank_program(g, core, T, topo):
@@ -58,263 +58,291 @@ def rank_program(g, core, T, topo):
         return
     A, F = AluOpType, ActivationFunctionType
     V, S, P, Y = g.vector, g.scalar, g.tensor, g.sync
-    nxt = T.cores[(rank + 1) % NR]
-    rid, pid = topo.addr(nxt, core)
-    eng = topo.engines(core, nxt)[:8]
+    ops, seq, seen = [], [None], {}
+    NK, NE, NX, NP, ENG, GAM = CFG["nk"], CFG["ne"], CFG["nx"], CFG["np"], CFG["eng"], CFG["gam"]
 
-    def mask(es):
-        return sum(1 << e for e in es)
+    def near(a, b):
+        return T.cores[b % NR] in topo.cores_of(T.cores[a % NR])
 
-    o1 = 1 if rank == 0 else 0
-    ops, seq = [], [0]
+    def engines(a, b, kind):
+        ca = T.cores[a % NR]
+        out = topo.engines(ca, T.cores[(a + 2) % NR])
+        if near(a, b):
+            return [e for e in topo.engines(ca, T.cores[b % NR]) if e not in out]
+        return out
 
-    def op(q, dur, emit, R=(), W=(), banks=(), sem=None, val=1, lat=0, skip=False, bias=0):
-        ops.append({"q": q, "dur": dur, "emit": emit, "R": list(R), "W": list(W), "banks": list(banks), "sem": sem, "val": val,
-                    "lat": lat, "skip": skip, "i": len(ops), "bias": bias - 4000 * seq[0]})
+    def giver(k, r):
+        return r + 1 if near(r, r + 1) else r + k
 
-    def cyc(n):
-        return max(64, n) + 4
+    def op(q, dur, emit, R=(), W=(), banks=(), sem=None, val=1, lat=0, bias=0):
+        kind = None
+        if seq[0] is not None and q in "VSP" and not isinstance(W[0], str):
+            seen[seq[0], W[0][0]] = seen.get((seq[0], W[0][0]), 0) + 1
+            kind = "%s%d" % (W[0][0], seen[seq[0], W[0][0]] - 1)
+        ops.append({"q": q, "dur": dur * (0.83 * CFG["f"] if q in "VSP" else 1), "emit": emit, "R": list(R), "W": list(W),
+                    "banks": list(banks), "sem": sem, "val": val, "lat": lat, "i": len(ops), "bias": bias, "seq": seq[0],
+                    "kind": kind})
 
-    def load(q, name, fn, W, done, skip=False, bias=0):
-        op(q, 80, fn, (), W, sem="ld_" + name, val=16, lat=done, skip=skip, bias=bias)
+    def load(q, name, fn, W, done):
+        op(q, 80, fn, ["L" + q], W + ["L" + q], sem="ld_" + name, val=16, lat=done, bias=1e7)
 
-    load("Y", "pl", lambda: Y.dma_start(T.plb[:], T.pl[:]), ["plb"], 2300, bias=9e6)
-    load("S", "q", lambda: S.dma_start(T.qb[:], T.q[:]), ["qb"], 2300, bias=9e6)
-    load("Y", "key", lambda: Y.dma_start(T.keyb[:, 0:2048], T.key[:]), ["key"], 4600, bias=8e6)
-    load("S", "w", lambda: S.dma_start(T.wb[:], T.w[:]), ["wb"], 2300, bias=8e6)
-    load("S", "th", lambda: S.dma_start(T.thf[:], T.th[:]), ["thf"], 2300, bias=7e6)
-    load("S", "emb", lambda: S.dma_start(T.eb[:], T.emb[:]), ["eb"], 2300, bias=6e6)
-    load("Y", "cl", lambda: Y.dma_start(T.clb[:, 0:1024], T.cl[:]), ["cl"], 6900, bias=7e6)
-    load("Y", "em", lambda: Y.dma_start(T.emt[:, 0:2048], T.em[:]), ["em"], 9000, bias=6e6)
-    load("Y", "keys", lambda: Y.dma_start(T.keys[:, 0:2047], T.key[:, 1:2048]), ["keys"], 11000, skip=rank != 0, bias=5e6)
-
-    op("V", cyc(256), lambda: V.tensor_copy(T.LU[:, 0:256], T.plb[:]), ["plb"], [("LU", 0, b) for b in range(NB)])
-    op("V", cyc(128), lambda: V.tensor_copy(T.LX[:, 0:256], T.qb[:]), ["qb"], [("LX", 0, b) for b in range(NB)])
-    op("V", cyc(256), lambda: V.tensor_copy(T.LP[:, 0:256], T.plb[:]), ["plb"], [("LP", 0, b) for b in range(NB)])
-    op("V", 68, lambda: V.memset(T.ob[:], 1.0), (), ["ob"])
-
-    def aff(out, src, pat, cmp, base, cm, n):
-        op("G", 180 + 2 * n, lambda: g.affine_select(T[out][:], T[src][:], pat, cmp, 0.0, base, cm), [src], [out])
-
-    aff("bm0", "ob", [[-16, 8], [0, 16]], A.is_ge, 0, 1, 128)
-    aff("bm", "bm0", [[16, 8], [0, 16]], A.is_ge, 15, -1, 128)
-    aff("idb", "ob", [[-1, 128]], A.is_equal, 0, 1, 128)
-    op("G", 140, lambda: g.iota(T.ii[:], [[0, 1]], 0, 1), (), ["ii"])
-    aff("ub", "bm", [[1, 128]], A.is_ge, -1, -1, 128)
-    aff("f10r", "ob", [[1, 128]], A.is_equal, -16, -1, 128)
-    aff("f01r", "ob", [[1, 128]], A.is_equal, 16, -1, 128)
-    aff("sl", "ob", [[-1, 16], [-16, 8]], A.is_equal, 0, 1, 128)
-
-    def ts(out, i, s1, s2, a, b, R, W, n=1):
+    def ts(out, i, s1, s2, a, b, R, W, n=64, banks=()):
         if b is None:
-            op("V", cyc(n), lambda: V.tensor_scalar(out, i, s1, None, a), R, W)
+            op("V", n, lambda: V.tensor_scalar(out, i, s1, None, a), R, W, banks)
         else:
-            op("V", cyc(n), lambda: V.tensor_scalar(out, i, s1, s2, a, b), R, W)
+            op("V", n, lambda: V.tensor_scalar(out, i, s1, s2, a, b), R, W, banks)
 
-    def cp(out, i, R, W, n=1):
-        op("V", cyc(n), lambda: V.tensor_copy(out, i), R, W)
+    def tt(out, a, b, o, R, W, n=64, banks=()):
+        op("V", n, lambda: V.tensor_tensor(out, a, b, o), R, W, banks)
 
-    op("V", 76, lambda: V.memset(T.wd[:], 0.0), (), ["wd"])
-    cp(T.wd[:, 15:128:16], T.bm[:, 0::16], ["bm"], ["wd"])
-    ts(T.ik[:], T.ii[:], 15, None, A.bitwise_and, None, ["ii"], ["ik"])
-    ts(T.io16[:], T.ii[:], 16, None, A.bitwise_and, None, ["ii"], ["io16"])
-    cp(T.kc[:], T.ik[:], ["ik"], ["kc"])
-    ts(T.odd[:], T.io16[:], 0.0625, None, A.mult, None, ["io16"], ["odd"])
-    ts(T.even[:], T.odd[:], -1.0, 1.0, A.mult, A.add, ["odd"], ["even"])
-    ts(T.thb[:], T.thf[:], -0.5, None, A.add, None, ["thf"], ["thb"])
-    cp(T.idh[:], T.idb[:], ["idb"], ["idh"], 64)
-    ts(T.u2[:], T.ub[:], -2048.0, None, A.mult, None, ["ub"], ["u2"], 64)
-    ts(T.q2[:], T.idb[:], 2048.0, None, A.mult, None, ["idb"], ["q2"], 64)
-    op("V", 260, lambda: V.tensor_tensor(T.cnt[:], T.u2[:], T.q2[:], A.add), ["u2", "q2"], ["cnt"])
-    ts(T.bn[:], T.bm[:], -2048.0, None, A.mult, None, ["bm"], ["bn"], 64)
-    ts(T.nk[:], T.idb[:], -2048.0, None, A.mult, None, ["idb"], ["nk"], 64)
-    ts(T.n4[:], T.idb[:], -4096.0, None, A.mult, None, ["idb"], ["n4"], 64)
-    for t in range(NT):
-        ts(T.wt[:, 128 * t:128 * t + 128], T.bm[:], T.wb[:], 2.0 ** (1 - t), A.mult, A.mult, ["bm", "wb"], [("wt", t)], 64)
-    op("P", 64, lambda: P.matmul(T.pb0[:, 511:512], T.bm[:], T.wb[:], True, True), ["bm", "wb"], ["sw"], banks=["b0"])
-    op("V", 68, lambda: V.tensor_scalar(T.ck[:], T.pb0[:, 511:512], -1.0, 1025.0 - 511.5 / 1024, A.mult, A.add), ["sw"], ["ck"],
-       banks=["b0"])
-    op("V", 68, lambda: V.tensor_scalar(T.cn[:], T.pb0[:, 511:512], -2048.0, float(2048 * 1025 + 2 - 32768), A.mult, A.add),
-       ["sw"], ["cn"], banks=["b0"])
-    ts(T.ca0[:], T.kc[:], -2048.0, -2046.0, A.mult, A.add, ["kc"], ["ca0"])
-    op("V", 68, lambda: V.memset(T.zb[:], 0.0), (), ["zb"])
-    cp(T.zb[:, 0:128:32], T.bm[:, 0::32], ["bm"], ["zb"])
-    cp(T.zb[:, 128:256:32], T.bm[:, 16::32], ["bm"], ["zb"])
-    ts(T.m0[:], T.kc[:], 0.0, None, A.is_equal, None, ["kc"], ["m0"])
-    ts(T.zb[:, 256:384:32], T.bm[:, 0::32], T.m0[:], None, A.mult, None, ["bm", "m0"], ["zb"])
-    ts(T.zb[:, 384:512:32], T.bm[:, 16::32], T.m0[:], None, A.mult, None, ["bm", "m0"], ["zb"])
-    cp(T.zm[:], T.zb[:], ["zb"], ["zm"], 256)
-    cp(T.oh[:], T.ob[:, 0:64], ["ob"], ["oh"])
-    ts(T.vb[:], T.kc[:], -0.0625, 0.46875, A.mult, A.add, ["kc"], ["vb"])
-    ts(T.db[:], T.idb[:], T.vb[:], None, A.mult, None, ["idb", "vb"], ["db"], 64)
-    op("V", 68, lambda: V.memset(T.mk[:], 1.0), (), ["mk"])
-    op("V", 68, lambda: V.memset(T.mk[:, 0::16], 0.0), (), ["mk"])
-    fsrc = [("idb", "even"), ("f01r", "odd"), ("f10r", "even"), ("idb", "odd")]
-    for j, (m, c) in enumerate(fsrc):
-        ts(T.fx[:, 128 * j:128 * j + 128], T[m][:], T[c][:], None, A.mult, None, [m, c], [("fx", j)], 64)
-    ts(T.m2[:, 0:16], T.eb[:], T.even[:], None, A.mult, None, ["eb", "even"], ["m2"])
-    ts(T.m2[:, 16:32], T.eb[:], T.odd[:], None, A.mult, None, ["eb", "odd"], ["m2b"])
-    op("V", 68, lambda: V.transpose(T.t2[:], T.m2[:]), ["m2", "m2b"], ["t2"])
-    op("V", 68, lambda: V.tensor_tensor(T.et[:], T.t2[:, 0:16], T.t2[:, 16:32], A.add), ["t2"], ["et"])
-    for t in range(NT):
-        ts(T.tab[:, 16 * t:16 * t + 16], T.et[:], 2047.5 if t == 0 else 1023.5, 2.0 ** t, A.add, A.mult, ["et"], [("tab", t)])
-    ts(T.ca1[:], T.kc[:], -2048.0, -2046.0 + o1, A.mult, A.add, ["kc"], ["ca1"])
-    cp(T.clb[:, 1024:1025], T.clb[:, 0:1], ["cl"], ["clx"])
-    op("S", 80, lambda: S.activation(T.emt[:, 2048:2049], T.emt[:, 0:1], F.Copy), ["em"], ["emx"])
-    op("S", 80, lambda: S.activation(T.keyb[:, 2048:2049], T.keyb[:, 0:1], F.Copy), ["key"], ["keyx"])
-    op("S", 80, lambda: S.activation(T.keys[:, 2047:2048], T.keyb[:, 0:1], F.Copy), ["key", "keys"], ["keysx"], skip=rank != 0)
+    def cp(out, i, R, W, n=64):
+        op("V", n, lambda: V.tensor_copy(out, i), R, W)
 
-    def group(ms):
+    def ms(out, c, W, n=64):
+        op("V", n, lambda: V.memset(out, c), (), W)
+
+    def lin(q, out, i, mul, add, R, W, n=64, banks=()):
+        if q == "V":
+            ts(out, i, mul, add, A.mult, A.add, R, W, n, banks)
+        else:
+            op("S", n, lambda: S.activation(out, i, F.Identity, bias=add, scale=mul), R, W, banks)
+
+    def scan(out, d0, d1, o, R, W, n, banks=()):
+        op("V", n, lambda: V.tensor_tensor_scan(out, d0, d1, 0.0, A.mult, o), R, W, banks)
+
+    def turn(out, i, R, W, n, banks=()):
+        op("V", n, lambda: V.transpose(out, i), R, W, banks)
+
+    def act(out, i, f, R, W, n, banks=(), bias=0.0):
+        op("S", n, lambda: S.activation(out, i, f, bias=bias), R, W, banks)
+
+    def mm(ms_, R, W, bank):
         def f():
             last = None
-            for m in ms:
+            for m in ms_:
                 last = P.matmul(*m)
             return last
-        return f
+        op("P", 64 * len(ms_), f, R, W, [bank])
 
-    def arrive(t, b):
-        return "ar%d_%d" % (t, b)
+    def aff(out, src, pat, cmp, base, cm):
+        op("G", 460, lambda: g.affine_select(T[out][:], T[src][:], pat, cmp, 0.0, base, cm), [src], [out])
 
-    def yt_out(k, ts_):
-        n = len(ts_)
-        lo, hi = ts_[0], ts_[-1] + 1
-        cp(T.tokb[:, 16 * lo:16 * hi], T.toku[:, 16 * lo:16 * hi], [("tok", t, b) for t in ts_ for b in range(NB)], [("tokb", k)])
-        bk, lastb = T["pa%d" % (NB - 1)], NB - 1
-        op("P", 16 * 64, group([(bk[0:8, 0:8 * n, j::16], T.sl[:, 8 * j:8 * j + 8], T.tokb[:, 16 * lo:16 * hi], True, True)
-                                for j in range(16)]), ["sl", ("tokb", k)], ["ytp"] + [(x, lastb) for x in ("D", "Q", "Z", "TK")],
-           banks=["a%d" % lastb])
-        op("S", 80 + 256 * n, lambda: S.activation(T.ytb[0:8, 256 * lo:256 * hi], bk[0:8, 0:8 * n, :], F.Copy), ["ytp"],
-           [("ytb", k)], banks=["a%d" % lastb])
-        op("Y", 80, lambda: Y.dma_start(T.yt[:, 256 * lo:256 * hi], T.ytb[0:8, 256 * lo:256 * hi]), [("ytb", k)], (),
-           sem="oy%d" % k, val=16, lat=2200)
+    load("Y", "pl", lambda: Y.dma_start(T.plb[:], T.pl[:]), ["plb"], 2300)
+    load("S", "q", lambda: S.dma_start(T.qb[:], T.q[:]), ["qb"], 2300)
+    load("Y", "key", lambda: Y.dma_start(T.key0[:, 0:2048], T.key[:]), ["key"], 4600)
+    load("S", "w", lambda: S.dma_start(T.wb[:], T.w[:]), ["wb"], 4700)
+    load("S", "th", lambda: S.dma_start(T.thf[:], T.th[:]), ["thf"], 4800)
+    load("S", "emb", lambda: S.dma_start(T.eb[:, 0:16], T.emb[:]), ["eb"], 4900)
+    load("Y", "cl", lambda: Y.dma_start(T.cl0[:, 0:1024], T.cl[:]), ["cl"], 6900)
+    load("Y", "em", lambda: Y.dma_start(T.em0[:, 0:2048], T.em[:]), ["em"], 9000)
+
+    ms(T.ob[:], 1.0, ["ob"])
+    op("G", 140, lambda: g.iota(T.ii[:], [[0, 1]], 0, 1), (), ["ii"])
+    aff("bm0", "ob", [[-16, 8], [0, 16]], A.is_ge, 0, 1)
+    aff("bm", "bm0", [[16, 8], [0, 16]], A.is_ge, 15, -1)
+    aff("idb", "ob", [[-1, 128]], A.is_equal, 0, 1)
+    aff("ub", "bm", [[1, 128]], A.is_ge, -1, -1)
+    op("G", 400, lambda: g.iota(T.ci[:], [[0, 8], [1, 16]], 1, 0, allow_small_or_imprecise_dtypes=True), (), ["ci"])
+    for k in range(NB):
+        ms(T["xs%d" % k][:], 0, [("xs", k)], 512)
+    ms(T.m16[:, 0:1024 // NX], 1.0, ["m16"], 512 // NX)
+    ms(T.m16[:, 0:1024 // NX:16], 0.0, ["m16"])
+    ms(T.m32[:], 1.0, ["m32"], 128)
+    ms(T.m32[:, 0::32], 0.0, ["m32"])
+    ts(T.ik[:], T.ii[:], 15, None, A.bitwise_and, None, ["ii"], ["ik"])
+    ts(T.i16[:], T.ii[:], 16, None, A.bitwise_and, None, ["ii"], ["i16"])
+    cp(T.kc[:], T.ik[:], ["ik"], ["kc"])
+    ts(T.odd[:], T.i16[:], 0.0625, None, A.mult, None, ["i16"], ["odd"])
+    lin("S", T.even[:], T.odd[:], -1.0, 1.0, ["odd"], ["even"])
+    for j in range(4):
+        ts(T["r%d" % j][:], T.kc[:], float(j), None, A.is_equal, None, ["kc"], ["r%d" % j])
+    lin("S", T.th0[:], T.thf[:], -1.0, 0.5, ["thf"], [("th", 0)])
+    ms(T.wd[:], 0.0, ["wd"], 72)
+    cp(T.wd[:, 15:128:16], T.bm[:, 0::16], ["bm"], ["wd"])
+    ms(T.wk[:], 0.0, ["wk"], 66)
+    ts(T.wk[:, 3:35:4], T.bm[:, 0::16], T.kc[:], None, A.mult, None, ["bm", "kc"], ["wk"])
+    ms(T.xc[:], 0.0, ["xc"])
+    cp(T.xc[:, 16::32], T.bm[:, 0::32], ["bm"], ["xc"])
+    cp(T.xc[:, 0::32], T.bm[:, 16::32], ["bm"], ["xc"])
+    lin("S", T.ksc[:], T.r0[:], 2.0 ** -10, 0.0, ["r0"], ["ksc"])
+    lin("S", T.kb[:], T.r1[:], 2048.0, T.r3[:], ["r1", "r3"], ["kb"])
+    lin("S", T.kb0[:], T.r0[:], 1025.0 - 511.5 / 1024, T.kb[:], ["r0", "kb"], ["kb0"])
+    lin("S", T.kb1[:], T.r2[:], 1.0, T.kb0[:], ["r2", "kb0"], ["kb1"])
+    lin("S", T.xk1[:], T.r1[:], 1009.0, 0.0, ["r1"], ["xk1"])
+    lin("S", T.xk[:], T.r0[:], -2048.0, T.xk1[:], ["r0", "xk1"], ["xk"])
+    lin("S", T.rq[:], T.r1[:], -1.0, T.r2[:], ["r1", "r2"], ["rq"])
+    lin("S", T.we[:], T.wb[:], T.even[:], 0.0, ["wb", "even"], ["we"])
+    lin("S", T.wo[:], T.wb[:], T.odd[:], 0.0, ["wb", "odd"], ["wo"])
+    par = [("even", "we"), ("odd", "wo")]
+    cp(T.idh[:], T.idb[:], ["idb"], ["idh"])
+    ts(T.n2[:], T.idb[:], -2048.0, None, A.mult, None, ["idb"], ["n2"])
+    ts(T.cs0[:, 0:128], T.bm[:], T.wb[:], None, A.mult, None, ["bm", "wb"], ["wm"])
+    tt(T.t1[:], T.ub[:], T.idb[:], A.subtract, ["ub", "idb"], ["t1"], 256)
+    tt(T.t2[:], T.t1[:], T.xc[:], A.add, ["t1", "xc"], ["t2"], 256)
+    ts(T.k1[:], T.ci[:], T.rq[:], 1.0, A.mult, A.min, ["ci", "rq"], ["k1"])
+    tt(T.k3[:], T.k1[:], T.bm[:], A.mult, ["k1", "bm"], ["k3"], 256)
+    lin("S", T.k4[:], T.xc[:], T.xk[:], 0.0, ["xc", "xk"], ["k4"], 128)
+    tt(T.k5[:], T.k3[:], T.k4[:], A.add, ["k3", "k4"], ["k5"], 256)
+    for e, (c, w) in enumerate(par):
+        ts(T["sm%d" % e][:], T.t2[:], T[c][:], 2048.0, A.mult, A.mult, ["t2", c], [("sm", e)])
+        lin("S", T["ih%d" % e][:], T.idb[:], T[c][:], 0.0, ["idb", c], [("ih", e)], 128)
+        ts(T.cs0[:, 128 * e + 128:128 * e + 256], T.xc[:], T[w][:], 2.0, A.mult, A.mult, ["xc", w], [("wx", e)])
+        ts(T["km%d" % e][:], T.k5[:], T[c][:], None, A.mult, None, ["k5", c], [("km", e)])
+    lin("S", T.cq[:], T.bm[:], T.rq[:], 0.0, ["bm", "rq"], ["cq"], 128)
+    lin("S", T.k2[:], T.ci[:], -0.0625, 1.0, ["ci"], ["k2"], 128)
+    lin("S", T.k4[:], T.bm[:], T.r3[:], 0.0, ["bm", "r3"], ["k4"], 128)
+    tt(T.cv[:], T.k2[:], T.k4[:], A.mult, ["k2", "k4"], ["cv"], 256)
+    for n in (16, 32, 64):
+        cp(T.eb[:, n:2 * n], T.eb[:, 0:n], ["eb"], ["eb"])
+    tt(T.cs0[:, 384:512], T.eb[:], T.bm[:], A.mult, ["eb", "bm"], ["em2"], 256)
+    cp(T.cl0[:, 1024:1025], T.cl0[:, 0:1], ["cl"], ["clx"])
+    cp(T.cl0[:, 1025:1026], T.thf[:], ["cl", "thf"], ["clt"])
+    act(T.em0[:, 2048:2049], T.em0[:, 0:1], F.Copy, ["em"], ["emx"], 64)
+    act(T.key0[:, 2048:2049], T.key0[:, 0:1], F.Copy, ["key"], ["keyx"], 64)
+    own = {"cs": ["wm", ("wx", 0), ("wx", 1), "em2"], "key": ["key", "keyx"], "cl": ["cl", "clx", "clt"], "em": ["em", "emx"]}
+
+    def tab(n, k):
+        return own[n] if k == 0 else [(n, k)]
+
+    def send(to, kind, dst, src, sem, R, due=0.0):
+        rid, pid = topo.addr(T.cores[to % NR], core)
+        es = engines(rank, to, kind)
+        op("G", CFG["iss"], lambda: g.remote_dma(dst, src, T.sem[sem], T.sem.sent, pid, rid, sum(1 << e for e in es)), R + ["LG"],
+           ["LG", ("snd", sem)], sem="sent", val=len(es))
+        ops[-1]["due"], ops[-1]["bias"] = due, -2000 if due else 0
+
+    def arrival(frm, kind, sem, R, W, lat=0):
+        op("N", 0, None, R, W, sem=sem, val=len(engines(frm, rank, kind)), lat=lat)
+
+    def hand_on(k, early):
+        for r in range(rank - NR + 1, rank):
+            mine = (r + k - rank) % NR
+            if (giver(k, r) - rank) % NR == 0:
+                for n, w in PIECES.items():
+                    if early == (mine == 0 and (k == 1 or k == 2 and n in CFG["ahead"])):
+                        send(r, "tab", T["%s%d" % (n, k)][:, 0:w], T["%s%d" % (n, mine)][:, 0:w], "a%s%d" % (n, k), tab(n, mine),
+                             CFG["due"] if early else 0.0)
+
+    def store(dst, src, sem, R):
+        op("Y", 80, lambda: Y.dma_start(dst, src), R, (), sem=sem, val=16, lat=2200)
+
+    for k in range(1, NR):
+        for i, n in enumerate(PIECES):
+            arrival(giver(k, rank), "tab", "a%s%d" % (n, k), [], [(n, k)], lat=CFG["tab"][k - 1] + CFG["piece"] * i)
+        lin("V", T["th%d" % k][:], T["cl%d" % k][:, 1025:1026], -1.0, 0.5, [("cl", k)], [("th", k)])
+    hand_on(2, True)
+    hand_on(1, True)
 
     for t in range(NT):
+        k = max(t - 1, 0)
+        wrap = t > 0 and (rank + k) % NR == 0
+        key, emt, clb, cs = [T["%s%d" % (n, k)] for n in ("key", "em", "cl", "cs")]
         for b in range(NB):
-            c0 = 256 * t + LB * b
-            seq[0] = t * NB + b
-            cs = slice(c0, c0 + LB)
+            seq[0] = j = t * NB + b
             bA, bB = "a%d" % b, "b%d" % b
             pa, pb = T["pa%d" % b], T["pb%d" % b]
-            D, Q, Z, TK = pa[:, 4:6, :], pa[:, 6:8, :], pa[:, 0:4, :], pa[:, 8, 0:4]
-            H, PA, PN, VT = pb[:, 0:64], pb[:, 64:128], pb[:, 128:192], pb[:, 192:256]
-            xr, df, ad, eg = T["xr%d" % b], T["df%d" % b], T["ad%d" % b], T["eg%d" % b]
-            bl, b4 = slice(LB * b, LB * b + LB), slice(4 * b, 4 * b + 4)
-            kk, sg, nn, cm, vt, sc = [T[n][:, bl] for n in ("kk", "sg", "nn", "cm", "vt", "sc")]
-            y, zh, zt = [T[n][:, b4, :] for n in ("y", "zh", "zt")]
-            cc, ti, tv = [T[n][:, b4] for n in ("cc", "ti", "tv")]
-            shifted = rank == 0 and t > 0
-            if t:
-                op("N", 0, None, [("snd", t - 1, b)], [(n, t, b) for n in ("LU", "LP", "LX")], sem=arrive(t, b), val=8)
-            LU, LP, LX = T.LU[:, cs], T.LP[:, cs], T.LX[:, cs]
-            wt = T.wt[:, 128 * t:128 * t + 128]
-            if t:
-                op("V", cyc(32), lambda xr=xr, LX=LX, t=t: V.tensor_scalar(xr[:, 0::16], LX, 2.0 ** -t, -1024.0, A.mult, A.add),
-                   [("LX", t, b)], [("xr", b, j) for j in range(2)])
-            else:
-                op("V", cyc(32), lambda xr=xr, LX=LX: V.tensor_copy(xr[:, 0::16], LX), [("LX", t, b)],
-                   [("xr", b, j) for j in range(2)])
-            for st in (8, 4, 2):
-                op("V", cyc(256 // st), lambda xr=xr, st=st: V.tensor_copy(xr[:, st::2 * st], xr[:, 0::2 * st]), [("xr", b, 0)],
-                   [("xr", b, 0)])
-            op("V", cyc(256), lambda xr=xr: V.tensor_copy(xr[:, 1::2], xr[:, 0::2]), [("xr", b, 0)], [("xr", b, 1)])
-            for h in range(NC):
-                e = slice(GW * h, GW * h + GW)
-                win = T.keys[:, 0:2048] if shifted else T.keyb[:, 0:2049] if t else T.keyb[:, 0:2048]
-                off = T.LU[:, c0 + GW // 16 * h:c0 + GW // 16 * (h + 1)]
-                op("V", 60 + 1.6 * GW, lambda df=df, xr=xr, e=e, win=win, off=off: V.tensor_tensor(df[:, e], win.indirect(off),
-                                                                                                   xr[:, e], A.subtract),
-                   (["keys", "keysx"] if shifted else ["key", "keyx"] if t else ["key"])
-                   + [("LU", t, b), ("xr", b, 0), ("xr", b, 1)], [("df", b, h)])
-                op("S", 70 + GW, lambda df=df, ad=ad, e=e: S.activation(ad[:, e], df[:, e], F.Abs), [("df", b, h)], [("ad", b, h)])
-                if h == 0:
-                    op("P", 64, group([(H, wt, LX, True, True)]), [("LX", t, b), ("wt", t)], [("H", b)], banks=[bB])
-                    op("V", 68, lambda kk=kk, H=H, t=t: V.tensor_scalar(kk, H, 2.0 ** -11, T.ck[:] if t else 1025.0 - 511.5 / 1024,
-                                                                        A.mult, A.add), [("H", b), "ck"], [("kk", b)], banks=[bB])
-            op("P", 1024, group([(D, T.wd[:, 15 - i:143 - i], ad[:, i::16], i == 0, i == 15) for i in range(16)]),
-               [("ad", b, h) for h in range(NC)] + ["wd"], [("D", b)], banks=[bA])
-            op("S", 140, lambda sg=sg, D=D: S.activation(sg, D, F.Sign, bias=T.thb[:], scale=-1.0), [("D", b), "thb"],
-               [("sg", b)], banks=[bA])
-            op("P", 320, group([(PA, T.idh[:], LP, True, False), (PA, T.cnt[:], sg, False, True),
-                                (PN, wt, LX, True, False), (PN, T.nk[:], kk, False, False), (PN, T.bn[:], sg, False, True)]),
-               [("LP", t, b), ("LX", t, b), ("wt", t), ("kk", b), ("sg", b), "idh", "cnt", "nk", "bn"], [("AN", b)], banks=[bB])
-            op("S", 140, lambda sg=sg, nn=nn: S.activation(nn, sg, F.Relu, scale=-1.0), [("sg", b)], [("nn", b)])
-            op("V", 68, lambda y=y, PA=PA, t=t: V.tensor_scalar(y, PA, T.ca1[:] if t else T.ca0[:], 0.0, A.add, A.max),
-               [("AN", b), "ca1", "ca0"], [("y", b)], banks=[bB])
-            op("V", 68, lambda zh=zh, PN=PN, t=t: V.tensor_scalar(zh, PN, T.cn[:] if t else float(2048 * 1025 + 2 - 32768), 0.0,
-                                                                  A.add, A.max), [("AN", b), "cn"], [("zh", b)], banks=[bB])
-            zm = T.zm
-            op("P", 256, group([(Z[:, :, 0:16], zm[:, 0:128], y, True, False), (Z[:, :, 0:16], zm[:, 256:384], zh, False, True),
-                                (Z[:, :, 16:32], zm[:, 128:256], y, True, False),
-                                (Z[:, :, 16:32], zm[:, 384:512], zh, False, True)]),
-               [("y", b), ("zh", b), "zm"], [("Z", b)], banks=[bA])
-            op("V", cyc(128), lambda zt=zt, Z=Z: V.transpose(zt, Z), [("Z", b)], [("zt", b)], banks=[bA])
-            op("P", 128 + 64 * (t > 0), group([(Q, T.idh[:], LP, True, False)]
-                                              + ([(Q, T.idh[:], T.oh[:], False, False)] if shifted else [])
-                                              + [(Q, T.n4[:], nn, False, True)]),
-               [("LP", t, b), ("nn", b), "idh", "oh", "n4"], [("Q", b)], banks=[bA])
-            op("V", 68, lambda cc=cc, zt=zt: V.tensor_scalar(cc, zt[:, :, 0], 0.5, -1.25, A.mult, A.add), [("zt", b)], [("cc", b)])
-            clw = T.clb[:, 0:1025] if t else T.clb[:, 0:1024]
-            op("V", 170, lambda cm=cm, cc=cc, nn=nn, clw=clw: V.tensor_tensor(cm, clw.indirect(cc), nn, A.mult),
-               [("cc", b), ("nn", b), "cl"] + (["clx"] if t else []), [("cm", b)])
-            SP, SU, SX = T.SP[:, cs], T.SU[:, cs], T.SX[:, cs]
-            op("V", 68, lambda SP=SP, cm=cm, Q=Q: V.tensor_tensor(SP, cm, Q, A.max), [("cm", b), ("Q", b)], [("SP", t, b)],
-               banks=[bA])
-            op("V", 68, lambda SU=SU, SP=SP: V.tensor_copy(SU, SP), [("SP", t, b)], [("SU", t, b)])
-            emw = T.emt[:, 0:2049] if t else T.emt[:, 0:2048]
-            for h in range(NC):
-                e = slice(GW * h, GW * h + GW)
-                off = T.SU[:, c0 + GW // 16 * h:c0 + GW // 16 * (h + 1)]
-                op("S", 80 + 1.6 * GW, lambda eg=eg, e=e, emw=emw, off=off: S.activation(eg[:, e], emw.indirect(off), F.Copy),
-                   [("SU", t, b), "em"] + (["emx"] if t else []), [("eg", b, h)])
+            D, Q, E, TK, SC = [pa[:, 64 * i:64 * i + 64] for i in range(5)]
+            H, PA, VT = pb[:, 0:2, :], pb[:, 2:6, :], pb[:, 6:8, :]
+            xs, xr, df, ad, eg = [T["%s%d" % (n, b)] for n in ("xs", "xr", "df", "ad", "eg")]
+            bl, b4, b128 = slice(LB * b, LB * b + LB), slice(4 * b, 4 * b + 4), slice(128 * b, 128 * b + 128)
+            kk, sg, cm, LU, SU, vt, sc, eq = [T[n][:, bl] for n in ("kk", "sg", "cm", "LU", "SU", "vt", "sc", "eq")]
+            at, am, cc = T.at[:, b128], T.am[:, b128], T.cc[:, b4]
+            SP, SX = T.SA[:, j, 0:64], T.SA[:, j, 64:128]
+            LP = T.P0[:, bl] if t == 0 else T.LA[:, b, 0:64] if t == 1 else T.SA[:, j - NB, 0:64]
+            oh = T.oh[:, LB * j:LB * j + LB]
+            x = xr[:, 0::16]
+            kP, kx = ("LP", j) if t < 2 else ("SP", j - NB), ("xs", b)
+            lu = "LU" if t < 2 or wrap else "SU"
+            if t == 0:
+                cp(LU, T.plb[:, bl], ["plb"], [("LU", b)])
+                lin(ENG["xs"], xs[:, 0::16], T.qb[:, bl], 1.0, 0.0, ["qb"], [kx])
+                cp(LP, T.plb[:, bl], ["plb"], [kP])
+            elif lu == "LU":
+                lin(ENG["lu"], LU, LP, 1.0, float(wrap), [kP], [("LU", b)])
+            if t == 1:
+                lin(ENG["xs"], xs[:, 0::16], T.LA[:, b, 64:128], 1.0, -XO, [kP], [kx])
+            for h in range(NX):
+                w = 1024 // NX
+                scan(xr[:, w * h:w * h + w], T.m16[:, 0:w], xs[:, w * h:w * h + w], A.add, [kx, "m16"], [("xr", b, h)], w // 2)
+            XR = [("xr", b, h) for h in range(NX)]
+            win = key[:, 0:2049] if t else key[:, 0:2048]
+            for h in range(NK):
+                w = 1024 // NK
+                e = slice(w * h, w * h + w)
+                off = T[lu][:, LB * b + w // 16 * h:LB * b + w // 16 * (h + 1)]
+                tt(df[:, e], win.indirect(off), xr[:, e], A.subtract,
+                   (tab("key", k) if t else ["key"]) + [(lu, b)] + XR[h * NX // NK:((h + 1) * NX - 1) // NK + 1], [("df", b, h)],
+                   60 + GAM * w)
+                act(ad[:, e], df[:, e], F.Abs, [("df", b, h)], [("ad", b, h)], w)
+            mm([(H, cs[:, 0:128], x, True, True)], XR + (tab("cs", k) if k else ["wm"]), [("H", b)], bB)
+            lin(ENG["kk"], kk, H, T.ksc[:], T.kb1[:] if wrap else T.kb0[:], [("H", b), "ksc", "kb0", "kb1"], [("kk", b)], banks=[bB])
+            for e in range(2):
+                o = PA[:, :, 16 * e:16 * e + 16]
+                mm([(o, T["ih%d" % e][:], LP, e == 0, False), (o, cs[:, 128 * e + 128:128 * e + 256], x, False, False),
+                    (o, T["km%d" % e][:], kk, False, False)],
+                   XR + [kP, ("kk", b), ("ih", e), ("km", e)] + (tab("cs", k) if k else [("wx", e)]), [("PA", b)], bB)
+            for h in range(NP):
+                mm([(D, T.wd[:, 15 - i:143 - i], ad[:, i::16], i == 0, i == 15) for i in range(16 // NP * h, 16 // NP * (h + 1))],
+                   [("ad", b, i) for i in range(NK)] + ["wd"], [("D", b)], bA)
+            act(sg, D, F.Sign, [("D", b), ("th", k)], [("sg", b)], 64, [bA], T["th%d" % k][:])
+            mm([(PA[:, :, 16 * e:16 * e + 16], T["sm%d" % e][:], sg, False, e == 1) for e in range(2)],
+               [("sg", b), ("sm", 0), ("sm", 1)], [("PA", b)], bB)
+            mm([(Q, T.idh[:], LP, True, False), (Q, T.cq[:], kk, False, False), (Q, T.n2[:], sg, False, True)],
+               [kP, ("kk", b), ("sg", b), "idh", "cq", "n2"], [("Q", b)], bA)
+            turn(at, PA, [("PA", b)], [("at", b)], 128, [bB])
+            scan(am, T.m32[:], at, A.max, [("at", b), "m32"], [("am", b)], 128)
+            lin(ENG["cc"], cc, am[:, 31::32], 0.5, -0.25, [("am", b)], [("cc", b)])
+            clw = clb[:, 0:1025] if t else clb[:, 0:1024]
+            tt(cm, clw.indirect(cc), sg, A.mult, [("cc", b), ("sg", b)] + (tab("cl", k) if t else ["cl"]), [("cm", b)], 60 + GAM * 64)
+            tt(SP, cm, Q, A.max, [("cm", b), ("Q", b)], [("SP", j)], banks=[bA])
+            lin(ENG["su"], SU, SP, 1.0, 0.0, [("SP", j)], [("SU", b)])
+            mm([(VT, T.cv[:], kk, True, False)], [("kk", b), "cv"], [("VT", b)], bB)
+            mm([(E, T.idb[:], x, True, False)], XR + ["idb"], [("E", b)], bA)
+            emw = emt[:, 0:2049] if t else emt[:, 0:2048]
+            for h in range(NE):
+                w = 1024 // NE
+                off = T.SU[:, LB * b + w // 16 * h:LB * b + w // 16 * (h + 1)]
+                act(eg[:, w * h:w * h + w], emw.indirect(off), F.Copy, [("SU", b)] + (tab("em", k) if t else ["em"]), [("eg", b, h)],
+                    78 + GAM * w)
             if t == NT - 1:
-                ts(T.ip[:, bl], SP, 1.0 if rank == NR - 1 else 0.0, None, A.add, None, [("SP", t, b)], [("ip", b)], 64)
-                ts(T.iq[:, bl], T.ip[:, bl], 2047, None, A.bitwise_and, None, [("ip", b)], [("iq", b)], 64)
-                cp(T.SYP[:, bl], T.iq[:, bl], [("iq", b)], [("SYP", b)], 64)
-                op("G", 900, lambda b=b, bl=bl: g.remote_dma(T.FYP[:, bl], T.SYP[:, bl], T.sem["ap%d" % b], T.sem.sent, pid, rid,
-                                                             mask(eng)), [("SYP", b)], [("fp", b)], sem="sent", val=len(eng))
-                op("N", 0, None, [("fp", b)], [("FYP", b)], sem="ap%d" % b, val=8)
-                op("Y", 80, lambda b=b, bl=bl: Y.dma_start(T.yp[:, bl], T.FYP[:, bl]), [("FYP", b)], (), sem="op%d" % b, val=16,
-                   lat=2200)
-            op("P", 17 * 64, group([(VT, T.db[:], T.ob[:, 0:64], True, False)]
-                                   + [(VT, T.idb[:], eg[:, i::16], False, i == 15) for i in range(16)]),
-               [("eg", b, h) for h in range(NC)] + ["db", "ob", "idb"], [("VT", b)], banks=[bB])
-            op("V", 68, lambda vt=vt, VT=VT: V.transpose(vt, VT), [("VT", b)], [("vt", b)], banks=[bB])
-            op("V", 68, lambda vt=vt, sc=sc: V.tensor_tensor_scan(sc, T.mk[:], vt, 0.0, A.mult, A.max), [("vt", b), "mk"],
-               [("sc", b)])
-            op("V", 68, lambda ti=ti, sc=sc: V.tensor_copy(ti, sc[:, 15::16]), [("sc", b)], [("ti", b)])
-            op("V", 68, lambda tv=tv, ti=ti, sc=sc: V.tensor_tensor(tv, sc[:, 15::16], ti, A.subtract), [("sc", b), ("ti", b)],
-               [("tv", b)])
-            op("P", 256, group([(TK[:, hf::2], T.fx[:, 256 * e + 128 * hf:256 * e + 128 * hf + 128], tv[:, e::2], e == 0, e == 1)
-                                for hf in range(2) for e in range(2)]), [("tv", b)] + [("fx", j) for j in range(4)], [("TK", b)],
-               banks=[bA])
-            tok = T.toku[:, 16 * t + 4 * b:16 * t + 4 * b + 4]
-            op("V", 68, lambda tok=tok, TK=TK: V.tensor_scalar(tok, TK, -16.0, 7.5, A.mult, A.add), [("TK", b)], [("tok", t, b)],
-               banks=[bA])
-            op("V", 170, lambda SX=SX, tok=tok, LX=LX, t=t: V.tensor_tensor(SX, T.tab[:, 16 * t:16 * t + 16].indirect(tok), LX, A.add),
-               [("tok", t, b), ("LX", t, b), ("tab", t)], [("SX", t, b)])
-            if t < NT - 1:
-                d0 = 256 * (t + 1) + LB * b
-                ds = slice(d0, d0 + LB)
-
-                def send(ds=ds, SU=SU, SP=SP, SX=SX, t=t, b=b):
-                    dst, sem = [DstId(rid=rid, pnc=pid)], T.sem[arrive(t + 1, b)]
-                    return g.remote_dma_fused([
-                        RemoteDMATransfer(dst_ids=dst, dma_engine_mask=mask(es), remote_sem=sem, src=a, dst=d)
-                        for es, a, d in ((eng[0:2], SU, T.LU[:, ds]), (eng[2:4], SP, T.LP[:, ds]), (eng[4:8], SX, T.LX[:, ds]))],
-                        local_sem=T.sem.sent)
-                op("G", 900, send, [("SU", t, b), ("SP", t, b), ("SX", t, b)], [("snd", t, b)], sem="sent", val=len(eng))
+                lin("V", T.ip[:, bl], SP, 1.0, 1.0 if rank == 0 else 0.0, [("SP", j)], [("ip", b)])
+                ts(T.iq[:, bl], T.ip[:, bl], 2047, None, A.bitwise_and, None, [("ip", b)], [("iq", b)])
+                cp(T.SYP[:, bl], T.iq[:, bl], [("iq", b)], [("SYP", b)])
+                if b == NB - 1:
+                    store(T.yp[:], T.SYP[:], "op", [("SYP", i) for i in range(NB)])
+            for h in range(NP):
+                mm([(VT, T.idb[:], eg[:, i::16], False, i == 15) for i in range(16 // NP * h, 16 // NP * (h + 1))],
+                   [("eg", b, i) for i in range(NE)] + ["idb"], [("VT", b)], bB)
+            turn(vt, VT, [("VT", b)], [("vt", b)], 64, [bB])
+            scan(sc, T.m16[:, 0:64], vt, A.max, [("vt", b), "m16"], [("sc", b)], 64)
+            scan(SC[:, ::-1], T.m16[:, 0:64], sc[:, ::-1], A.max, [("sc", b), "m16"], [("SC", b)], 64, [bA])
+            tt(eq, vt, SC, A.is_equal, [("vt", b), ("SC", b)], [("eq", b)], banks=[bA])
+            turn(oh, eq, [("eq", b)], [("oh", j)], 64)
+            mm([(E, cs[:, 384:512], oh, False, True)], [("oh", j)] + (tab("cs", k) if k else ["em2"]), [("E", b)], bA)
+            if 0 < t < NT - 1:
+                lin(ENG["sx"], xs[:, 0::16], E, 0.5, -0.25, [("E", b)], [("SX", j), kx], banks=[bA])
             else:
-                ts(T.SYQ[:, bl], SX, 2.0 ** -NT, -1024.0, A.mult, A.add, [("SX", t, b)], [("SYQ", b)], 32)
-                op("G", 900, lambda b=b, bl=bl: g.remote_dma(T.FYQ[:, bl], T.SYQ[:, bl], T.sem["aq%d" % b], T.sem.sent, pid, rid,
-                                                             mask(eng)), [("SYQ", b)], [("fq", b)], sem="sent", val=len(eng))
-                op("N", 0, None, [("fq", b)], [("FYQ", b)], sem="aq%d" % b, val=8)
-                op("Y", 80, lambda b=b, bl=bl: Y.dma_start(T.yq[:, bl], T.FYQ[:, bl]), [("FYQ", b)], (), sem="oq%d" % b, val=16,
-                   lat=2200)
-        if t == 1:
-            yt_out(0, [0, 1])
-        if t == 3:
-            yt_out(1, [2, 3])
-    yt_out(2, [4])
+                lin(ENG["sx"], SX, E, 0.5, XO - 0.25, [("E", b)], [("SX", j)], banks=[bA])
+            if t == 0:
+                send(rank + 1, "lanes", T.LA[:, b, :], T.SA[:, j, :], "ar%d" % b, [("SP", j), ("SX", j)])
+                arrival(rank - 1, "lanes", "ar%d" % b, [("snd", "ar%d" % b)], [("LP", j + NB)])
+            if t == NT - 1:
+                lin(ENG["sx"], T.SYQ[:, bl], SX, 1.0, -XO, [("SX", j)], [("SYQ", b)])
+                if b >= NB - 2:
+                    c = slice(0, 192) if b == NB - 2 else bl
+                    store(T.yq[:, c], T.SYQ[:, c], "oq%d" % (b - NB + 2), [("SYQ", i) for i in range(b + 1)])
+            if b == NB - 1:
+                mm([(TK, T.wk[:, 3 - i:131 - i], T.oh[:, LB * (NB * t + i):LB * (NB * t + i + 1)], i == 0, i == NB - 1)
+                    for i in range(NB)], [("oh", NB * t + i) for i in range(NB)] + ["wk"], ["TK"], bA)
+                c = slice(LB * t, LB * t + LB)
+                act(T.ytb[:, c], TK, F.Copy, ["TK"], [("yt", t)], 64, [bA])
+                if k:
+                    send(rank + k, "tok", T.ytl[:, c], T.ytb[:, c], "ay%d" % t, [("yt", t)])
+                    arrival(rank - k, "tok", "ay%d" % t, [("snd", "ay%d" % t)], [("yl", t)])
+                store(T.yt[:, 256 * t:256 * t + 256], T["ytl" if k else "ytb"][0:32, c], "oy%d" % t, [("yl" if k else "yt", t)])
+        if t == 0:
+            for i in range(2, NR):
+                hand_on(i, False)
 
     schedule(ops)
     emit_all(ops, {"V": V, "S": S, "P": P, "G": g, "Y": Y}, T, g)
@@ -323,13 +351,37 @@ def rank_program(g, core, T, topo):
 CNT_SEM = {"V": "cv", "S": "cs", "P": "ct", "G": "cg"}
 
 
+def place(ops, order, before, gap, first):
+    start, slots = [0.0] * len(ops), {q: [] for q in "VSPGY"}
+    for i in order:
+        o = ops[i]
+        st = max([start[d] + ops[d]["dur"] + gap(d, i) for d in before[i]] + [first[i]])
+        if o["q"] != "N":
+            sl = slots[o["q"]]
+            at, hi = 0, len(sl)
+            while at < hi:
+                mid = (at + hi) // 2
+                if sl[mid][1] > st:
+                    hi = mid
+                else:
+                    at = mid + 1
+            while at < len(sl) and sl[at][0] < st + o["dur"]:
+                st = max(st, sl[at][1])
+                at += 1
+            sl.insert(at, (st, st + o["dur"]))
+        start[i] = st
+    return start
+
+
 def schedule(ops):
     lastw, readers, bank = {}, {}, {}
     for o in ops:
-        d = set()
+        d, order = set(), set()
         for k in o["R"]:
             if k in lastw:
                 d.add(lastw[k])
+                if k in ("LG", "LY", "LS"):
+                    order.add(lastw[k])
             readers.setdefault(k, []).append(o["i"])
         for k in o["W"]:
             if k in lastw:
@@ -337,63 +389,47 @@ def schedule(ops):
             d.update(readers.get(k, []))
             lastw[k], readers[k] = o["i"], []
         for k in o["banks"]:
-            for q, i in bank.setdefault(k, [])[-40:]:
-                if q != o["q"]:
+            for q, i in bank.setdefault(k, {}).items():
+                if q != o["q"] or q == "P":
                     d.add(i)
-            bank[k].append((o["q"], o["i"]))
+            bank[k][o["q"]] = o["i"]
         d.discard(o["i"])
-        o["D"] = d
+        if o["q"] == "P":
+            order = {i for i in d if ops[i]["q"] == "P"}
+        o["D"], o["O"] = d, order
     n = len(ops)
-    succ = [[] for _ in range(n)]
+    pred, succ = [sorted(o["D"]) for o in ops], [[] for _ in range(n)]
     for o in ops:
         for d in o["D"]:
             succ[d].append(o["i"])
-    tail = [0.0] * n
+        o["after"] = o["lat"] + (CFG["link"] if o["q"] == "N" else CFG["hop"])
+
+    def gap(d, i):
+        return 0.0 if d in ops[i]["O"] else ops[d]["after"]
+
+    def gap_back(d, i):
+        return gap(i, d)
+
+    key = [0.0] * n
     for o in reversed(ops):
-        w = max([tail[s] for s in succ[o["i"]]] + [0])
-        tail[o["i"]] = w + o["dur"] + o["lat"] + (LINK if o["q"] == "N" else HOP)
-    free = {q: 0.0 for q in "VSPGYN"}
-    left = [len(o["D"]) for o in ops]
-    ready = {q: [] for q in "VSPGYN"}
-    avail = [0.0] * n
-    for o in ops:
-        if not left[o["i"]]:
-            ready[o["q"]].append(o["i"])
-    done = 0
-    while done < n:
-        best = None
-        for q in "VSPGYN":
-            if not ready[q]:
-                continue
-            if q == "N":
-                i = min(ready[q], key=lambda j: avail[j])
-                st = avail[i]
-            else:
-                st = max(free[q], min(avail[j] for j in ready[q]))
-                i = max((j for j in ready[q] if avail[j] <= st + 1e-9), key=lambda j: tail[j] + ops[j]["bias"])
-            if best is None or st < best[0]:
-                best = (st, q, i)
-        st, q, i = best
-        o = ops[i]
-        ready[q].remove(i)
-        o["st"] = st
-        end = st + o["dur"]
-        if q != "N":
-            free[q] = end
-        fin = end + o["lat"] + (LINK if q == "N" else HOP)
-        o["end"] = fin
-        done += 1
-        for s in succ[i]:
-            avail[s] = max(avail[s], fin)
-            left[s] -= 1
-            if not left[s]:
-                ready[ops[s]["q"]].append(s)
+        mine = CFG["per"] * o["seq"] + CFG["off"].get(o["kind"], 1e9) if o["kind"] else -o["bias"] if o["bias"] else 1e9
+        key[o["i"]] = min([mine] + [key[s] - o["dur"] for s in succ[o["i"]]])
+    best, last = None, [o.get("due", 0.0) if succ[o["i"]] else o["lat"] for o in ops]
+    for turn in range(CFG["rounds"]):
+        start = place(ops, sorted(range(n), key=lambda i: (key[i], i)), pred, gap, [0.0] * n)
+        ends = [start[i] + ops[i]["dur"] + last[i] for i in range(n)]
+        if best is None or max(ends) < best[0]:
+            best = (max(ends), start)
+        back = place(ops, sorted(range(n), key=lambda i: (-ends[i], -i)), succ, gap_back, last)
+        key = [-(back[i] + ops[i]["dur"]) for i in range(n)]
+    for i, o in enumerate(ops):
+        o["st"], o["end"] = best[1][i], best[1][i] + o["dur"] + o["after"]
+    return best[0]
 
 
 def emit_all(ops, queues, T, g):
-    order = sorted((o for o in ops if not o["skip"]), key=lambda o: (o["st"], o["i"]))
     count, known, total, clock = {}, {q: {} for q in "VSPGYN"}, {}, {}
-    for o in order:
+    for o in sorted(ops, key=lambda o: (o["st"], o["i"])):
         q = o["q"]
         kn = known[q]
         if q == "N":
@@ -402,9 +438,7 @@ def emit_all(ops, queues, T, g):
             o["tok"] = (o["sem"], o["val"])
             continue
         eng = queues[q]
-        for d in sorted((ops[i] for i in o["D"]), key=lambda x: -x["end"]):
-            if d["skip"]:
-                continue
+        for d in sorted((ops[i] for i in o["D"] - o["O"]), key=lambda x: -x["end"]):
             s, v = d["tok"]
             if kn.get(s, 0) >= v:
                 continue

@@ -1,16 +1,17 @@
 from concourse.mybir import AluOpType, ActivationFunctionType
+from concourse.bass import DstId, RemoteDMATransfer
 
 NR, NB, LB, NT = 4, 4, 64, 5
 XO = 1536.0
 CFG = {"nk": 2, "ne": 2, "nx": 2, "np": 4,
-       "f": 1.2, "gam": 1.56, "hop": 180, "link": 2600, "iss": 700, "rounds": 1, "per": 3260,
-       "off": {'xr0': 6740, 'xr1': 3850, 'df0': -550, 'ad0': 8500, 'df1': 950, 'ad1': 11080, 'H0': 5470, 'kk0': -900, 'PA0': 2010,
-               'PA1': 4680, 'D0': 4940, 'D1': 1530, 'D2': 3930, 'D3': 3070, 'sg0': 3590, 'PA2': 2330, 'Q0': 7000, 'at0': 13380,
-               'am0': 3490, 'cc0': 5260, 'cm0': 16090, 'SP0': 6270, 'SU0': 11280, 'VT0': 9880, 'E0': 10450, 'eg0': 6070, 'eg1': 5330,
-               'VT1': 7500, 'VT2': 12480, 'VT3': 7550, 'VT4': 17950, 'vt0': 9450, 'sc0': 11360, 'SC0': 9810, 'eq0': 11530,
-               'oh0': 13080, 'E1': 14810, 'SX0': 10410},
-       "tab": [27000, 42000, 57000], "piece": 2000, "due": 70000, "ahead": ["key"],
-       "eng": {"lu": "V", "xs": "S", "kk": "S", "cc": "V", "su": "S", "sx": "S"}}
+       "f": 1.2, "gam": 1.56, "hop": 180, "link": 2600, "iss": 700, "per": 3302, "move": 4,
+       "off": {'xr0': 10160, 'xr1': 2570, 'df0': 2390, 'ad0': 13410, 'df1': 2560, 'ad1': 11570, 'H0': 9030, 'kk0': 3080, 'PA0': 8440,
+               'PA1': 10740, 'D0': 1880, 'D1': 10550, 'D2': 9990, 'D3': 4110, 'sg0': 1960, 'PA2': 6740, 'Q0': 14120, 'at0': 2380,
+               'am0': 4470, 'cc0': 3630, 'cm0': 19850, 'SP0': 13020, 'SU0': 8800, 'VT0': 25030, 'E0': 13010, 'eg0': 8500,
+               'eg1': 5180, 'VT1': 7100, 'VT2': 9530, 'VT3': 32110, 'VT4': 21720, 'vt0': 8610, 'sc0': 7640, 'SC0': 28400,
+               'eq0': 13800, 'oh0': 20490, 'E1': 20150, 'SX0': 10640, 'SYP0': 9500},
+       "tab": [14000, 28000, 42000], "piece": 2000, "due": 70000, "ahead": ["key", "cs", "cl", "em"],
+       "eng": {"lu": "V", "xs": "S", "kk": "S", "cc": "V", "sp": "S", "sx": "S"}, "both": 2}
 
 SCRATCH = {
     "plb": ("sbuf", [128, 256], "int32"), "qb": ("sbuf", [128, 256], "bfloat16"),
@@ -18,8 +19,10 @@ SCRATCH = {
     "LU": ("sbuf", [128, 256], "uint16"), "SU": ("sbuf", [128, 256], "uint16"),
     "LA": ("sbuf", [128, 4, 128], "float16"), "P0": ("sbuf", [128, 256], "float16"), "SA": ("sbuf", [128, 20, 128], "float16"),
     "SYP": ("sbuf", [128, 256], "float32"), "SYQ": ("sbuf", [128, 256], "bfloat16"),
+    "FYP": ("sbuf", [128, 256], "float32"), "FYQ": ("sbuf", [128, 256], "bfloat16"),
     "ip": ("sbuf", [128, 256], "int32"), "iq": ("sbuf", [128, 256], "int32"),
-    "m16": ("sbuf", [128, 1024], "bfloat16"), "m32": ("sbuf", [128, 128], "float32"),
+    "xs0": ("sbuf", [128, 1024], "uint16"), "xs1": ("sbuf", [128, 1024], "uint16"),
+    "m16": ("sbuf", [128, 1024], "bfloat16"), "m32": ("sbuf", [128, 128], "bfloat16"),
     "wd": ("sbuf", [128, 144], "bfloat16"), "wk": ("sbuf", [128, 132], "bfloat16"),
     "ii": ("sbuf", [128, 1], "int32"), "ik": ("sbuf", [128, 1], "int32"), "i16": ("sbuf", [128, 1], "int32"),
     "oh": ("sbuf", [128, 1280], "bfloat16"), "ytb": ("sbuf", [128, 320], "float32"), "ytl": ("sbuf", [128, 320], "float32"),
@@ -28,11 +31,11 @@ for _k in range(NR):
     SCRATCH.update({"key%d" % _k: ("sbuf", [128, 2064], "bfloat16"), "em%d" % _k: ("sbuf", [128, 2064], "bfloat16"),
                     "cl%d" % _k: ("sbuf", [128, 1032], "int32"), "cs%d" % _k: ("sbuf", [128, 512], "bfloat16"),
                     "th%d" % _k: ("sbuf", [128, 1], "float32")})
-for _n in ("ob", "bm0", "bm", "idb", "ub", "xc", "ci", "t1", "t2", "sm0", "sm1", "n2"):
+for _n in ("ob", "bm0", "bm", "idb", "ub", "ci", "c1", "c2", "t1", "e1", "sm0", "sm1", "n2"):
     SCRATCH[_n] = ("sbuf", [128, 128], "bfloat16")
-for _n in ("idh", "ih0", "ih1", "k1", "k2", "k3", "k4", "k5", "km0", "km1", "cq", "cv"):
+for _n in ("idh", "ih0", "ih1", "k5", "km0", "km1", "cv"):
     SCRATCH[_n] = ("sbuf", [128, 128], "float16")
-for _n in ("kc", "odd", "even", "r0", "r1", "r2", "r3", "ksc", "kb", "kb0", "kb1", "xk", "xk1", "rq", "we", "wo"):
+for _n in ("kc", "odd", "even", "r0", "r1", "r2", "ksc", "kb", "kb0", "xk", "xk1", "wf"):
     SCRATCH[_n] = ("sbuf", [128, 1], "float32")
 for _n, _s, _d in (("kk", [128, 256], "float16"), ("sg", [128, 256], "bfloat16"), ("at", [128, 512], "float32"),
                    ("am", [128, 512], "float32"), ("cc", [128, 16], "uint16"), ("cm", [128, 256], "float16"),
@@ -40,48 +43,64 @@ for _n, _s, _d in (("kk", [128, 256], "float16"), ("sg", [128, 256], "bfloat16")
     SCRATCH[_n] = ("sbuf", _s, _d)
 for _b in range(NB):
     SCRATCH.update({
-        "xs%d" % _b: ("sbuf", [128, 1024], "uint16"),
         "xr%d" % _b: ("sbuf", [128, 1024], "bfloat16"), "df%d" % _b: ("sbuf", [128, 1024], "bfloat16"),
         "ad%d" % _b: ("sbuf", [128, 1024], "bfloat16"), "eg%d" % _b: ("sbuf", [128, 1024], "bfloat16"),
         "pa%d" % _b: ("psum", [128, 512], "float32"), "pb%d" % _b: ("psum", [128, 16, 32], "float32"),
     })
-PIECES = {"key": 2049, "cs": 512, "cl": 1026, "em": 2049}
+PIECES = {"key": 2064, "cl": 1032, "cs": 512, "em": 2064}
+SPLIT = ["key", "cl", "em"]
 LOADS = ["pl", "q", "key", "w", "th", "cl", "emb", "em"]
 SEMAPHORES = (["cv", "cs", "ct", "cg", "sent"] + ["ld_" + n for n in LOADS]
               + ["ar%d" % b for b in range(NB)] + ["a%s%d" % (n, k) for n in PIECES for k in range(1, NR)]
-              + ["op", "oq0", "oq1"] + ["oy%d" % t for t in range(NT)] + ["ay%d" % t for t in range(2, NT)])
+              + ["h%s%d" % (n, k) for n in SPLIT for k in range(1, NR)]
+              + ["op", "oq0", "oq1", "ap", "aq0", "aq1"] + ["oy%d" % t for t in range(NT)] + ["ay%d" % t for t in range(NT)])
 
 
 def rank_program(g, core, T, topo):
     rank = T.rank_of(core)
+
+    def at(r):
+        return T.cores[r % NR]
+
+    def near(a, b):
+        return at(b) in topo.cores_of(at(a))
+
+    def helper(r):
+        return [c for c in topo.cores_of(at(r))
+                if topo.die(c) != topo.die(at(r)) and T.rank_of(c) is None and topo.may_write(c, at(r - 1))][0]
+
+    def giver(k, r):
+        return r + k if near(r, r + k) else r + 1
+
+    def halves(n):
+        return slice(0, PIECES[n] // 2), slice(PIECES[n] // 2, PIECES[n])
+
     if rank is None:
+        for r in range(NR):
+            if not near(r, r - 1) and core == helper(r):
+                rid, pid = topo.addr(at(r - 1), core)
+                came = len(topo.engines(at(r), core)) - len(topo.engines(at(r), at(r - 1)))
+                far = [(k, n) for k in range(1, NR) for n in SPLIT if not near(r - 1, r - 1 + k)]
+                for k, n in far:
+                    part = T["%s%d" % (n, k)][:, halves(n)[1]]
+                    g.wait_ge(T.sem["h%s%d" % (n, k)], came)
+                    g.remote_dma(part, part, T.sem["a%s%d" % (n, k)], T.sem.sent, pid, rid, topo.mask(core, at(r - 1)))
+                g.wait_ge(T.sem.sent, len(far) * len(topo.engines(core, at(r - 1))))
         return
     A, F = AluOpType, ActivationFunctionType
     V, S, P, Y = g.vector, g.scalar, g.tensor, g.sync
     ops, seq, seen = [], [None], {}
-    NK, NE, NX, NP, ENG, GAM = CFG["nk"], CFG["ne"], CFG["nx"], CFG["np"], CFG["eng"], CFG["gam"]
-
-    def near(a, b):
-        return T.cores[b % NR] in topo.cores_of(T.cores[a % NR])
-
-    def engines(a, b, kind):
-        ca = T.cores[a % NR]
-        out = topo.engines(ca, T.cores[(a + 2) % NR])
-        if near(a, b):
-            return [e for e in topo.engines(ca, T.cores[b % NR]) if e not in out]
-        return out
-
-    def giver(k, r):
-        return r + 1 if near(r, r + 1) else r + k
+    NK, NE, NX, NP, ENG, GAM, MOVE = CFG["nk"], CFG["ne"], CFG["nx"], CFG["np"], CFG["eng"], CFG["gam"], CFG["move"]
 
     def op(q, dur, emit, R=(), W=(), banks=(), sem=None, val=1, lat=0, bias=0):
         kind = None
         if seq[0] is not None and q in "VSP" and not isinstance(W[0], str):
             seen[seq[0], W[0][0]] = seen.get((seq[0], W[0][0]), 0) + 1
             kind = "%s%d" % (W[0][0], seen[seq[0], W[0][0]] - 1)
-        ops.append({"q": q, "dur": dur * (0.83 * CFG["f"] if q in "VSP" else 1), "emit": emit, "R": list(R), "W": list(W),
-                    "banks": list(banks), "sem": sem, "val": val, "lat": lat, "i": len(ops), "bias": bias, "seq": seq[0],
-                    "kind": kind})
+        cyc, gat = dur if isinstance(dur, tuple) else (dur, 0)
+        ops.append({"q": q, "cyc": cyc, "gat": gat, "dur": (cyc + GAM * gat) * (0.83 * CFG["f"] if q in "VSP" else 1), "emit": emit,
+                    "R": list(R), "W": list(W), "banks": list(banks), "sem": sem, "val": val, "lat": lat, "i": len(ops),
+                    "bias": bias, "seq": seq[0], "kind": kind})
 
     def load(q, name, fn, W, done):
         op(q, 80, fn, ["L" + q], W + ["L" + q], sem="ld_" + name, val=16, lat=done, bias=1e7)
@@ -124,11 +143,15 @@ def rank_program(g, core, T, topo):
             return last
         op("P", 64 * len(ms_), f, R, W, [bank])
 
-    def aff(out, src, pat, cmp, base, cm):
-        op("G", 460, lambda: g.affine_select(T[out][:], T[src][:], pat, cmp, 0.0, base, cm), [src], [out])
+    def aff(out, src, pat, cmp, base, cm, fill=0.0, R=(), W=()):
+        op("G", 460, lambda: g.affine_select(out, src, pat, cmp, fill, base, cm), R, W)
 
+    def inside(out, tmp, src, R, W):
+        aff(T[tmp][:], src, [[-16, 8], [0, 16]], A.is_ge, 0, 1, R=R, W=[tmp])
+        aff(out, T[tmp][:], [[16, 8], [0, 16]], A.is_ge, 15, -1, R=[tmp], W=W)
+
+    load("S", "q", lambda: S.dma_start(T.qb[:], T.q[:]), ["qb"], 2000)
     load("Y", "pl", lambda: Y.dma_start(T.plb[:], T.pl[:]), ["plb"], 2300)
-    load("S", "q", lambda: S.dma_start(T.qb[:], T.q[:]), ["qb"], 2300)
     load("Y", "key", lambda: Y.dma_start(T.key0[:, 0:2048], T.key[:]), ["key"], 4600)
     load("S", "w", lambda: S.dma_start(T.wb[:], T.w[:]), ["wb"], 4700)
     load("S", "th", lambda: S.dma_start(T.thf[:], T.th[:]), ["thf"], 4800)
@@ -138,104 +161,116 @@ def rank_program(g, core, T, topo):
 
     ms(T.ob[:], 1.0, ["ob"])
     op("G", 140, lambda: g.iota(T.ii[:], [[0, 1]], 0, 1), (), ["ii"])
-    aff("bm0", "ob", [[-16, 8], [0, 16]], A.is_ge, 0, 1)
-    aff("bm", "bm0", [[16, 8], [0, 16]], A.is_ge, 15, -1)
-    aff("idb", "ob", [[-1, 128]], A.is_equal, 0, 1)
-    aff("ub", "bm", [[1, 128]], A.is_ge, -1, -1)
-    op("G", 400, lambda: g.iota(T.ci[:], [[0, 8], [1, 16]], 1, 0, allow_small_or_imprecise_dtypes=True), (), ["ci"])
-    for k in range(NB):
-        ms(T["xs%d" % k][:], 0, [("xs", k)], 512)
-    ms(T.m16[:, 0:1024 // NX], 1.0, ["m16"], 512 // NX)
-    ms(T.m16[:, 0:1024 // NX:16], 0.0, ["m16"])
-    ms(T.m32[:], 1.0, ["m32"], 128)
+    inside(T.bm[:], "bm0", T.ob[:], ["ob"], ["bm"])
+    aff(T.idb[:], T.ob[:], [[-1, 128]], A.is_equal, 0, 1, R=["ob"], W=["idb"])
+    aff(T.ub[:], T.bm[:], [[1, 128]], A.is_ge, -1, -1, R=["bm"], W=["ub"])
+    aff(T.t1[:], T.ub[:], [[1, 128]], A.not_equal, 0, -1, -1.0, ["ub"], ["t1"])
+    op("G", 400, lambda: g.iota(T.ci[:], [[0, 8], [-1, 16]], 0, 0, allow_small_or_imprecise_dtypes=True), (), ["ci"])
+    inside(T.c2[:], "c1", T.ci[:], ["ci"], ["c2"])
+    ms(T.xs0[:], 0, [("xs", 0)], 512)
+    ms(T.m16[:, 0:512], 1.0, ["m16"], 256)
+    ms(T.m16[:, 0:512:16], 0.0, ["m16"])
+    for h in range(2):
+        lin("S", T.xs1[:, 512 * h:512 * h + 512], T.m16[:, 0:512], 0.0, 0.0, ["m16"], [("xs", 1)], 512)
+    ms(T.m32[:], 1.0, ["m32"])
     ms(T.m32[:, 0::32], 0.0, ["m32"])
     ts(T.ik[:], T.ii[:], 15, None, A.bitwise_and, None, ["ii"], ["ik"])
     ts(T.i16[:], T.ii[:], 16, None, A.bitwise_and, None, ["ii"], ["i16"])
     cp(T.kc[:], T.ik[:], ["ik"], ["kc"])
     ts(T.odd[:], T.i16[:], 0.0625, None, A.mult, None, ["i16"], ["odd"])
     lin("S", T.even[:], T.odd[:], -1.0, 1.0, ["odd"], ["even"])
-    for j in range(4):
+    for j in range(3):
         ts(T["r%d" % j][:], T.kc[:], float(j), None, A.is_equal, None, ["kc"], ["r%d" % j])
     lin("S", T.th0[:], T.thf[:], -1.0, 0.5, ["thf"], [("th", 0)])
+    lin("S", T.wf[:], T.wb[:], 1.0, 0.0, ["wb"], ["wf"])
     ms(T.wd[:], 0.0, ["wd"], 72)
     cp(T.wd[:, 15:128:16], T.bm[:, 0::16], ["bm"], ["wd"])
     ms(T.wk[:], 0.0, ["wk"], 66)
-    ts(T.wk[:, 3:35:4], T.bm[:, 0::16], T.kc[:], None, A.mult, None, ["bm", "kc"], ["wk"])
-    ms(T.xc[:], 0.0, ["xc"])
-    cp(T.xc[:, 16::32], T.bm[:, 0::32], ["bm"], ["xc"])
-    cp(T.xc[:, 0::32], T.bm[:, 16::32], ["bm"], ["xc"])
+    lin("S", T.wk[:, 3:35:4], T.bm[:, 0::16], T.kc[:], 0.0, ["bm", "kc"], ["wk"])
     lin("S", T.ksc[:], T.r0[:], 2.0 ** -10, 0.0, ["r0"], ["ksc"])
-    lin("S", T.kb[:], T.r1[:], 2048.0, T.r3[:], ["r1", "r3"], ["kb"])
-    lin("S", T.kb0[:], T.r0[:], 1025.0 - 511.5 / 1024, T.kb[:], ["r0", "kb"], ["kb0"])
-    lin("S", T.kb1[:], T.r2[:], 1.0, T.kb0[:], ["r2", "kb0"], ["kb1"])
+    lin("S", T.kb[:], T.r2[:], 2.0 ** -15, T.r1[:], ["r1", "r2"], ["kb"])
+    lin("S", T.xk[:], T.r0[:], (1025.0 - 511.5 / 1024) / 2048, T.kb[:], ["r0", "kb"], ["xk"])
+    lin("S", T.kb0[:], T.xk[:], 2048.0, 0.0, ["xk"], ["kb0"])
     lin("S", T.xk1[:], T.r1[:], 1009.0, 0.0, ["r1"], ["xk1"])
     lin("S", T.xk[:], T.r0[:], -2048.0, T.xk1[:], ["r0", "xk1"], ["xk"])
-    lin("S", T.rq[:], T.r1[:], -1.0, T.r2[:], ["r1", "r2"], ["rq"])
-    lin("S", T.we[:], T.wb[:], T.even[:], 0.0, ["wb", "even"], ["we"])
-    lin("S", T.wo[:], T.wb[:], T.odd[:], 0.0, ["wb", "odd"], ["wo"])
-    par = [("even", "we"), ("odd", "wo")]
-    cp(T.idh[:], T.idb[:], ["idb"], ["idh"])
-    ts(T.n2[:], T.idb[:], -2048.0, None, A.mult, None, ["idb"], ["n2"])
-    ts(T.cs0[:, 0:128], T.bm[:], T.wb[:], None, A.mult, None, ["bm", "wb"], ["wm"])
-    tt(T.t1[:], T.ub[:], T.idb[:], A.subtract, ["ub", "idb"], ["t1"], 256)
-    tt(T.t2[:], T.t1[:], T.xc[:], A.add, ["t1", "xc"], ["t2"], 256)
-    ts(T.k1[:], T.ci[:], T.rq[:], 1.0, A.mult, A.min, ["ci", "rq"], ["k1"])
-    tt(T.k3[:], T.k1[:], T.bm[:], A.mult, ["k1", "bm"], ["k3"], 256)
-    lin("S", T.k4[:], T.xc[:], T.xk[:], 0.0, ["xc", "xk"], ["k4"], 128)
-    tt(T.k5[:], T.k3[:], T.k4[:], A.add, ["k3", "k4"], ["k5"], 256)
-    for e, (c, w) in enumerate(par):
-        ts(T["sm%d" % e][:], T.t2[:], T[c][:], 2048.0, A.mult, A.mult, ["t2", c], [("sm", e)])
+    lin("S", T.idh[:], T.idb[:], 1.0, 0.0, ["idb"], ["idh"], 128)
+    lin("S", T.n2[:], T.idb[:], -2048.0, 0.0, ["idb"], ["n2"], 128)
+    lin("S", T.cs0[:, 0:128], T.bm[:], T.wf[:], 0.0, ["bm", "wf"], ["wm"], 128)
+    lin("S", T.k5[:], T.c2[:], T.r1[:], 0.0, ["c2", "r1"], ["k5"], 128)
+    lin("S", T.cv[:], T.c2[:], T.r2[:], 0.0, ["c2", "r2"], ["cv"], 128)
+    ms(T.cs0[:, 128:384], 0.0, [("wx", 0), ("wx", 1)], 128)
+    for e, c in enumerate(("even", "odd")):
+        own_, other = slice(16 * e, 128, 32), slice(16 - 16 * e, 128, 32)
+        tt(T.t1[:, other], T.t1[:, other], T.bm[:, own_], A.add, ["t1", "bm"], ["t1"])
+        ts(T.k5[:, other], T.bm[:, own_], T.xk[:], None, A.mult, None, ["k5", "bm", "xk"], ["k5"])
+        ts(T.cs0[:, 144 + 112 * e:256 + 128 * e:32], T.bm[:, own_], T.wf[:], 2.0, A.mult, A.mult, ["bm", "wf"], [("wx", e)])
         lin("S", T["ih%d" % e][:], T.idb[:], T[c][:], 0.0, ["idb", c], [("ih", e)], 128)
-        ts(T.cs0[:, 128 * e + 128:128 * e + 256], T.xc[:], T[w][:], 2.0, A.mult, A.mult, ["xc", w], [("wx", e)])
-        ts(T["km%d" % e][:], T.k5[:], T[c][:], None, A.mult, None, ["k5", c], [("km", e)])
-    lin("S", T.cq[:], T.bm[:], T.rq[:], 0.0, ["bm", "rq"], ["cq"], 128)
-    lin("S", T.k2[:], T.ci[:], -0.0625, 1.0, ["ci"], ["k2"], 128)
-    lin("S", T.k4[:], T.bm[:], T.r3[:], 0.0, ["bm", "r3"], ["k4"], 128)
-    tt(T.cv[:], T.k2[:], T.k4[:], A.mult, ["k2", "k4"], ["cv"], 256)
+    for e, c in enumerate(("even", "odd")):
+        ts(T["sm%d" % e][:], T.t1[:], T[c][:], 2048.0, A.mult, A.mult, ["t1", c], [("sm", e)])
+        lin("S", T["km%d" % e][:], T.k5[:], T[c][:], 0.0, ["k5", c], [("km", e)], 128)
     for n in (16, 32, 64):
-        cp(T.eb[:, n:2 * n], T.eb[:, 0:n], ["eb"], ["eb"])
-    tt(T.cs0[:, 384:512], T.eb[:], T.bm[:], A.mult, ["eb", "bm"], ["em2"], 256)
-    cp(T.cl0[:, 1024:1025], T.cl0[:, 0:1], ["cl"], ["clx"])
-    cp(T.cl0[:, 1025:1026], T.thf[:], ["cl", "thf"], ["clt"])
-    act(T.em0[:, 2048:2049], T.em0[:, 0:1], F.Copy, ["em"], ["emx"], 64)
-    act(T.key0[:, 2048:2049], T.key0[:, 0:1], F.Copy, ["key"], ["keyx"], 64)
+        lin("S", T.eb[:, n:2 * n], T.eb[:, 0:n], 1.0, 0.0, ["eb"], ["eb"])
+    inside(T.cs0[:, 384:512], "e1", T.eb[:], ["eb"], ["em2"])
+    cp(T.cl0[:, 1024:1031], T.cl0[:, 0:7], ["cl"], ["clx"])
+    cp(T.cl0[:, 1031:1032], T.thf[:], ["cl", "thf"], ["clt"])
+    act(T.em0[:, 2048:2064], T.em0[:, 0:16], F.Copy, ["em"], ["emx"], 64)
+    act(T.key0[:, 2048:2064], T.key0[:, 0:16], F.Copy, ["key"], ["keyx"], 64)
     own = {"cs": ["wm", ("wx", 0), ("wx", 1), "em2"], "key": ["key", "keyx"], "cl": ["cl", "clx", "clt"], "em": ["em", "emx"]}
 
     def tab(n, k):
         return own[n] if k == 0 else [(n, k)]
 
-    def send(to, kind, dst, src, sem, R, due=0.0):
-        rid, pid = topo.addr(T.cores[to % NR], core)
-        es = engines(rank, to, kind)
-        op("G", CFG["iss"], lambda: g.remote_dma(dst, src, T.sem[sem], T.sem.sent, pid, rid, sum(1 << e for e in es)), R + ["LG"],
-           ["LG", ("snd", sem)], sem="sent", val=len(es))
-        ops[-1]["due"], ops[-1]["bias"] = due, -2000 if due else 0
+    def send(ways, R, name, first=False):
+        def f():
+            return g.remote_dma_fused([
+                RemoteDMATransfer(dst_ids=[DstId(rid=topo.addr(c, core)[0], pnc=topo.addr(c, core)[1])],
+                                  dma_engine_mask=sum(1 << e for e in es), remote_sem=T.sem[sem], src=src, dst=dst)
+                for c, dst, src, sem, es in ways], local_sem=T.sem.sent)
+        op("G", CFG["iss"], f, R + ["LG"], ["LG", ("snd", name)], sem="sent", val=sum(len(w[4]) for w in ways),
+           bias=-2000 if first else 0)
 
-    def arrival(frm, kind, sem, R, W, lat=0):
-        op("N", 0, None, R, W, sem=sem, val=len(engines(frm, rank, kind)), lat=lat)
+    def pass_on(d, dst, src, sem, R, W):
+        send([(at(rank + d), dst, src, sem, topo.engines(core, at(rank + d)))], R, sem)
+        op("N", 0, None, [("snd", sem)], W, sem=sem, val=len(topo.engines(at(rank - d), core)))
 
-    def hand_on(k, early):
+    def hand_on(k, n):
         for r in range(rank - NR + 1, rank):
-            mine = (r + k - rank) % NR
             if (giver(k, r) - rank) % NR == 0:
-                for n, w in PIECES.items():
-                    if early == (mine == 0 and (k == 1 or k == 2 and n in CFG["ahead"])):
-                        send(r, "tab", T["%s%d" % (n, k)][:, 0:w], T["%s%d" % (n, mine)][:, 0:w], "a%s%d" % (n, k), tab(n, mine),
-                             CFG["due"] if early else 0.0)
+                mine = (r + k - rank) % NR
+                dst, src, sem, es = T["%s%d" % (n, k)], T["%s%d" % (n, mine)], "a%s%d" % (n, k), topo.engines(core, at(r))
+                if near(rank, r) or n not in SPLIT:
+                    send([(at(r), dst[:], src[:], sem, es)], tab(n, mine), sem, k == 1)
+                else:
+                    a, b = halves(n)
+                    rest = [e for e in topo.engines(core, helper(rank)) if e not in es]
+                    send([(at(r), dst[:, a], src[:, a], sem, es), (helper(rank), dst[:, b], src[:, b], "h%s%d" % (n, k), rest)],
+                         tab(n, mine), sem, k == 1)
 
     def store(dst, src, sem, R):
         op("Y", 80, lambda: Y.dma_start(dst, src), R, (), sem=sem, val=16, lat=2200)
 
+    def repeat(b, i):
+        w = 1024 // NX
+        for h in range(NX):
+            e = slice(w * h, w * h + w)
+            scan(T["xr%d" % b][:, e], T.m16[:, 0:w], T["xs%d" % i][:, e], A.add, [("xs", i), "m16"], [("xr", b, h)], w // 2)
+
     for k in range(1, NR):
         for i, n in enumerate(PIECES):
-            arrival(giver(k, rank), "tab", "a%s%d" % (n, k), [], [(n, k)], lat=CFG["tab"][k - 1] + CFG["piece"] * i)
-        lin("V", T["th%d" % k][:], T["cl%d" % k][:, 1025:1026], -1.0, 0.5, [("cl", k)], [("th", k)])
-    hand_on(2, True)
-    hand_on(1, True)
+            frm = giver(k, rank)
+            val = len(topo.engines(at(frm), core))
+            if n in SPLIT and not near(frm, rank):
+                val += len(topo.engines(helper(frm), core))
+            op("N", 0, None, [], [(n, k)], sem="a%s%d" % (n, k), val=val, lat=CFG["tab"][k - 1] + CFG["piece"] * i)
+        lin("V", T["th%d" % k][:], T["cl%d" % k][:, 1031:1032], -1.0, 0.5, [("cl", k)], [("th", k)])
+    for k in range(1, NR):
+        for n in PIECES:
+            hand_on(k, n)
 
+    wrap = False
     for t in range(NT):
-        k = max(t - 1, 0)
-        wrap = t > 0 and (rank + k) % NR == 0
+        k = (t - (t > MOVE)) % NR
+        came, wrap = wrap, (rank + k) % NR == NR - 1
         key, emt, clb, cs = [T["%s%d" % (n, k)] for n in ("key", "em", "cl", "cs")]
         for b in range(NB):
             seq[0] = j = t * NB + b
@@ -243,27 +278,27 @@ def rank_program(g, core, T, topo):
             pa, pb = T["pa%d" % b], T["pb%d" % b]
             D, Q, E, TK, SC = [pa[:, 64 * i:64 * i + 64] for i in range(5)]
             H, PA, VT = pb[:, 0:2, :], pb[:, 2:6, :], pb[:, 6:8, :]
-            xs, xr, df, ad, eg = [T["%s%d" % (n, b)] for n in ("xs", "xr", "df", "ad", "eg")]
+            xr, df, ad, eg = [T["%s%d" % (n, b)] for n in ("xr", "df", "ad", "eg")]
             bl, b4, b128 = slice(LB * b, LB * b + LB), slice(4 * b, 4 * b + 4), slice(128 * b, 128 * b + 128)
             kk, sg, cm, LU, SU, vt, sc, eq = [T[n][:, bl] for n in ("kk", "sg", "cm", "LU", "SU", "vt", "sc", "eq")]
-            at, am, cc = T.at[:, b128], T.am[:, b128], T.cc[:, b4]
+            pt, am, cc = T.at[:, b128], T.am[:, b128], T.cc[:, b4]
             SP, SX = T.SA[:, j, 0:64], T.SA[:, j, 64:128]
-            LP = T.P0[:, bl] if t == 0 else T.LA[:, b, 0:64] if t == 1 else T.SA[:, j - NB, 0:64]
+            landed = t == MOVE + 1
+            LP = T.P0[:, bl] if t == 0 else T.LA[:, b, 0:64] if landed else T.SA[:, j - NB, 0:64]
             oh = T.oh[:, LB * j:LB * j + LB]
             x = xr[:, 0::16]
-            kP, kx = ("LP", j) if t < 2 else ("SP", j - NB), ("xs", b)
-            lu = "LU" if t < 2 or wrap else "SU"
+            kP = ("LP", j) if t == 0 or landed else ("SP", j - NB)
+            lu = "LU" if t == 0 or landed or came else "SU"
             if t == 0:
                 cp(LU, T.plb[:, bl], ["plb"], [("LU", b)])
-                lin(ENG["xs"], xs[:, 0::16], T.qb[:, bl], 1.0, 0.0, ["qb"], [kx])
-                cp(LP, T.plb[:, bl], ["plb"], [kP])
+                lin(ENG["xs"], T.xs0[:, 0::16], T.qb[:, bl], 1.0, 0.0, ["qb"], [("xs", 0)])
+                lin("V", LP, T.plb[:, bl], 1.0, -2048.0, ["plb"], [kP])
             elif lu == "LU":
-                lin(ENG["lu"], LU, LP, 1.0, float(wrap), [kP], [("LU", b)])
-            if t == 1:
-                lin(ENG["xs"], xs[:, 0::16], T.LA[:, b, 64:128], 1.0, -XO, [kP], [kx])
-            for h in range(NX):
-                w = 1024 // NX
-                scan(xr[:, w * h:w * h + w], T.m16[:, 0:w], xs[:, w * h:w * h + w], A.add, [kx, "m16"], [("xr", b, h)], w // 2)
+                lin(ENG["lu"], LU, LP, 1.0, 2048.0, [kP], [("LU", b)])
+            if landed:
+                lin(ENG["xs"], T.xs0[:, 0::16], T.LA[:, b, 64:128], 1.0, -XO, [kP], [("xs", 0)])
+            if t == 0 or landed:
+                repeat(b, 0)
             XR = [("xr", b, h) for h in range(NX)]
             win = key[:, 0:2049] if t else key[:, 0:2048]
             for h in range(NK):
@@ -272,10 +307,10 @@ def rank_program(g, core, T, topo):
                 off = T[lu][:, LB * b + w // 16 * h:LB * b + w // 16 * (h + 1)]
                 tt(df[:, e], win.indirect(off), xr[:, e], A.subtract,
                    (tab("key", k) if t else ["key"]) + [(lu, b)] + XR[h * NX // NK:((h + 1) * NX - 1) // NK + 1], [("df", b, h)],
-                   60 + GAM * w)
+                   (60, w))
                 act(ad[:, e], df[:, e], F.Abs, [("df", b, h)], [("ad", b, h)], w)
             mm([(H, cs[:, 0:128], x, True, True)], XR + (tab("cs", k) if k else ["wm"]), [("H", b)], bB)
-            lin(ENG["kk"], kk, H, T.ksc[:], T.kb1[:] if wrap else T.kb0[:], [("H", b), "ksc", "kb0", "kb1"], [("kk", b)], banks=[bB])
+            lin(ENG["kk"], kk, H, T.ksc[:], T.kb0[:], [("H", b), "ksc", "kb0"], [("kk", b)], banks=[bB])
             for e in range(2):
                 o = PA[:, :, 16 * e:16 * e + 16]
                 mm([(o, T["ih%d" % e][:], LP, e == 0, False), (o, cs[:, 128 * e + 128:128 * e + 256], x, False, False),
@@ -287,29 +322,35 @@ def rank_program(g, core, T, topo):
             act(sg, D, F.Sign, [("D", b), ("th", k)], [("sg", b)], 64, [bA], T["th%d" % k][:])
             mm([(PA[:, :, 16 * e:16 * e + 16], T["sm%d" % e][:], sg, False, e == 1) for e in range(2)],
                [("sg", b), ("sm", 0), ("sm", 1)], [("PA", b)], bB)
-            mm([(Q, T.idh[:], LP, True, False), (Q, T.cq[:], kk, False, False), (Q, T.n2[:], sg, False, True)],
-               [kP, ("kk", b), ("sg", b), "idh", "cq", "n2"], [("Q", b)], bA)
-            turn(at, PA, [("PA", b)], [("at", b)], 128, [bB])
-            scan(am, T.m32[:], at, A.max, [("at", b), "m32"], [("am", b)], 128)
+            mm([(Q, T.idh[:], LP, True, False), (Q, T.n2[:], sg, False, True)], [kP, ("sg", b), "idh", "n2"], [("Q", b)], bA)
+            turn(pt, PA, [("PA", b)], [("at", b)], 128, [bB])
+            scan(am, T.m32[:], pt, A.max, [("at", b), "m32"], [("am", b)], 128)
             lin(ENG["cc"], cc, am[:, 31::32], 0.5, -0.25, [("am", b)], [("cc", b)])
             clw = clb[:, 0:1025] if t else clb[:, 0:1024]
-            tt(cm, clw.indirect(cc), sg, A.mult, [("cc", b), ("sg", b)] + (tab("cl", k) if t else ["cl"]), [("cm", b)], 60 + GAM * 64)
-            tt(SP, cm, Q, A.max, [("cm", b), ("Q", b)], [("SP", j)], banks=[bA])
-            lin(ENG["su"], SU, SP, 1.0, 0.0, [("SP", j)], [("SU", b)])
+            tt(cm, clw.indirect(cc), sg, A.mult, [("cc", b), ("sg", b)] + (tab("cl", k) if t else ["cl"]), [("cm", b)], (60, 64))
+            tt(SU, cm, Q, A.max, [("cm", b), ("Q", b)], [("SU", b)], banks=[bA])
+            if t < NT - 1:
+                lin(ENG["sp"], SP, SU, 1.0, wrap - 2048.0, [("SU", b)], [("SP", j)])
             mm([(VT, T.cv[:], kk, True, False)], [("kk", b), "cv"], [("VT", b)], bB)
             mm([(E, T.idb[:], x, True, False)], XR + ["idb"], [("E", b)], bA)
             emw = emt[:, 0:2049] if t else emt[:, 0:2048]
             for h in range(NE):
                 w = 1024 // NE
                 off = T.SU[:, LB * b + w // 16 * h:LB * b + w // 16 * (h + 1)]
-                act(eg[:, w * h:w * h + w], emw.indirect(off), F.Copy, [("SU", b)] + (tab("em", k) if t else ["em"]), [("eg", b, h)],
-                    78 + GAM * w)
+                R = [("SU", b)] + (tab("em", k) if t else ["em"])
+                if h % 2 and j >= NB * NT - CFG["both"]:
+                    cp(eg[:, w * h:w * h + w], emw.indirect(off), R, [("eg", b, h)], (60, w))
+                else:
+                    act(eg[:, w * h:w * h + w], emw.indirect(off), F.Copy, R, [("eg", b, h)], (78, w))
             if t == NT - 1:
-                lin("V", T.ip[:, bl], SP, 1.0, 1.0 if rank == 0 else 0.0, [("SP", j)], [("ip", b)])
+                lin("V", T.ip[:, bl], SU, 1.0, float(wrap), [("SU", b)], [("ip", b)])
                 ts(T.iq[:, bl], T.ip[:, bl], 2047, None, A.bitwise_and, None, [("ip", b)], [("iq", b)])
                 cp(T.SYP[:, bl], T.iq[:, bl], [("iq", b)], [("SYP", b)])
                 if b == NB - 1:
-                    store(T.yp[:], T.SYP[:], "op", [("SYP", i) for i in range(NB)])
+                    R = [("SYP", i) for i in range(NB)]
+                    if t == MOVE:
+                        pass_on(1, T.FYP[:], T.SYP[:], "ap", R, ["FYP"])
+                    store(T.yp[:], T["FYP" if t == MOVE else "SYP"][:], "op", ["FYP"] if t == MOVE else R)
             for h in range(NP):
                 mm([(VT, T.idb[:], eg[:, i::16], False, i == 15) for i in range(16 // NP * h, 16 // NP * (h + 1))],
                    [("eg", b, i) for i in range(NE)] + ["idb"], [("VT", b)], bB)
@@ -319,30 +360,30 @@ def rank_program(g, core, T, topo):
             tt(eq, vt, SC, A.is_equal, [("vt", b), ("SC", b)], [("eq", b)], banks=[bA])
             turn(oh, eq, [("eq", b)], [("oh", j)], 64)
             mm([(E, cs[:, 384:512], oh, False, True)], [("oh", j)] + (tab("cs", k) if k else ["em2"]), [("E", b)], bA)
-            if 0 < t < NT - 1:
-                lin(ENG["sx"], xs[:, 0::16], E, 0.5, -0.25, [("E", b)], [("SX", j), kx], banks=[bA])
+            if t != MOVE and t < NT - 1:
+                lin(ENG["sx"], T.xs1[:, 0::16], E, 0.5, -0.25, [("E", b)], [("SX", j), ("xs", 1)], banks=[bA])
+                seq[0] = j + NB
+                repeat(b, 1)
+                seq[0] = j
             else:
                 lin(ENG["sx"], SX, E, 0.5, XO - 0.25, [("E", b)], [("SX", j)], banks=[bA])
-            if t == 0:
-                send(rank + 1, "lanes", T.LA[:, b, :], T.SA[:, j, :], "ar%d" % b, [("SP", j), ("SX", j)])
-                arrival(rank - 1, "lanes", "ar%d" % b, [("snd", "ar%d" % b)], [("LP", j + NB)])
+            if t == MOVE < NT - 1:
+                pass_on(1, T.LA[:, b, :], T.SA[:, j, :], "ar%d" % b, [("SP", j), ("SX", j)], [("LP", j + NB)])
             if t == NT - 1:
                 lin(ENG["sx"], T.SYQ[:, bl], SX, 1.0, -XO, [("SX", j)], [("SYQ", b)])
                 if b >= NB - 2:
-                    c = slice(0, 192) if b == NB - 2 else bl
-                    store(T.yq[:, c], T.SYQ[:, c], "oq%d" % (b - NB + 2), [("SYQ", i) for i in range(b + 1)])
+                    c, i, R = slice(0, 192) if b == NB - 2 else bl, b - NB + 2, [("SYQ", i) for i in range(b + 1)]
+                    if t == MOVE:
+                        pass_on(1, T.FYQ[:, c], T.SYQ[:, c], "aq%d" % i, R, [("FYQ", i)])
+                    store(T.yq[:, c], T["FYQ" if t == MOVE else "SYQ"][:, c], "oq%d" % i, [("FYQ", i)] if t == MOVE else R)
             if b == NB - 1:
                 mm([(TK, T.wk[:, 3 - i:131 - i], T.oh[:, LB * (NB * t + i):LB * (NB * t + i + 1)], i == 0, i == NB - 1)
                     for i in range(NB)], [("oh", NB * t + i) for i in range(NB)] + ["wk"], ["TK"], bA)
                 c = slice(LB * t, LB * t + LB)
                 act(T.ytb[:, c], TK, F.Copy, ["TK"], [("yt", t)], 64, [bA])
                 if k:
-                    send(rank + k, "tok", T.ytl[:, c], T.ytb[:, c], "ay%d" % t, [("yt", t)])
-                    arrival(rank - k, "tok", "ay%d" % t, [("snd", "ay%d" % t)], [("yl", t)])
+                    pass_on(k, T.ytl[:, c], T.ytb[:, c], "ay%d" % t, [("yt", t)], [("yl", t)])
                 store(T.yt[:, 256 * t:256 * t + 256], T["ytl" if k else "ytb"][0:32, c], "oy%d" % t, [("yl" if k else "yt", t)])
-        if t == 0:
-            for i in range(2, NR):
-                hand_on(i, False)
 
     schedule(ops)
     emit_all(ops, {"V": V, "S": S, "P": P, "G": g, "Y": Y}, T, g)
@@ -351,11 +392,11 @@ def rank_program(g, core, T, topo):
 CNT_SEM = {"V": "cv", "S": "cs", "P": "ct", "G": "cg"}
 
 
-def place(ops, order, before, gap, first):
-    start, slots = [0.0] * len(ops), {q: [] for q in "VSPGY"}
+def place(ops, order):
+    slots = {q: [] for q in "VSPGY"}
     for i in order:
         o = ops[i]
-        st = max([start[d] + ops[d]["dur"] + gap(d, i) for d in before[i]] + [first[i]])
+        st = max([ops[d]["st"] + ops[d]["dur"] + (0.0 if d in o["O"] else ops[d]["after"]) for d in o["D"]] + [0.0])
         if o["q"] != "N":
             sl = slots[o["q"]]
             at, hi = 0, len(sl)
@@ -369,8 +410,7 @@ def place(ops, order, before, gap, first):
                 st = max(st, sl[at][1])
                 at += 1
             sl.insert(at, (st, st + o["dur"]))
-        start[i] = st
-    return start
+        o["st"], o["end"] = st, st + o["dur"] + o["after"]
 
 
 def schedule(ops):
@@ -397,34 +437,15 @@ def schedule(ops):
         if o["q"] == "P":
             order = {i for i in d if ops[i]["q"] == "P"}
         o["D"], o["O"] = d, order
-    n = len(ops)
-    pred, succ = [sorted(o["D"]) for o in ops], [[] for _ in range(n)]
-    for o in ops:
-        for d in o["D"]:
-            succ[d].append(o["i"])
         o["after"] = o["lat"] + (CFG["link"] if o["q"] == "N" else CFG["hop"])
-
-    def gap(d, i):
-        return 0.0 if d in ops[i]["O"] else ops[d]["after"]
-
-    def gap_back(d, i):
-        return gap(i, d)
-
-    key = [0.0] * n
+    key = [1e9] * len(ops)
     for o in reversed(ops):
         mine = CFG["per"] * o["seq"] + CFG["off"].get(o["kind"], 1e9) if o["kind"] else -o["bias"] if o["bias"] else 1e9
-        key[o["i"]] = min([mine] + [key[s] - o["dur"] for s in succ[o["i"]]])
-    best, last = None, [o.get("due", 0.0) if succ[o["i"]] else o["lat"] for o in ops]
-    for turn in range(CFG["rounds"]):
-        start = place(ops, sorted(range(n), key=lambda i: (key[i], i)), pred, gap, [0.0] * n)
-        ends = [start[i] + ops[i]["dur"] + last[i] for i in range(n)]
-        if best is None or max(ends) < best[0]:
-            best = (max(ends), start)
-        back = place(ops, sorted(range(n), key=lambda i: (-ends[i], -i)), succ, gap_back, last)
-        key = [-(back[i] + ops[i]["dur"]) for i in range(n)]
-    for i, o in enumerate(ops):
-        o["st"], o["end"] = best[1][i], best[1][i] + o["dur"] + o["after"]
-    return best[0]
+        key[o["i"]] = min(key[o["i"]], mine)
+        for d in o["D"]:
+            key[d] = min(key[d], key[o["i"]] - ops[d]["dur"])
+    place(ops, sorted(range(len(ops)), key=lambda i: (key[i], i)))
+    return max(o["st"] + o["dur"] + o["lat"] for o in ops)
 
 
 def emit_all(ops, queues, T, g):

@@ -1,44 +1,54 @@
-from concourse.mybir import AluOpType, ActivationFunctionType
+import math
+from concourse.mybir import AluOpType, ActivationFunctionType, AxisListType
 from concourse.bass import DstId, RemoteDMATransfer
 
 NR, NB, LB, NT = 4, 4, 64, 5
 XO = 1536.0
-CFG = {"nk": 2, "ne": 2, "nx": 2, "np": 4,
-       "f": 1.2, "gam": 1.56, "hop": 180, "link": 2600, "iss": 700, "per": 3302, "move": 4,
-       "off": {'xr0': 10160, 'xr1': 2570, 'df0': 2390, 'ad0': 13410, 'df1': 2560, 'ad1': 11570, 'H0': 9030, 'kk0': 3080, 'PA0': 8440,
-               'PA1': 10740, 'D0': 1880, 'D1': 10550, 'D2': 9990, 'D3': 4110, 'sg0': 1960, 'PA2': 6740, 'Q0': 14120, 'at0': 2380,
-               'am0': 4470, 'cc0': 3630, 'cm0': 19850, 'SP0': 13020, 'SU0': 8800, 'VT0': 25030, 'E0': 13010, 'eg0': 8500,
-               'eg1': 5180, 'VT1': 7100, 'VT2': 9530, 'VT3': 32110, 'VT4': 21720, 'vt0': 8610, 'sc0': 7640, 'SC0': 28400,
-               'eq0': 13800, 'oh0': 20490, 'E1': 20150, 'SX0': 10640, 'SYP0': 9500},
-       "tab": [14000, 28000, 42000], "piece": 2000, "due": 70000, "ahead": ["key", "cs", "cl", "em"],
-       "eng": {"lu": "V", "xs": "S", "kk": "S", "cc": "V", "sp": "S", "sx": "S"}, "both": 2}
+CFG = {
+    "cut": 640,
+    "votes": 576,
+    "gx": 5,
+    "both": 2,
+    "round": {
+        "V": [("SU0", 2), ("vt0", 3), ("eg1", 2), ("xr0", 0), ("sc0", 3), ("xr1", 0), ("df0", 0), ("SC0", 3), ("df1", 0), ("eq0", 3),
+              ("at0", 1), ("oh0", 3), ("cc0", 1), ("cm0", 1)],
+        "S": [("sg0", 1), ("kk0", 0), ("eg1", 2), ("ad0", 0), ("SP0", 2), ("ad1", 0), ("SX0", 3), ("eg0", 1)],
+        "P": [("D0", 1), ("D1", 1), ("D2", 1), ("D3", 1), ("H0", 0), ("E0", 2), ("PA2", 1), ("PA0", 0), ("Q0", 1), ("PA1", 0),
+              ("VT0", 2), ("VT1", 2), ("VT2", 2), ("E1", 3), ("VT3", 2)]},
+    "own": [("lay", "cs"), ("on", "key"), ("on", "cs"), ("on", "cu"), ("on", "em"), ("lay", "eb")],
+    "other": [("on", "key"), ("on", "cs"), ("lay", "cs"), ("on", "cu"), ("lay", "cu"), ("on", "em"), ("lay", "eb")],
+    "f": 1.15, "gam": 1.56, "hop": 200, "link": 2600, "iss": 700, "first": 2000, "tab": [29000, 43000], "piece": 1500,
+    "way": {"key": 8500, "cs": 3500, "cu": 9500, "em": 10500},
+    "cases": [(1.0, 1.56, 200, 1.0), (1.3, 1.4, 140, 1.3), (1.4, 1.9, 200, 1.1), (1.1, 1.3, 180, 1.6)],
+    "ends": [0.4, 0.78], "tries": 9000, "heat": 40, "soon": 0.85}
 
 SCRATCH = {
     "plb": ("sbuf", [128, 256], "int32"), "qb": ("sbuf", [128, 256], "bfloat16"),
-    "wb": ("sbuf", [128, 1], "bfloat16"), "thf": ("sbuf", [128, 1], "float32"), "eb": ("sbuf", [128, 128], "bfloat16"),
+    "wb": ("sbuf", [128, 1], "bfloat16"), "thf": ("sbuf", [128, 1], "float32"),
     "LU": ("sbuf", [128, 256], "uint16"), "SU": ("sbuf", [128, 256], "uint16"),
-    "LA": ("sbuf", [128, 4, 128], "float16"), "P0": ("sbuf", [128, 256], "float16"), "SA": ("sbuf", [128, 20, 128], "float16"),
+    "SP": ("sbuf", [128, 1280], "float16"), "SX": ("sbuf", [128, 256], "float16"),
     "SYP": ("sbuf", [128, 256], "float32"), "SYQ": ("sbuf", [128, 256], "bfloat16"),
     "FYP": ("sbuf", [128, 256], "float32"), "FYQ": ("sbuf", [128, 256], "bfloat16"),
     "ip": ("sbuf", [128, 256], "int32"), "iq": ("sbuf", [128, 256], "int32"),
     "xs0": ("sbuf", [128, 1024], "uint16"), "xs1": ("sbuf", [128, 1024], "uint16"),
-    "m16": ("sbuf", [128, 1024], "bfloat16"), "m32": ("sbuf", [128, 128], "bfloat16"),
+    "m16": ("sbuf", [128, 640], "bfloat16"), "up": ("sbuf", [128, 64], "bfloat16"), "dn": ("sbuf", [128, 64], "bfloat16"),
     "wd": ("sbuf", [128, 144], "bfloat16"), "wk": ("sbuf", [128, 132], "bfloat16"),
     "ii": ("sbuf", [128, 1], "int32"), "ik": ("sbuf", [128, 1], "int32"), "i16": ("sbuf", [128, 1], "int32"),
     "oh": ("sbuf", [128, 1280], "bfloat16"), "ytb": ("sbuf", [128, 320], "float32"), "ytl": ("sbuf", [128, 320], "float32"),
 }
 for _k in range(NR):
     SCRATCH.update({"key%d" % _k: ("sbuf", [128, 2064], "bfloat16"), "em%d" % _k: ("sbuf", [128, 2064], "bfloat16"),
-                    "cl%d" % _k: ("sbuf", [128, 1032], "int32"), "cs%d" % _k: ("sbuf", [128, 512], "bfloat16"),
-                    "th%d" % _k: ("sbuf", [128, 1], "float32")})
-for _n in ("ob", "bm0", "bm", "idb", "ub", "ci", "c1", "c2", "t1", "e1", "sm0", "sm1", "n2"):
+                    "cl%d" % _k: ("sbuf", [128, 1032], "int32"), "cu%d" % _k: ("sbuf", [128, 1032], "uint16"),
+                    "cs%d" % _k: ("sbuf", [128, 32], "bfloat16"), "eb%d" % _k: ("sbuf", [128, 128], "bfloat16"),
+                    "wx%d" % _k: ("sbuf", [128, 256], "bfloat16"), "th%d" % _k: ("sbuf", [128, 1], "float32")})
+for _n in ("ob", "bm0", "bm", "idb", "ub", "ci", "p2", "n2", "e0", "e1", "sm0", "sm1"):
     SCRATCH[_n] = ("sbuf", [128, 128], "bfloat16")
-for _n in ("idh", "ih0", "ih1", "k5", "km0", "km1", "cv"):
+for _n in ("idh", "ih0", "ih1", "k1", "km0", "km1"):
     SCRATCH[_n] = ("sbuf", [128, 128], "float16")
-for _n in ("kc", "odd", "even", "r0", "r1", "r2", "ksc", "kb", "kb0", "xk", "xk1", "wf"):
+for _n in ("kc", "odd", "even", "ksc", "ka", "kb", "kb0", "r8", "m9", "hc", "wf"):
     SCRATCH[_n] = ("sbuf", [128, 1], "float32")
-for _n, _s, _d in (("kk", [128, 256], "float16"), ("sg", [128, 256], "bfloat16"), ("at", [128, 512], "float32"),
-                   ("am", [128, 512], "float32"), ("cc", [128, 16], "uint16"), ("cm", [128, 256], "float16"),
+for _n, _s, _d in (("kk", [128, 256], "float16"), ("sg", [128, 256], "bfloat16"),
+                   ("at", [128, 512], "float32"), ("cc", [128, 16], "uint16"), ("cm", [128, 256], "float16"),
                    ("vt", [128, 256], "float32"), ("sc", [128, 256], "float32"), ("eq", [128, 256], "bfloat16")):
     SCRATCH[_n] = ("sbuf", _s, _d)
 for _b in range(NB):
@@ -47,13 +57,12 @@ for _b in range(NB):
         "ad%d" % _b: ("sbuf", [128, 1024], "bfloat16"), "eg%d" % _b: ("sbuf", [128, 1024], "bfloat16"),
         "pa%d" % _b: ("psum", [128, 512], "float32"), "pb%d" % _b: ("psum", [128, 16, 32], "float32"),
     })
-PIECES = {"key": 2064, "cl": 1032, "cs": 512, "em": 2064}
-SPLIT = ["key", "cl", "em"]
-LOADS = ["pl", "q", "key", "w", "th", "cl", "emb", "em"]
+PIECES = {"key": 2064, "cs": 32, "cu": 1032, "em": 2064}
+STRAIGHT = {("key", 1): 1, ("cu", 1): 0, ("cs", 1): 1, ("cs", 2): 1}
+LOADS = ["pl0", "q", "key", "pl1", "w", "th", "cl", "emb", "em"]
 SEMAPHORES = (["cv", "cs", "ct", "cg", "sent"] + ["ld_" + n for n in LOADS]
-              + ["ar%d" % b for b in range(NB)] + ["a%s%d" % (n, k) for n in PIECES for k in range(1, NR)]
-              + ["h%s%d" % (n, k) for n in SPLIT for k in range(1, NR)]
-              + ["op", "oq0", "oq1", "ap", "aq0", "aq1"] + ["oy%d" % t for t in range(NT)] + ["ay%d" % t for t in range(NT)])
+              + ["%s%s%d" % (a, n, k) for a in "ah" for n in PIECES for k in range(1, NR)]
+              + ["op", "oq0", "oq1", "ap", "aq0", "aq1"] + ["oy%d" % t for t in range(NT)] + ["ay%d" % t for t in range(1, NR)])
 
 
 def rank_program(g, core, T, topo):
@@ -72,44 +81,45 @@ def rank_program(g, core, T, topo):
     def giver(k, r):
         return r + k if near(r, r + k) else r + 1
 
-    def halves(n):
-        return slice(0, PIECES[n] // 2), slice(PIECES[n] // 2, PIECES[n])
+    def parts(n, k):
+        cut = int(PIECES[n] * STRAIGHT.get((n, k), 0.5))
+        return slice(0, cut), slice(cut, PIECES[n])
+
+    def some(c):
+        return c.stop > c.start
 
     if rank is None:
         for r in range(NR):
             if not near(r, r - 1) and core == helper(r):
                 rid, pid = topo.addr(at(r - 1), core)
                 came = len(topo.engines(at(r), core)) - len(topo.engines(at(r), at(r - 1)))
-                far = [(k, n) for k in range(1, NR) for n in SPLIT if not near(r - 1, r - 1 + k)]
+                far = [(k, n) for k in range(1, NR) for n in PIECES if not near(r - 1, r - 1 + k) and some(parts(n, k)[1])]
                 for k, n in far:
-                    part = T["%s%d" % (n, k)][:, halves(n)[1]]
+                    part = T["%s%d" % (n, k)][:, parts(n, k)[1]]
                     g.wait_ge(T.sem["h%s%d" % (n, k)], came)
                     g.remote_dma(part, part, T.sem["a%s%d" % (n, k)], T.sem.sent, pid, rid, topo.mask(core, at(r - 1)))
                 g.wait_ge(T.sem.sent, len(far) * len(topo.engines(core, at(r - 1))))
         return
     A, F = AluOpType, ActivationFunctionType
     V, S, P, Y = g.vector, g.scalar, g.tensor, g.sync
-    ops, seq, seen = [], [None], {}
-    NK, NE, NX, NP, ENG, GAM, MOVE = CFG["nk"], CFG["ne"], CFG["nx"], CFG["np"], CFG["eng"], CFG["gam"], CFG["move"]
+    ops, seq, seen, CUT = [], [None], {}, CFG["cut"]
 
     def op(q, dur, emit, R=(), W=(), banks=(), sem=None, val=1, lat=0, bias=0):
         kind = None
-        if seq[0] is not None and q in "VSP" and not isinstance(W[0], str):
+        if seq[0] is not None and q in "VSPG" and not isinstance(W[0], str):
             seen[seq[0], W[0][0]] = seen.get((seq[0], W[0][0]), 0) + 1
             kind = "%s%d" % (W[0][0], seen[seq[0], W[0][0]] - 1)
         cyc, gat = dur if isinstance(dur, tuple) else (dur, 0)
-        ops.append({"q": q, "cyc": cyc, "gat": gat, "dur": (cyc + GAM * gat) * (0.83 * CFG["f"] if q in "VSP" else 1), "emit": emit,
-                    "R": list(R), "W": list(W), "banks": list(banks), "sem": sem, "val": val, "lat": lat, "i": len(ops),
-                    "bias": bias, "seq": seq[0], "kind": kind})
+        ops.append({"q": q, "cyc": cyc, "gat": gat, "dur": (cyc + CFG["gam"] * gat) * (0.83 * CFG["f"] if q in "VSP" else 1),
+                    "emit": emit, "R": list(R), "W": list(W), "banks": list(banks), "sem": sem, "val": val, "lat": lat,
+                    "i": len(ops), "bias": bias, "seq": seq[0], "kind": kind})
 
-    def load(q, name, fn, W, done):
-        op(q, 80, fn, ["L" + q], W + ["L" + q], sem="ld_" + name, val=16, lat=done, bias=1e7)
+    def load(q, name, out, src, done):
+        op(q, 80, lambda: (S if q == "S" else Y).dma_start(out, src), ["L" + q], [name, "L" + q], sem="ld_" + name, val=16, lat=done,
+           bias=1e7)
 
-    def ts(out, i, s1, s2, a, b, R, W, n=64, banks=()):
-        if b is None:
-            op("V", n, lambda: V.tensor_scalar(out, i, s1, None, a), R, W, banks)
-        else:
-            op("V", n, lambda: V.tensor_scalar(out, i, s1, s2, a, b), R, W, banks)
+    def ts(out, i, s1, a, R, W, n=64):
+        op("V", n, lambda: V.tensor_scalar(out, i, s1, None, a), R, W)
 
     def tt(out, a, b, o, R, W, n=64, banks=()):
         op("V", n, lambda: V.tensor_tensor(out, a, b, o), R, W, banks)
@@ -122,12 +132,12 @@ def rank_program(g, core, T, topo):
 
     def lin(q, out, i, mul, add, R, W, n=64, banks=()):
         if q == "V":
-            ts(out, i, mul, add, A.mult, A.add, R, W, n, banks)
+            op("V", n, lambda: V.tensor_scalar(out, i, mul, add, A.mult, A.add), R, W, banks)
         else:
             op("S", n, lambda: S.activation(out, i, F.Identity, bias=add, scale=mul), R, W, banks)
 
-    def scan(out, d0, d1, o, R, W, n, banks=()):
-        op("V", n, lambda: V.tensor_tensor_scan(out, d0, d1, 0.0, A.mult, o), R, W, banks)
+    def scan(out, d0, d1, o0, o1, R, W, n, banks=()):
+        op("V", n, lambda: V.tensor_tensor_scan(out, d0, d1, 0.0, o0, o1), R, W, banks)
 
     def turn(out, i, R, W, n, banks=()):
         op("V", n, lambda: V.transpose(out, i), R, W, banks)
@@ -135,90 +145,95 @@ def rank_program(g, core, T, topo):
     def act(out, i, f, R, W, n, banks=(), bias=0.0):
         op("S", n, lambda: S.activation(out, i, f, bias=bias), R, W, banks)
 
-    def mm(ms_, R, W, bank):
+    def unit(q, n, calls, R, W, banks=()):
         def f():
             last = None
-            for m in ms_:
-                last = P.matmul(*m)
+            for c in calls:
+                last = c()
             return last
-        op("P", 64 * len(ms_), f, R, W, [bank])
+        op(q, n, f, R, W, banks)
 
-    def aff(out, src, pat, cmp, base, cm, fill=0.0, R=(), W=()):
-        op("G", 460, lambda: g.affine_select(out, src, pat, cmp, fill, base, cm), R, W)
+    def mm(ms_, R, W, bank):
+        unit("P", 64 * len(ms_), [lambda m=m: P.matmul(*m) for m in ms_], R, W, [bank])
+
+    def aff(out, src, pat, cmp, base, cm, R, W, n=128):
+        op("G", 205 + 2 * n, lambda: g.affine_select(out, src, pat, cmp, 0.0, base, cm), R, W)
+
+    def gcp(out, src, n, R, W):
+        aff(out, src, [[0, n]], A.is_ge, 0, 0, R, W, n)
 
     def inside(out, tmp, src, R, W):
-        aff(T[tmp][:], src, [[-16, 8], [0, 16]], A.is_ge, 0, 1, R=R, W=[tmp])
-        aff(out, T[tmp][:], [[16, 8], [0, 16]], A.is_ge, 15, -1, R=[tmp], W=W)
+        aff(T[tmp][:], src, [[-16, 8], [0, 16]], A.is_ge, 0, 1, R, [tmp])
+        aff(out, T[tmp][:], [[16, 8], [0, 16]], A.is_ge, 15, -1, [tmp] + [r for r in R if r == "LG"], W)
 
-    load("S", "q", lambda: S.dma_start(T.qb[:], T.q[:]), ["qb"], 2000)
-    load("Y", "pl", lambda: Y.dma_start(T.plb[:], T.pl[:]), ["plb"], 2300)
-    load("Y", "key", lambda: Y.dma_start(T.key0[:, 0:2048], T.key[:]), ["key"], 4600)
-    load("S", "w", lambda: S.dma_start(T.wb[:], T.w[:]), ["wb"], 4700)
-    load("S", "th", lambda: S.dma_start(T.thf[:], T.th[:]), ["thf"], 4800)
-    load("S", "emb", lambda: S.dma_start(T.eb[:, 0:16], T.emb[:]), ["eb"], 4900)
-    load("Y", "cl", lambda: Y.dma_start(T.cl0[:, 0:1024], T.cl[:]), ["cl"], 6900)
-    load("Y", "em", lambda: Y.dma_start(T.em0[:, 0:2048], T.em[:]), ["em"], 9000)
+    load("S", "q", T.qb[:], T.q[:], 1200)
+    load("Y", "pl0", T.plb[:, 0:LB], T.pl[:, 0:LB], 1300)
+    load("Y", "key", T.key0[:, 0:2048], T.key[:], 2600)
+    load("S", "w", T.wb[:], T.w[:], 1600)
+    load("Y", "pl1", T.plb[:, LB:], T.pl[:, LB:], 3000)
+    load("S", "th", T.thf[:], T.th[:], 3100)
+    load("S", "emb", T.cs0[:, 16:32], T.emb[:], 3200)
+    load("Y", "cl", T.cl0[:, 0:1024], T.cl[:], 4400)
+    load("Y", "em", T.em0[:, 0:2048], T.em[:], 5700)
 
     ms(T.ob[:], 1.0, ["ob"])
     op("G", 140, lambda: g.iota(T.ii[:], [[0, 1]], 0, 1), (), ["ii"])
     inside(T.bm[:], "bm0", T.ob[:], ["ob"], ["bm"])
-    aff(T.idb[:], T.ob[:], [[-1, 128]], A.is_equal, 0, 1, R=["ob"], W=["idb"])
-    aff(T.ub[:], T.bm[:], [[1, 128]], A.is_ge, -1, -1, R=["bm"], W=["ub"])
-    aff(T.t1[:], T.ub[:], [[1, 128]], A.not_equal, 0, -1, -1.0, ["ub"], ["t1"])
+    aff(T.idb[:], T.ob[:], [[-1, 128]], A.is_equal, 0, 1, ["ob"], ["idb"])
+    aff(T.ub[:], T.bm[:], [[1, 128]], A.is_ge, -1, -1, ["bm"], ["ub"])
     op("G", 400, lambda: g.iota(T.ci[:], [[0, 8], [-1, 16]], 0, 0, allow_small_or_imprecise_dtypes=True), (), ["ci"])
-    inside(T.c2[:], "c1", T.ci[:], ["ci"], ["c2"])
     ms(T.xs0[:], 0, [("xs", 0)], 512)
-    ms(T.m16[:, 0:512], 1.0, ["m16"], 256)
-    ms(T.m16[:, 0:512:16], 0.0, ["m16"])
+    ms(T.m16[:], 1.0, ["m16"], 320)
+    ms(T.m16[:, 0::16], 0.0, ["m16"])
     for h in range(2):
         lin("S", T.xs1[:, 512 * h:512 * h + 512], T.m16[:, 0:512], 0.0, 0.0, ["m16"], [("xs", 1)], 512)
-    ms(T.m32[:], 1.0, ["m32"])
-    ms(T.m32[:, 0::32], 0.0, ["m32"])
-    ts(T.ik[:], T.ii[:], 15, None, A.bitwise_and, None, ["ii"], ["ik"])
-    ts(T.i16[:], T.ii[:], 16, None, A.bitwise_and, None, ["ii"], ["i16"])
+    for n, c in (("up", 1 / 32), ("dn", -1 / 32)):
+        lin("S", T[n][:], T.m16[:, 0:64], 8192.0 + c, -8192.0, ["m16", "cl"], [n])
+    ts(T.ik[:], T.ii[:], 15, A.bitwise_and, ["ii"], ["ik"])
+    ts(T.i16[:], T.ii[:], 16, A.bitwise_and, ["ii"], ["i16"])
     cp(T.kc[:], T.ik[:], ["ik"], ["kc"])
-    ts(T.odd[:], T.i16[:], 0.0625, None, A.mult, None, ["i16"], ["odd"])
-    lin("S", T.even[:], T.odd[:], -1.0, 1.0, ["odd"], ["even"])
-    for j in range(3):
-        ts(T["r%d" % j][:], T.kc[:], float(j), None, A.is_equal, None, ["kc"], ["r%d" % j])
-    lin("S", T.th0[:], T.thf[:], -1.0, 0.5, ["thf"], [("th", 0)])
-    lin("S", T.wf[:], T.wb[:], 1.0, 0.0, ["wb"], ["wf"])
+    ts(T.odd[:], T.i16[:], 0.03125, A.mult, ["i16"], ["odd"])
+    lin("S", T.even[:], T.odd[:], -1.0, 0.5, ["odd"], ["even"])
+    lin("S", T.th0[:], T.thf[:], -1.0, 0.5, ["th"], [("th", 0)])
+    lin("S", T.wf[:], T.wb[:], 1.0, 0.0, ["w"], ["wf"])
     ms(T.wd[:], 0.0, ["wd"], 72)
     cp(T.wd[:, 15:128:16], T.bm[:, 0::16], ["bm"], ["wd"])
     ms(T.wk[:], 0.0, ["wk"], 66)
     lin("S", T.wk[:, 3:35:4], T.bm[:, 0::16], T.kc[:], 0.0, ["bm", "kc"], ["wk"])
-    lin("S", T.ksc[:], T.r0[:], 2.0 ** -10, 0.0, ["r0"], ["ksc"])
-    lin("S", T.kb[:], T.r2[:], 2.0 ** -15, T.r1[:], ["r1", "r2"], ["kb"])
-    lin("S", T.xk[:], T.r0[:], (1025.0 - 511.5 / 1024) / 2048, T.kb[:], ["r0", "kb"], ["xk"])
-    lin("S", T.kb0[:], T.xk[:], 2048.0, 0.0, ["xk"], ["kb0"])
-    lin("S", T.xk1[:], T.r1[:], 1009.0, 0.0, ["r1"], ["xk1"])
-    lin("S", T.xk[:], T.r0[:], -2048.0, T.xk1[:], ["r0", "xk1"], ["xk"])
+    lin("S", T.ksc[:], T.ub[:, 8:9], 2.0 ** -10, 0.0, ["ub"], ["ksc"])
+    lin("S", T.r8[:], T.idb[:, 8:9], 0.5, 0.0, ["idb"], ["r8"])
+    lin("S", T.m9[:], T.idb[:, 9:10], -4.0, 0.0, ["idb"], ["m9"])
+    lin("S", T.ka[:], T.idb[:, 9:10], 0.0625, 0.0, ["idb"], ["ka"])
+    lin("S", T.kb[:], T.idb[:, 8:9], 2048.0, T.ka[:], ["idb", "ka"], ["kb"])
+    lin("S", T.kb0[:], T.ub[:, 8:9], 1025.0 - 511.5 / 1024, T.kb[:], ["ub", "kb"], ["kb0"])
+    lin("S", T.hc[:], T.idb[:, 8:9], 504.5, T.m9[:], ["idb", "m9"], ["hc"])
     lin("S", T.idh[:], T.idb[:], 1.0, 0.0, ["idb"], ["idh"], 128)
     lin("S", T.n2[:], T.idb[:], -2048.0, 0.0, ["idb"], ["n2"], 128)
-    lin("S", T.cs0[:, 0:128], T.bm[:], T.wf[:], 0.0, ["bm", "wf"], ["wm"], 128)
-    lin("S", T.k5[:], T.c2[:], T.r1[:], 0.0, ["c2", "r1"], ["k5"], 128)
-    lin("S", T.cv[:], T.c2[:], T.r2[:], 0.0, ["c2", "r2"], ["cv"], 128)
-    ms(T.cs0[:, 128:384], 0.0, [("wx", 0), ("wx", 1)], 128)
+    lin("V", T.p2[:], T.idb[:], 2048.0, 0.0, ["idb"], ["p2"])
+    ms(T.cs0[:, 8:16], 0.0, ["wm0"])
+    lin("S", T.cs0[:, 0:8], T.bm[:, 0::16], T.wf[:], 0.0, ["bm", "wf"], ["wm"])
+    lin("S", T.k1[0:16, :], T.ci[0:16, :], T.r8[0:16, :], T.m9[0:16, :], ["ci", "r8", "m9"], ["k1"], 128)
+    sm = T.pa0[:, 320:448]
+    mm([(sm, T.p2[:], T.ub[:], True, False), (sm, T.n2[:], T.idb[:], False, False),
+        (sm[:, 16::32], T.p2[:], T.bm[:, 0::32], False, False), (sm[:, 0::32], T.p2[:], T.bm[:, 16::32], False, True)],
+       ["p2", "ub", "n2", "idb", "bm"], ["sm"], "a0")
     for e, c in enumerate(("even", "odd")):
-        own_, other = slice(16 * e, 128, 32), slice(16 - 16 * e, 128, 32)
-        tt(T.t1[:, other], T.t1[:, other], T.bm[:, own_], A.add, ["t1", "bm"], ["t1"])
-        ts(T.k5[:, other], T.bm[:, own_], T.xk[:], None, A.mult, None, ["k5", "bm", "xk"], ["k5"])
-        ts(T.cs0[:, 144 + 112 * e:256 + 128 * e:32], T.bm[:, own_], T.wf[:], 2.0, A.mult, A.mult, ["bm", "wf"], [("wx", e)])
+        km = T["km%d" % e]
+        aff(km[0:16, :], T.k1[0:16, :], [[0, 4], [1, 2], [0, 16]], A.is_equal, -e, 0, ["k1"], [("km", e)])
+        lin("S", km[0:16, 16 - 16 * e::32], T.idb[0:16, e:8:2], -1024.0, T.hc[0:16, :], ["idb", "hc", ("km", e)], [("km", e)])
         lin("S", T["ih%d" % e][:], T.idb[:], T[c][:], 0.0, ["idb", c], [("ih", e)], 128)
-    for e, c in enumerate(("even", "odd")):
-        ts(T["sm%d" % e][:], T.t1[:], T[c][:], 2048.0, A.mult, A.mult, ["t1", c], [("sm", e)])
-        lin("S", T["km%d" % e][:], T.k5[:], T[c][:], 0.0, ["k5", c], [("km", e)], 128)
-    for n in (16, 32, 64):
-        lin("S", T.eb[:, n:2 * n], T.eb[:, 0:n], 1.0, 0.0, ["eb"], ["eb"])
-    inside(T.cs0[:, 384:512], "e1", T.eb[:], ["eb"], ["em2"])
-    cp(T.cl0[:, 1024:1031], T.cl0[:, 0:7], ["cl"], ["clx"])
-    cp(T.cl0[:, 1031:1032], T.thf[:], ["cl", "thf"], ["clt"])
-    act(T.em0[:, 2048:2064], T.em0[:, 0:16], F.Copy, ["em"], ["emx"], 64)
-    act(T.key0[:, 2048:2064], T.key0[:, 0:16], F.Copy, ["key"], ["keyx"], 64)
-    own = {"cs": ["wm", ("wx", 0), ("wx", 1), "em2"], "key": ["key", "keyx"], "cl": ["cl", "clx", "clt"], "em": ["em", "emx"]}
+        lin("S", T["sm%d" % e][:], sm, T[c][:], 0.0, ["sm", c], [("sm", e)], 128, ["a0"])
+    ms(T.wx0[:], 0.0, [("wx", 0)], 128)
+    for k in range(1, NR):
+        op("G", 670, lambda k=k: g.iota(T["wx%d" % k][:], [[0, 256]], 0, 0, allow_small_or_imprecise_dtypes=True), (), [("wx", k)])
+    gcp(T.cl0[:, 1024:1025], T.cl0[:, 0:1], 1, ["cl"], ["clx"])
+    gcp(T.key0[:, 2048:2064], T.key0[:, 0:16], 16, ["key"], ["keyx"])
+    gcp(T.em0[:, 2048:2064], T.em0[:, 0:16], 16, ["em"], ["emx"])
+    own = {"cs": ["wm", "wm0", "emb"], "key": ["key", "keyx"], "cl": ["cl", "clx"], "em": ["em", "emx"],
+           "cu": ["cu%d" % i for i in range(4)]}
 
     def tab(n, k):
-        return own[n] if k == 0 else [(n, k)]
+        return own[n] if k == 0 else [(n, k, c) for c in range(0, 1032, 258)] if n == "cl" else [(n, k)]
 
     def send(ways, R, name, first=False):
         def f():
@@ -226,8 +241,8 @@ def rank_program(g, core, T, topo):
                 RemoteDMATransfer(dst_ids=[DstId(rid=topo.addr(c, core)[0], pnc=topo.addr(c, core)[1])],
                                   dma_engine_mask=sum(1 << e for e in es), remote_sem=T.sem[sem], src=src, dst=dst)
                 for c, dst, src, sem, es in ways], local_sem=T.sem.sent)
-        op("G", CFG["iss"], f, R + ["LG"], ["LG", ("snd", name)], sem="sent", val=sum(len(w[4]) for w in ways),
-           bias=-2000 if first else 0)
+        op("G", CFG["iss"] + CFG["first"] * (name == "akey1"), f, R + ["LG"], ["LG", ("snd", name)], sem="sent",
+           val=sum(len(w[4]) for w in ways), bias=-2000 if first else 0)
 
     def pass_on(d, dst, src, sem, R, W):
         send([(at(rank + d), dst, src, sem, topo.engines(core, at(rank + d)))], R, sem)
@@ -238,144 +253,159 @@ def rank_program(g, core, T, topo):
             if (giver(k, r) - rank) % NR == 0:
                 mine = (r + k - rank) % NR
                 dst, src, sem, es = T["%s%d" % (n, k)], T["%s%d" % (n, mine)], "a%s%d" % (n, k), topo.engines(core, at(r))
-                if near(rank, r) or n not in SPLIT:
+                if near(rank, r):
                     send([(at(r), dst[:], src[:], sem, es)], tab(n, mine), sem, k == 1)
                 else:
-                    a, b = halves(n)
+                    a, b = parts(n, k)
                     rest = [e for e in topo.engines(core, helper(rank)) if e not in es]
-                    send([(at(r), dst[:, a], src[:, a], sem, es), (helper(rank), dst[:, b], src[:, b], "h%s%d" % (n, k), rest)],
+                    send([(c, dst[:, cols], src[:, cols], s, e)
+                          for c, cols, s, e in ((at(r), a, sem, es), (helper(rank), b, "h%s%d" % (n, k), rest)) if some(cols)],
                          tab(n, mine), sem, k == 1)
 
+    def unpack(k, n):
+        G = ["LG"]
+        if n == "cs":
+            for e in range(2):
+                gcp(T["wx%d" % k][:, 16 + 112 * e:128 + 128 * e:32], T["cs%d" % k][:, e:8:2], 4,
+                    [("cs", k) if k else "wm", ("wx", k)] + G, [("wx", k, e)] + G)
+        if n == "eb":
+            gcp(T.e0[:, 0:16], T["cs%d" % k][:, 16:32], 16, tab("cs", k) + G, ["e0"] + G)
+            for w in (16, 32, 64):
+                gcp(T.e0[:, w:2 * w], T.e0[:, 0:w], w, ["e0"] + G, ["e0"] + G)
+            inside(T["eb%d" % k][:], "e1", T.e0[:], ["e0"] + G, [("eb", k)] + G)
+        if n == "cu":
+            for c in range(0, 1032, 258):
+                gcp(T["cl%d" % k][:, c:c + 258], T["cu%d" % k][:, c:c + 258], 258, [("cu", k)] + G, [("cl", k, c)] + G)
+            lin("S", T["th%d" % k][:], T["cu%d" % k][:, 1031:1032], -1.0, 0.5, [("cu", k)], [("th", k)])
+
     def store(dst, src, sem, R):
-        op("Y", 80, lambda: Y.dma_start(dst, src), R, (), sem=sem, val=16, lat=2200)
+        op("Y", 80, lambda: Y.dma_start(dst, src), R, (), sem=sem, val=16, lat=1500)
 
     def repeat(b, i):
-        w = 1024 // NX
-        for h in range(NX):
-            e = slice(w * h, w * h + w)
-            scan(T["xr%d" % b][:, e], T.m16[:, 0:w], T["xs%d" % i][:, e], A.add, [("xs", i), "m16"], [("xr", b, h)], w // 2)
+        xr, xs, c, R = T["xr%d" % b], T["xs%d" % i], CUT, [("xs", i), "m16"]
+        scan(xr[:, 0:c], T.m16[:, 0:c], xs[:, 0:c], A.mult, A.add, R, [("xr", b, 0)], c // 2)
+        if seq[0] < CFG["gx"]:
+            scan(xr[:, c:], T.m16[:, 0:1024 - c], xs[:, c:], A.mult, A.add, R, [("xr", b, 1), ("xo", b)], (1024 - c) // 2)
+        else:
+            scan(xr[:, c::2], T.m16[:, 0:1024 - c:2], xs[:, c::2], A.mult, A.add, R, [("xr", b, 1)], (1024 - c) // 4)
+            gcp(xr[:, c + 1::2], xr[:, c::2], (1024 - c) // 2, [("xr", b, 1)], [("xo", b)])
 
-    for k in range(1, NR):
+    def arrivals(k):
         for i, n in enumerate(PIECES):
             frm = giver(k, rank)
             val = len(topo.engines(at(frm), core))
-            if n in SPLIT and not near(frm, rank):
-                val += len(topo.engines(helper(frm), core))
-            op("N", 0, None, [], [(n, k)], sem="a%s%d" % (n, k), val=val, lat=CFG["tab"][k - 1] + CFG["piece"] * i)
-        lin("V", T["th%d" % k][:], T["cl%d" % k][:, 1031:1032], -1.0, 0.5, [("cl", k)], [("th", k)])
-    for k in range(1, NR):
-        for n in PIECES:
-            hand_on(k, n)
+            if not near(frm, rank):
+                val = val * some(parts(n, k)[0]) + len(topo.engines(helper(frm), core)) * some(parts(n, k)[1])
+            op("N", 0, None, [("snd", "a%s%d" % (n, k))] * (k == 1), [(n, k)], sem="a%s%d" % (n, k), val=val,
+               lat=CFG["way"][n] if k == 1 else CFG["tab"][k - 2] + CFG["piece"] * i)
+
+    for h in range(2):
+        lin("S", T.cu0[:, 512 * h:512 * h + 512], T.cl0[:, 512 * h:512 * h + 512], 1.0, 0.0, ["cl"], ["cu%d" % h], 512)
+    lin("S", T.cu0[:, 1024:1031], T.cl0[:, 0:7], 1.0, 0.0, ["cl"], ["cu2"])
+    lin("S", T.cu0[:, 1031:1032], T.thf[:], 1.0, 0.0, ["th"], ["cu3"])
+    for k in range(NR):
+        if k:
+            arrivals(k)
+        for what, n in CFG["own" if k == 0 else "other"]:
+            if what == "lay":
+                unpack(k, n)
+            elif k < NR - 1:
+                hand_on(k + 1, n)
 
     wrap = False
     for t in range(NT):
-        k = (t - (t > MOVE)) % NR
+        k = t % NR
         came, wrap = wrap, (rank + k) % NR == NR - 1
-        key, emt, clb, cs = [T["%s%d" % (n, k)] for n in ("key", "em", "cl", "cs")]
+        key, emt, clb, cs, wx, eb = [T["%s%d" % (n, k)] for n in ("key", "em", "cl", "cs", "wx", "eb")]
         for b in range(NB):
             seq[0] = j = t * NB + b
             bA, bB = "a%d" % b, "b%d" % b
             pa, pb = T["pa%d" % b], T["pb%d" % b]
             D, Q, E, TK, SC = [pa[:, 64 * i:64 * i + 64] for i in range(5)]
-            H, PA, VT = pb[:, 0:2, :], pb[:, 2:6, :], pb[:, 6:8, :]
+            H, PA, VT = pb[0:16, 0:2, :], pb[:, 2:6, :], pb[:, 6:8, :]
             xr, df, ad, eg = [T["%s%d" % (n, b)] for n in ("xr", "df", "ad", "eg")]
-            bl, b4, b128 = slice(LB * b, LB * b + LB), slice(4 * b, 4 * b + 4), slice(128 * b, 128 * b + 128)
-            kk, sg, cm, LU, SU, vt, sc, eq = [T[n][:, bl] for n in ("kk", "sg", "cm", "LU", "SU", "vt", "sc", "eq")]
-            pt, am, cc = T.at[:, b128], T.am[:, b128], T.cc[:, b4]
-            SP, SX = T.SA[:, j, 0:64], T.SA[:, j, 64:128]
-            landed = t == MOVE + 1
-            LP = T.P0[:, bl] if t == 0 else T.LA[:, b, 0:64] if landed else T.SA[:, j - NB, 0:64]
-            oh = T.oh[:, LB * j:LB * j + LB]
-            x = xr[:, 0::16]
-            kP = ("LP", j) if t == 0 or landed else ("SP", j - NB)
-            lu = "LU" if t == 0 or landed or came else "SU"
+            bl = slice(LB * b, LB * b + LB)
+            sg, cm, LU, SU, SX, vt, sc, eq = [T[n][:, bl] for n in ("sg", "cm", "LU", "SU", "SX", "vt", "sc", "eq")]
+            kk, pt, cc = T.kk[0:16, bl], T.at[:, 128 * b:128 * b + 128], T.cc[:, 4 * b:4 * b + 4]
+            LP, oh = T.SP[:, LB * j:LB * j + LB], T.oh[:, LB * j:LB * j + LB]
+            x, XR, kP = xr[:, 0::16], [("xr", b, 0), ("xr", b, 1)], ("SP", j)
+            lu = "LU" if t == 0 or came else "SU"
             if t == 0:
-                cp(LU, T.plb[:, bl], ["plb"], [("LU", b)])
-                lin(ENG["xs"], T.xs0[:, 0::16], T.qb[:, bl], 1.0, 0.0, ["qb"], [("xs", 0)])
-                lin("V", LP, T.plb[:, bl], 1.0, -2048.0, ["plb"], [kP])
-            elif lu == "LU":
-                lin(ENG["lu"], LU, LP, 1.0, 2048.0, [kP], [("LU", b)])
-            if landed:
-                lin(ENG["xs"], T.xs0[:, 0::16], T.LA[:, b, 64:128], 1.0, -XO, [kP], [("xs", 0)])
-            if t == 0 or landed:
+                pl = "pl%d" % (b > 0)
+                lin("S" if b else "V", LU, T.plb[:, bl], 1.0, 0.0, [pl], [("LU", b)])
+                lin("S" if b else "V", LP, T.plb[:, bl], 1.0, -2048.0, [pl], [("LP", j), kP])
+                lin("S", T.xs0[:, 0::16], T.qb[:, bl], 1.0, 0.0, ["q"], [("xs", 0)])
                 repeat(b, 0)
-            XR = [("xr", b, h) for h in range(NX)]
+            elif came:
+                lin("S", LU, SU, 1.0, 1.0, [("SU", b)], [("LU", b)])
             win = key[:, 0:2049] if t else key[:, 0:2048]
-            for h in range(NK):
-                w = 1024 // NK
-                e = slice(w * h, w * h + w)
-                off = T[lu][:, LB * b + w // 16 * h:LB * b + w // 16 * (h + 1)]
+            for h, e in enumerate((slice(0, CUT), slice(CUT, 1024))):
+                off = T[lu][:, LB * b + e.start // 16:LB * b + e.stop // 16]
                 tt(df[:, e], win.indirect(off), xr[:, e], A.subtract,
-                   (tab("key", k) if t else ["key"]) + [(lu, b)] + XR[h * NX // NK:((h + 1) * NX - 1) // NK + 1], [("df", b, h)],
-                   (60, w))
-                act(ad[:, e], df[:, e], F.Abs, [("df", b, h)], [("ad", b, h)], w)
-            mm([(H, cs[:, 0:128], x, True, True)], XR + (tab("cs", k) if k else ["wm"]), [("H", b)], bB)
-            lin(ENG["kk"], kk, H, T.ksc[:], T.kb0[:], [("H", b), "ksc", "kb0"], [("kk", b)], banks=[bB])
+                   (tab("key", k) if t else ["key"]) + [(lu, b), XR[h]] + [("xo", b)] * h, [("df", b, h)], (60, e.stop - e.start))
+                act(ad[:, e], df[:, e], F.Abs, [("df", b, h)], [("ad", b, h)], e.stop - e.start)
+            mm([(H, cs[:, 0:16], x, True, True)], XR + (tab("cs", k) if k else ["wm", "wm0"]), [("H", b)], bB)
+            lin("S", kk, H, T.ksc[0:16, :], T.kb0[0:16, :], [("H", b), "ksc", "kb0"], [("kk", b)], banks=[bB])
+            half = [PA[:, :, 16 * e:16 * e + 16] for e in range(2)]
             for e in range(2):
-                o = PA[:, :, 16 * e:16 * e + 16]
-                mm([(o, T["ih%d" % e][:], LP, e == 0, False), (o, cs[:, 128 * e + 128:128 * e + 256], x, False, False),
-                    (o, T["km%d" % e][:], kk, False, False)],
-                   XR + [kP, ("kk", b), ("ih", e), ("km", e)] + (tab("cs", k) if k else [("wx", e)]), [("PA", b)], bB)
-            for h in range(NP):
-                mm([(D, T.wd[:, 15 - i:143 - i], ad[:, i::16], i == 0, i == 15) for i in range(16 // NP * h, 16 // NP * (h + 1))],
-                   [("ad", b, i) for i in range(NK)] + ["wd"], [("D", b)], bA)
+                mm([(half[e], T["ih%d" % e][:], LP, e == 0, False), (half[e], wx[:, 128 * e:128 * e + 128], x, False, False),
+                    (half[e], T["km%d" % e][0:16, :], kk, False, False)],
+                   XR + [kP, ("kk", b), ("ih", e), ("km", e), ("wx", k, e)], [("PA", b)], bB)
+            for h in range(4):
+                mm([(D, T.wd[:, 15 - i:143 - i], ad[:, i::16], i == 0, i == 15) for i in range(4 * h, 4 * h + 4)],
+                   [("ad", b, 0), ("ad", b, 1), "wd"], [("D", b)], bA)
             act(sg, D, F.Sign, [("D", b), ("th", k)], [("sg", b)], 64, [bA], T["th%d" % k][:])
-            mm([(PA[:, :, 16 * e:16 * e + 16], T["sm%d" % e][:], sg, False, e == 1) for e in range(2)],
-               [("sg", b), ("sm", 0), ("sm", 1)], [("PA", b)], bB)
+            mm([(half[e], T["sm%d" % e][:], sg, False, e == 1) for e in range(2)], [("sg", b), ("sm", 0), ("sm", 1)], [("PA", b)], bB)
             mm([(Q, T.idh[:], LP, True, False), (Q, T.n2[:], sg, False, True)], [kP, ("sg", b), "idh", "n2"], [("Q", b)], bA)
             turn(pt, PA, [("PA", b)], [("at", b)], 128, [bB])
-            scan(am, T.m32[:], pt, A.max, [("at", b), "m32"], [("am", b)], 128)
-            lin(ENG["cc"], cc, am[:, 31::32], 0.5, -0.25, [("am", b)], [("cc", b)])
+            unit("V", 256, [lambda i=i, cc=cc, pt=pt: V.tensor_reduce(cc[:, i:i + 1], pt[:, 32 * i:32 * i + 32], AxisListType.X, A.max)
+                            for i in range(4)], [("at", b)], [("cc", b)])
             clw = clb[:, 0:1025] if t else clb[:, 0:1024]
             tt(cm, clw.indirect(cc), sg, A.mult, [("cc", b), ("sg", b)] + (tab("cl", k) if t else ["cl"]), [("cm", b)], (60, 64))
             tt(SU, cm, Q, A.max, [("cm", b), ("Q", b)], [("SU", b)], banks=[bA])
             if t < NT - 1:
-                lin(ENG["sp"], SP, SU, 1.0, wrap - 2048.0, [("SU", b)], [("SP", j)])
-            mm([(VT, T.cv[:], kk, True, False)], [("kk", b), "cv"], [("VT", b)], bB)
+                lin("S", T.SP[:, LB * (j + NB):LB * (j + NB + 1)], SU, 1.0, wrap - 2048.0, [("SU", b)], [("SP", j + NB)])
             mm([(E, T.idb[:], x, True, False)], XR + ["idb"], [("E", b)], bA)
             emw = emt[:, 0:2049] if t else emt[:, 0:2048]
-            for h in range(NE):
-                w = 1024 // NE
-                off = T.SU[:, LB * b + w // 16 * h:LB * b + w // 16 * (h + 1)]
+            both = j >= NB * NT - CFG["both"]
+            c = 512 if both else CFG["votes"]
+            for h, e in enumerate((slice(0, c), slice(c, 1024))):
+                off = T.SU[:, LB * b + e.start // 16:LB * b + e.stop // 16]
                 R = [("SU", b)] + (tab("em", k) if t else ["em"])
-                if h % 2 and j >= NB * NT - CFG["both"]:
-                    cp(eg[:, w * h:w * h + w], emw.indirect(off), R, [("eg", b, h)], (60, w))
+                if h and both:
+                    cp(eg[:, e], emw.indirect(off), R, [("eg", b, h)], (60, e.stop - e.start))
                 else:
-                    act(eg[:, w * h:w * h + w], emw.indirect(off), F.Copy, R, [("eg", b, h)], (78, w))
+                    act(eg[:, e], emw.indirect(off), F.Copy, R, [("eg", b, h)], (78, e.stop - e.start))
             if t == NT - 1:
-                lin("V", T.ip[:, bl], SU, 1.0, float(wrap), [("SU", b)], [("ip", b)])
-                ts(T.iq[:, bl], T.ip[:, bl], 2047, None, A.bitwise_and, None, [("ip", b)], [("iq", b)])
-                cp(T.SYP[:, bl], T.iq[:, bl], [("iq", b)], [("SYP", b)])
+                lin("S", T.ip[:, bl], SU, 1.0, float(wrap), [("SU", b)], [("SP", j + NB)])
+                if b % 2:
+                    c = slice(LB * (b - 1), LB * (b + 1))
+                    ts(T.iq[:, c], T.ip[:, c], 2047, A.bitwise_and, [("SP", j + NB - 1), ("SP", j + NB)], [("iq", b)], 128)
+                    gcp(T.SYP[:, c], T.iq[:, c], 2 * LB, [("iq", b)], [("SYP", b)])
                 if b == NB - 1:
-                    R = [("SYP", i) for i in range(NB)]
-                    if t == MOVE:
-                        pass_on(1, T.FYP[:], T.SYP[:], "ap", R, ["FYP"])
-                    store(T.yp[:], T["FYP" if t == MOVE else "SYP"][:], "op", ["FYP"] if t == MOVE else R)
-            for h in range(NP):
-                mm([(VT, T.idb[:], eg[:, i::16], False, i == 15) for i in range(16 // NP * h, 16 // NP * (h + 1))],
-                   [("eg", b, i) for i in range(NE)] + ["idb"], [("VT", b)], bB)
+                    pass_on(1, T.FYP[:], T.SYP[:], "ap", [("SYP", i) for i in range(1, NB, 2)], ["FYP"])
+                    store(T.yp[:], T.FYP[:], "op", ["FYP"])
+            for h in range(4):
+                mm([(VT, T.idb[:], eg[:, i::16], i == 0, i == 15) for i in range(4 * h, 4 * h + 4)],
+                   [("eg", b, 0), ("eg", b, 1), "idb"], [("VT", b)], bB)
             turn(vt, VT, [("VT", b)], [("vt", b)], 64, [bB])
-            scan(sc, T.m16[:, 0:64], vt, A.max, [("vt", b), "m16"], [("sc", b)], 64)
-            scan(SC[:, ::-1], T.m16[:, 0:64], sc[:, ::-1], A.max, [("sc", b), "m16"], [("SC", b)], 64, [bA])
+            scan(sc, T.up[:], vt, A.add, A.max, [("vt", b), "up"], [("sc", b)], 64)
+            scan(SC[:, ::-1], T.dn[:], sc[:, ::-1], A.add, A.max, [("sc", b), "dn"], [("SC", b)], 64, [bA])
             tt(eq, vt, SC, A.is_equal, [("vt", b), ("SC", b)], [("eq", b)], banks=[bA])
             turn(oh, eq, [("eq", b)], [("oh", j)], 64)
-            mm([(E, cs[:, 384:512], oh, False, True)], [("oh", j)] + (tab("cs", k) if k else ["em2"]), [("E", b)], bA)
-            if t != MOVE and t < NT - 1:
-                lin(ENG["sx"], T.xs1[:, 0::16], E, 0.5, -0.25, [("E", b)], [("SX", j), ("xs", 1)], banks=[bA])
+            mm([(E, eb[:], oh, False, True)], [("oh", j), ("eb", k)], [("E", b)], bA)
+            if t < NT - 1:
+                lin("S", T.xs1[:, 0::16], E, 0.5, -0.25, [("E", b)], [("SX", b), ("xs", 1)], banks=[bA])
                 seq[0] = j + NB
                 repeat(b, 1)
                 seq[0] = j
             else:
-                lin(ENG["sx"], SX, E, 0.5, XO - 0.25, [("E", b)], [("SX", j)], banks=[bA])
-            if t == MOVE < NT - 1:
-                pass_on(1, T.LA[:, b, :], T.SA[:, j, :], "ar%d" % b, [("SP", j), ("SX", j)], [("LP", j + NB)])
-            if t == NT - 1:
-                lin(ENG["sx"], T.SYQ[:, bl], SX, 1.0, -XO, [("SX", j)], [("SYQ", b)])
-                if b >= NB - 2:
-                    c, i, R = slice(0, 192) if b == NB - 2 else bl, b - NB + 2, [("SYQ", i) for i in range(b + 1)]
-                    if t == MOVE:
-                        pass_on(1, T.FYQ[:, c], T.SYQ[:, c], "aq%d" % i, R, [("FYQ", i)])
-                    store(T.yq[:, c], T["FYQ" if t == MOVE else "SYQ"][:, c], "oq%d" % i, [("FYQ", i)] if t == MOVE else R)
+                lin("S", SX, E, 0.5, XO - 0.25, [("E", b)], [("SX", b)], banks=[bA])
+                lin("S", T.SYQ[:, bl], SX, 1.0, -XO, [("SX", b)], [("SYQ", b)])
+                if b % 2:
+                    c, i = slice(LB * (b - 1), LB * (b + 1)), b // 2
+                    pass_on(1, T.FYQ[:, c], T.SYQ[:, c], "aq%d" % i, [("SYQ", b - 1), ("SYQ", b)], [("FYQ", i)])
+                    store(T.yq[:, c], T.FYQ[:, c], "oq%d" % i, [("FYQ", i)])
             if b == NB - 1:
                 mm([(TK, T.wk[:, 3 - i:131 - i], T.oh[:, LB * (NB * t + i):LB * (NB * t + i + 1)], i == 0, i == NB - 1)
                     for i in range(NB)], [("oh", NB * t + i) for i in range(NB)] + ["wk"], ["TK"], bA)
@@ -419,14 +449,13 @@ def schedule(ops):
         d, order = set(), set()
         for k in o["R"]:
             if k in lastw:
-                d.add(lastw[k])
-                if k in ("LG", "LY", "LS"):
-                    order.add(lastw[k])
+                (order if k in ("LG", "LY", "LS") else d).add(lastw[k])
             readers.setdefault(k, []).append(o["i"])
         for k in o["W"]:
-            if k in lastw:
-                d.add(lastw[k])
-            d.update(readers.get(k, []))
+            if k not in ("LG", "LY", "LS"):
+                if k in lastw:
+                    d.add(lastw[k])
+                d.update(readers.get(k, []))
             lastw[k], readers[k] = o["i"], []
         for k in o["banks"]:
             for q, i in bank.setdefault(k, {}).items():
@@ -436,16 +465,114 @@ def schedule(ops):
         d.discard(o["i"])
         if o["q"] == "P":
             order = {i for i in d if ops[i]["q"] == "P"}
-        o["D"], o["O"] = d, order
+        else:
+            order -= d
+        o["D"], o["O"] = d | order, order
         o["after"] = o["lat"] + (CFG["link"] if o["q"] == "N" else CFG["hop"])
-    key = [1e9] * len(ops)
-    for o in reversed(ops):
-        mine = CFG["per"] * o["seq"] + CFG["off"].get(o["kind"], 1e9) if o["kind"] else -o["bias"] if o["bias"] else 1e9
-        key[o["i"]] = min(key[o["i"]], mine)
+    n, soft = len(ops), []
+    key = [-o["bias"] if o["bias"] else 1e9 for o in ops]
+    for q, turn in CFG["round"].items():
+        spot = {kind: lag + at / len(turn) for at, (kind, lag) in enumerate(turn)}
+        mine = sorted((o["seq"] + spot[o["kind"]], o["i"]) for o in ops if o["q"] == q and o["kind"] in spot)
+        for (_, a), (_, b) in zip(mine, mine[1:]):
+            if a not in ops[b]["D"]:
+                ops[b]["D"].add(a)
+                ops[b]["O"].add(a)
+                soft.append((a, b))
+        for v, i in mine:
+            key[i] = v
+    succ, left = [[] for _ in ops], [len(o["D"]) for o in ops]
+    for o in ops:
         for d in o["D"]:
-            key[d] = min(key[d], key[o["i"]] - ops[d]["dur"])
-    place(ops, sorted(range(len(ops)), key=lambda i: (key[i], i)))
-    return max(o["st"] + o["dur"] + o["lat"] for o in ops)
+            succ[d].append(o["i"])
+    order, todo = [], [i for i in range(n) if not left[i]]
+    while todo:
+        order.append(todo.pop())
+        for s in succ[order[-1]]:
+            left[s] -= 1
+            if not left[s]:
+                todo.append(s)
+    assert len(order) == n, "the rounds ask for a call before what it needs"
+    for i in reversed(order):
+        key[i] = min([key[i]] + [key[s] - 1e-4 for s in succ[i]])
+    place(ops, sorted(range(n), key=lambda i: key[i]))
+    for a, b in soft:
+        ops[b]["D"].discard(a)
+        ops[b]["O"].discard(a)
+    if CFG["tries"]:
+        shorten(ops)
+
+
+def shorten(ops):
+    n = len(ops)
+    q, need = [o["q"] for o in ops], [o["D"] for o in ops]
+    lat = [o["lat"] * (CFG["soon"] if o["q"] == "N" else 1) for o in ops]
+    cases = []
+    for f, gam, hop, dma in CFG["cases"]:
+        cases.append(([(o["cyc"] + gam * o["gat"]) * (0.83 * f if o["sem"] is None else 1) for o in ops],
+                      [[(d, 0.0 if d in o["O"] else lat[d] + CFG["link"] if q[d] == "N" else dma * lat[d] + hop)
+                        for d in o["D"]] for o in ops]))
+
+    def times(order, frm, old):
+        seen, new = {}, []
+        for i in reversed(order[:frm]):
+            if q[i] not in seen:
+                seen[q[i]] = i
+                if len(seen) == 6:
+                    break
+        rest = order[frm:]
+        for (dur, pred), (_, end, why) in zip(cases, old):
+            end, why, last = end[:], why[:], dict(seen)
+            for i in rest:
+                p = last.get(q[i], -1) if q[i] != "N" else -1
+                st, w = (end[p], -2 - p) if p >= 0 else (0.0, -1)
+                for d, gap in pred[i]:
+                    if end[d] + gap > st:
+                        st, w = end[d] + gap, d
+                end[i], why[i], last[q[i]] = st + dur[i], w, i
+            new.append((max((end[i] + lat[i], i) for i in final), end, why))
+        return new
+
+    final = [i for i in range(n) if q[i] == "Y"]
+    order = [o["i"] for o in sorted(ops, key=lambda o: (o["st"], o["i"]))]
+    now = times(order, 0, [(0, [0.0] * n, [-1] * n)] * len(cases))
+    weight = [now[0][0][0] / c[0][0] / len(cases) for c in now]
+
+    def total(got):
+        return sum(w * c[0][0] for w, c in zip(weight, got))
+
+    best, x, pairs = (total(now), now), 12345, None
+    for turn in range(CFG["tries"]):
+        if pairs is None:
+            pairs = []
+            for (_, i), end, why in now:
+                while i >= 0:
+                    if why[i] <= -2 and not CFG["ends"][0] < end[i] / end[final[-1]] < CFG["ends"][1]:
+                        pairs.append((-2 - why[i], i))
+                    i = -2 - why[i] if why[i] <= -2 else why[i]
+        x = (x * 1103515245 + 12345) % 2 ** 31
+        a, b = pairs[(x >> 8) % len(pairs)]
+        ia, ib = order.index(a), order.index(b)
+        front, rest, qs = [b], [], {q[b]}
+        for i in reversed(order[ia:ib]):
+            if (q[i] in qs and q[i] != "N" and i != a) or any(i in need[j] for j in front):
+                front.append(i)
+                qs.add(q[i])
+            else:
+                rest.append(i)
+        if front[-1] == a:
+            continue
+        new = order[:ia] + front[::-1] + rest[::-1] + order[ib + 1:]
+        got = times(new, ia, now)
+        x = (x * 1103515245 + 12345) % 2 ** 31
+        heat = CFG["heat"] * (1 - turn / CFG["tries"]) + 1
+        if total(got) - total(now) <= -heat * math.log((x + 1) / 2 ** 31):
+            order, now, pairs = new, got, None
+            if total(now) < best[0]:
+                best = (total(now), now)
+    for o in ops:
+        o["st"] = best[1][0][1][o["i"]] - cases[0][0][o["i"]]
+        o["end"] = best[1][0][1][o["i"]] + o["after"]
 
 
 def emit_all(ops, queues, T, g):

@@ -3,24 +3,33 @@ from concourse.mybir import AluOpType, ActivationFunctionType, AxisListType
 from concourse.bass import DstId, RemoteDMATransfer
 
 NR, NB, LB, NT = 4, 4, 64, 5
+CORES = 256
 XO = 1536.0
 CFG = {
-    "cut": 640,
-    "votes": 576,
-    "gx": 5,
-    "both": 2,
+    "keys": [0, 512, 832, 928, 1024], "ahead": 6,
+    "cut": 512, "votes": 704,
+    "gx": 4,
+    "sum": [99, 18],
+    "both": 18,
+    "move": False, "pack": [1, 2], "close": 0.6, "every": 1, "late": 2, "mate": [],
+    "help": [],
     "round": {
-        "V": [("SU0", 2), ("vt0", 3), ("eg1", 2), ("xr0", 0), ("sc0", 3), ("xr1", 0), ("df0", 0), ("SC0", 3), ("df1", 0), ("eq0", 3),
-              ("at0", 1), ("oh0", 3), ("cc0", 1), ("cm0", 1)],
-        "S": [("sg0", 1), ("kk0", 0), ("eg1", 2), ("ad0", 0), ("SP0", 2), ("ad1", 0), ("SX0", 3), ("eg0", 1)],
-        "P": [("D0", 1), ("D1", 1), ("D2", 1), ("D3", 1), ("H0", 0), ("E0", 2), ("PA2", 1), ("PA0", 0), ("Q0", 1), ("PA1", 0),
-              ("VT0", 2), ("VT1", 2), ("VT2", 2), ("E1", 3), ("VT3", 2)]},
-    "own": [("lay", "cs"), ("on", "key"), ("on", "cs"), ("on", "cu"), ("on", "em"), ("lay", "eb")],
-    "other": [("on", "key"), ("on", "cs"), ("lay", "cs"), ("on", "cu"), ("lay", "cu"), ("on", "em"), ("lay", "eb")],
-    "f": 1.15, "gam": 1.56, "hop": 200, "link": 2600, "iss": 700, "first": 2000, "tab": [29000, 43000], "piece": 1500,
-    "way": {"key": 8500, "cs": 3500, "cu": 9500, "em": 10500},
-    "cases": [(1.0, 1.56, 200, 1.0), (1.3, 1.4, 140, 1.3), (1.4, 1.9, 200, 1.1), (1.1, 1.3, 180, 1.6)],
-    "ends": [0.4, 0.78], "tries": 9000, "heat": 40, "soon": 0.85}
+        "V": [("at1", 2), ("df2", 1), ("cc0", 2), ("cc1", 2), ("kg0", -1), ("cm0", 2), ("kg1", -1), ("SU0", 2), ("xr2", 0), ("xr0", 0),
+              ("vt0", 3), ("xr1", 0), ("sc0", 3), ("SC0", 3), ("df0", 0), ("eq0", 3), ("df1", 0), ("at0", 1), ("oh0", 3)],
+        "S": [("eg0", 2), ("LU0", -2), ("yt0", 2), ("sg0", 1), ("eg1", 2), ("ad0", 0), ("kk0", 0), ("ad1", 0), ("ad2", 0), ("SX0", 3),
+              ("ad3", 0)],
+        "P": [("VT6", 3), ("VT7", 3), ("D0", 1), ("D1", 1), ("D2", 1), ("D3", 1), ("D4", 1), ("D5", 1), ("D6", 1), ("D7", 1), ("H0", 0),
+              ("PA0", 1), ("PA1", 1), ("E0", 2), ("PA2", 1), ("Q0", 1), ("VT0", 2), ("VT1", 2), ("VT2", 2), ("E1", 3), ("VT3", 2),
+              ("VT4", 2), ("VT5", 2)],
+        "G": [("xo0", 0), ("SP0", 0)]},
+    "own": [("on", "cs"), ("lay", "cs"), ("on", "key"), ("on", "cu"), ("on", "em")],
+    "other": [("on", "key"), ("on", "cs"), ("on", "cu"), ("lay", "cu"), ("on", "em")],
+    "f": 1.05, "gam": 1.56, "hop": [245, 205, 250], "link": 2600, "iss": 700, "first": 2800, "piece": 1000,
+    "tab": [[12000, 22000, 0], [7500, 21000, 32000]],
+    "way": {"key": 8500, "cs": 3500, "cu": 8000, "em": 10500},
+    "cases": [(1.0, 1.56, [250, 200, 250], 1.0), (1.1, 1.2, [250, 210, 260], 1.3), (1.4, 1.9, [240, 200, 250], 1.1),
+              (1.2, 1.5, [220, 190, 260], 1.5)],
+    "full": [3, 21], "ends": [0.4, 0.78], "tries": 9000, "heat": 40, "soon": 0.85}
 
 SCRATCH = {
     "plb": ("sbuf", [128, 256], "int32"), "qb": ("sbuf", [128, 256], "bfloat16"),
@@ -31,19 +40,20 @@ SCRATCH = {
     "FYP": ("sbuf", [128, 256], "float32"), "FYQ": ("sbuf", [128, 256], "bfloat16"),
     "ip": ("sbuf", [128, 256], "int32"), "iq": ("sbuf", [128, 256], "int32"),
     "xs0": ("sbuf", [128, 1024], "uint16"), "xs1": ("sbuf", [128, 1024], "uint16"),
-    "m16": ("sbuf", [128, 640], "bfloat16"), "up": ("sbuf", [128, 64], "bfloat16"), "dn": ("sbuf", [128, 64], "bfloat16"),
+    "MV": ("sbuf", [128, 512], "uint16"), "MR": ("sbuf", [128, 512], "uint16"), "kg": ("sbuf", [128, 1024], "float16"),
+    "ob": ("sbuf", [128, 144], "bfloat16"), "m16": ("sbuf", [128, 640], "bfloat16"), "cs": ("sbuf", [128, NR, 16], "bfloat16"), "emt": ("sbuf", [128, 16], "bfloat16"),
+    "vs": ("sbuf", [128, 1024], "float16"),
     "wd": ("sbuf", [128, 144], "bfloat16"), "wk": ("sbuf", [128, 132], "bfloat16"),
-    "ii": ("sbuf", [128, 1], "int32"), "ik": ("sbuf", [128, 1], "int32"), "i16": ("sbuf", [128, 1], "int32"),
+    "junk": ("sbuf", [128, 8], "float32"),
     "oh": ("sbuf", [128, 1280], "bfloat16"), "ytb": ("sbuf", [128, 320], "float32"), "ytl": ("sbuf", [128, 320], "float32"),
 }
 for _k in range(NR):
-    SCRATCH.update({"key%d" % _k: ("sbuf", [128, 2064], "bfloat16"), "em%d" % _k: ("sbuf", [128, 2064], "bfloat16"),
+    SCRATCH.update({"key%d" % _k: ("sbuf", [128, 2064], "bfloat16"), "em%d" % _k: ("sbuf", [128, 2192], "bfloat16"),
                     "cl%d" % _k: ("sbuf", [128, 1032], "int32"), "cu%d" % _k: ("sbuf", [128, 1032], "uint16"),
-                    "cs%d" % _k: ("sbuf", [128, 32], "bfloat16"), "eb%d" % _k: ("sbuf", [128, 128], "bfloat16"),
                     "wx%d" % _k: ("sbuf", [128, 256], "bfloat16"), "th%d" % _k: ("sbuf", [128, 1], "float32")})
-for _n in ("ob", "bm0", "bm", "idb", "ub", "ci", "p2", "n2", "e0", "e1", "sm0", "sm1"):
+for _n in ("m32", "bm0", "bm", "idb", "ub", "p2", "n2", "am", "sm0", "sm1"):
     SCRATCH[_n] = ("sbuf", [128, 128], "bfloat16")
-for _n in ("idh", "ih0", "ih1", "k1", "km0", "km1"):
+for _n in ("idh", "ih0", "ih1", "km0", "km1"):
     SCRATCH[_n] = ("sbuf", [128, 128], "float16")
 for _n in ("kc", "odd", "even", "ksc", "ka", "kb", "kb0", "r8", "m9", "hc", "wf"):
     SCRATCH[_n] = ("sbuf", [128, 1], "float32")
@@ -53,16 +63,17 @@ for _n, _s, _d in (("kk", [128, 256], "float16"), ("sg", [128, 256], "bfloat16")
     SCRATCH[_n] = ("sbuf", _s, _d)
 for _b in range(NB):
     SCRATCH.update({
-        "xr%d" % _b: ("sbuf", [128, 1024], "bfloat16"), "df%d" % _b: ("sbuf", [128, 1024], "bfloat16"),
-        "ad%d" % _b: ("sbuf", [128, 1024], "bfloat16"), "eg%d" % _b: ("sbuf", [128, 1024], "bfloat16"),
+        "xr%d" % _b: ("sbuf", [128, 1024], "bfloat16"), "df%d" % _b: ("sbuf", [128, 1024], "float16"),
+        "ad%d" % _b: ("sbuf", [128, 1024], "bfloat16"), "eg%d" % _b: ("sbuf", [128, 1024], "float16"),
         "pa%d" % _b: ("psum", [128, 512], "float32"), "pb%d" % _b: ("psum", [128, 16, 32], "float32"),
     })
-PIECES = {"key": 2064, "cs": 32, "cu": 1032, "em": 2064}
-STRAIGHT = {("key", 1): 1, ("cu", 1): 0, ("cs", 1): 1, ("cs", 2): 1}
+PIECES = {"key": 2064, "cs": 8, "cu": 1032, "em": 2192}
+STRAIGHT = {("key", 1): 1, ("cu", 1): 0, ("cs", 2): 1}
 LOADS = ["pl0", "q", "key", "pl1", "w", "th", "cl", "emb", "em"]
 SEMAPHORES = (["cv", "cs", "ct", "cg", "sent"] + ["ld_" + n for n in LOADS]
               + ["%s%s%d" % (a, n, k) for a in "ah" for n in PIECES for k in range(1, NR)]
-              + ["op", "oq0", "oq1", "ap", "aq0", "aq1"] + ["oy%d" % t for t in range(NT)] + ["ay%d" % t for t in range(1, NR)])
+              + ["op", "oq0", "oq1", "ap", "aq0", "aq1"] + ["oy%d" % t for t in range(NT)] + ["ay%d" % t for t in range(NT)]
+              + ["am%d" % b for b in range(NB)] + ["m%s%d" % (n, h) for n in PIECES for h in range(2)])
 
 
 def rank_program(g, core, T, topo):
@@ -88,14 +99,42 @@ def rank_program(g, core, T, topo):
     def some(c):
         return c.stop > c.start
 
+    def form(n, k, r):
+        def far(k, r):
+            return k in CFG["pack"] and not near(giver(k, r), r)
+        return "cl" if n == "cu" and not (far(k, r) or (giver(k + 1, r - 1) - r) % NR == 0 and far(k + 1, r - 1)) else n
+
+    def tile(n, k, cols=None):
+        cols = cols or slice(0, PIECES[n if n != "cl" else "cu"])
+        return T.cs[:, k, cols] if n == "cs" else T["%s%d" % (n, k)][:, cols]
+
+    def aside(n, k, r):
+        return n in CFG["mate"] and k == 2 and not near(r, r + 1)
+
+    def mate(r):
+        return [c for c in range(CORES) if topo.mates(c, at(r)) and topo.die(c) == topo.die(at(r))
+                and topo.may_write(at(r + 2), c) and topo.may_write(c, at(r))][0]
+
+    def halves(n):
+        return [slice(PIECES[n] // 2 * h, PIECES[n] // 2 * (h + 1)) for h in range(2)]
+
     if rank is None:
         for r in range(NR):
+            if CFG["mate"] and not near(r, r + 1) and core == mate(r):
+                rid, pid = topo.addr(at(r), core)
+                for n in CFG["mate"]:
+                    for h, cols in enumerate(halves(n)):
+                        part = tile(form(n, 2, r), 2, cols)
+                        g.wait_ge(T.sem["m%s%d" % (n, h)], len(topo.engines(at(r + 2), core)))
+                        g.remote_dma(part, part, T.sem["a%s2" % n], T.sem.sent, pid, rid, topo.mask(core, at(r)))
+                g.wait_ge(T.sem.sent, 2 * len(CFG["mate"]) * len(topo.engines(core, at(r))))
             if not near(r, r - 1) and core == helper(r):
                 rid, pid = topo.addr(at(r - 1), core)
                 came = len(topo.engines(at(r), core)) - len(topo.engines(at(r), at(r - 1)))
-                far = [(k, n) for k in range(1, NR) for n in PIECES if not near(r - 1, r - 1 + k) and some(parts(n, k)[1])]
+                far = [(k, n) for k in range(1, NR) for n in PIECES
+                       if not near(r - 1, r - 1 + k) and some(parts(n, k)[1]) and not aside(n, k, r - 1)]
                 for k, n in far:
-                    part = T["%s%d" % (n, k)][:, parts(n, k)[1]]
+                    part = tile(form(n, k, r - 1), k, parts(n, k)[1])
                     g.wait_ge(T.sem["h%s%d" % (n, k)], came)
                     g.remote_dma(part, part, T.sem["a%s%d" % (n, k)], T.sem.sent, pid, rid, topo.mask(core, at(r - 1)))
                 g.wait_ge(T.sem.sent, len(far) * len(topo.engines(core, at(r - 1))))
@@ -103,6 +142,7 @@ def rank_program(g, core, T, topo):
     A, F = AluOpType, ActivationFunctionType
     V, S, P, Y = g.vector, g.scalar, g.tensor, g.sync
     ops, seq, seen, CUT = [], [None], {}, CFG["cut"]
+    GX = CFG["gx"] + CFG["late"] * (form("cu", 1, rank) == "cu")
 
     def op(q, dur, emit, R=(), W=(), banks=(), sem=None, val=1, lat=0, bias=0):
         kind = None
@@ -142,8 +182,8 @@ def rank_program(g, core, T, topo):
     def turn(out, i, R, W, n, banks=()):
         op("V", n, lambda: V.transpose(out, i), R, W, banks)
 
-    def act(out, i, f, R, W, n, banks=(), bias=0.0):
-        op("S", n, lambda: S.activation(out, i, f, bias=bias), R, W, banks)
+    def act(out, i, f, R, W, n, banks=(), bias=0.0, scale=1.0):
+        op("S", n, lambda: S.activation(out, i, f, bias=bias, scale=scale), R, W, banks)
 
     def unit(q, n, calls, R, W, banks=()):
         def f():
@@ -156,11 +196,17 @@ def rank_program(g, core, T, topo):
     def mm(ms_, R, W, bank):
         unit("P", 64 * len(ms_), [lambda m=m: P.matmul(*m) for m in ms_], R, W, [bank])
 
-    def aff(out, src, pat, cmp, base, cm, R, W, n=128):
-        op("G", 205 + 2 * n, lambda: g.affine_select(out, src, pat, cmp, 0.0, base, cm), R, W)
+    def aff(out, src, pat, cmp, base, cm, R, W, n=128, fill=0.0):
+        op("G", 205 + 2 * n, lambda: g.affine_select(out, src, pat, cmp, fill, base, cm), R, W)
 
     def gcp(out, src, n, R, W):
         aff(out, src, [[0, n]], A.is_ge, 0, 0, R, W, n)
+
+    def copy(out, src, n, R, W):
+        if seq[0] >= GX:
+            gcp(out, src, n, R, W)
+        else:
+            lin("S", out, src, 1.0, 0.0, R, W)
 
     def inside(out, tmp, src, R, W):
         aff(T[tmp][:], src, [[-16, 8], [0, 16]], A.is_ge, 0, 1, R, [tmp])
@@ -171,124 +217,150 @@ def rank_program(g, core, T, topo):
     load("Y", "key", T.key0[:, 0:2048], T.key[:], 2600)
     load("S", "w", T.wb[:], T.w[:], 1600)
     load("Y", "pl1", T.plb[:, LB:], T.pl[:, LB:], 3000)
-    load("S", "th", T.thf[:], T.th[:], 3100)
-    load("S", "emb", T.cs0[:, 16:32], T.emb[:], 3200)
+    load("Y", "th", T.thf[:], T.th[:], 3100)
+    load("Y", "emb", T.emt[:], T.emb[:], 3200)
     load("Y", "cl", T.cl0[:, 0:1024], T.cl[:], 4400)
     load("Y", "em", T.em0[:, 0:2048], T.em[:], 5700)
 
     ms(T.ob[:], 1.0, ["ob"])
-    op("G", 140, lambda: g.iota(T.ii[:], [[0, 1]], 0, 1), (), ["ii"])
-    inside(T.bm[:], "bm0", T.ob[:], ["ob"], ["bm"])
-    aff(T.idb[:], T.ob[:], [[-1, 128]], A.is_equal, 0, 1, ["ob"], ["idb"])
-    aff(T.ub[:], T.bm[:], [[1, 128]], A.is_ge, -1, -1, ["bm"], ["ub"])
-    op("G", 400, lambda: g.iota(T.ci[:], [[0, 8], [-1, 16]], 0, 0, allow_small_or_imprecise_dtypes=True), (), ["ci"])
-    ms(T.xs0[:], 0, [("xs", 0)], 512)
+    op("S", 1600, lambda: S.activation(T.wd[:], T.ob[:], F.Sigmoid, scale=-256.0), ["ob", "LS"], ["wd"], bias=1e6)
+    aff(T.idb[:], T.ob[:, 0:128], [[-1, 128]], A.is_equal, 0, 1, ["ob"], ["idb", "LG"])
+    inside(T.bm[:], "bm0", T.ob[:, 0:128], ["ob", "LG"], ["bm", "LG"])
+    aff(T.ub[:], T.bm[:], [[1, 128]], A.is_ge, -1, -1, ["bm", "LG"], ["ub", "LG"])
     ms(T.m16[:], 1.0, ["m16"], 320)
     ms(T.m16[:, 0::16], 0.0, ["m16"])
+    ms(T.xs0[:], 0, ["xs0"], 512)
     for h in range(2):
-        lin("S", T.xs1[:, 512 * h:512 * h + 512], T.m16[:, 0:512], 0.0, 0.0, ["m16"], [("xs", 1)], 512)
-    for n, c in (("up", 1 / 32), ("dn", -1 / 32)):
-        lin("S", T[n][:], T.m16[:, 0:64], 8192.0 + c, -8192.0, ["m16", "cl"], [n])
-    ts(T.ik[:], T.ii[:], 15, A.bitwise_and, ["ii"], ["ik"])
-    ts(T.i16[:], T.ii[:], 16, A.bitwise_and, ["ii"], ["i16"])
-    cp(T.kc[:], T.ik[:], ["ik"], ["kc"])
-    ts(T.odd[:], T.i16[:], 0.03125, A.mult, ["i16"], ["odd"])
-    lin("S", T.even[:], T.odd[:], -1.0, 0.5, ["odd"], ["even"])
-    lin("S", T.th0[:], T.thf[:], -1.0, 0.5, ["th"], [("th", 0)])
+        ms(T.xs1[:, 512 * h:512 * h + 512], 0, ["xs1"], 256)
+    aff(T.am[:], T.idb[:], [[-1, 128]], A.not_equal, -1, 1, ["idb"], ["am"], fill=-1.0)
+    gcp(T.am[:, 15::16], T.idb[:, 15::16], 8, ["idb", "am"], ["am"])
+
+    def total(n, src, mul, add, R):
+        op("S", 90, lambda: S.activation(T.junk[:, 0:src.shape[1]], src, F.Identity, bias=add, scale=mul, accum_out=T[n][:]), R, [n, "junk"])
+
+    total("kc", T.idb[:, 15::16], 16.0, -0.125, ["idb"])
+    total("even", T.bm[:, 0::32], 0.5, 0.0, ["bm"])
+    lin("S", T.odd[:], T.even[:], -1.0, 0.5, ["even"], ["odd"])
+    lin("S", T.th0[:], T.thf[:], -256.0, 128.0, ["th"], [("th", 0)])
     lin("S", T.wf[:], T.wb[:], 1.0, 0.0, ["w"], ["wf"])
-    ms(T.wd[:], 0.0, ["wd"], 72)
     cp(T.wd[:, 15:128:16], T.bm[:, 0::16], ["bm"], ["wd"])
     ms(T.wk[:], 0.0, ["wk"], 66)
     lin("S", T.wk[:, 3:35:4], T.bm[:, 0::16], T.kc[:], 0.0, ["bm", "kc"], ["wk"])
     lin("S", T.ksc[:], T.ub[:, 8:9], 2.0 ** -10, 0.0, ["ub"], ["ksc"])
-    lin("S", T.r8[:], T.idb[:, 8:9], 0.5, 0.0, ["idb"], ["r8"])
-    lin("S", T.m9[:], T.idb[:, 9:10], -4.0, 0.0, ["idb"], ["m9"])
-    lin("S", T.ka[:], T.idb[:, 9:10], 0.0625, 0.0, ["idb"], ["ka"])
-    lin("S", T.kb[:], T.idb[:, 8:9], 2048.0, T.ka[:], ["idb", "ka"], ["kb"])
+    lin("V", T.r8[:], T.idb[:, 8:9], -1.0, 0.0, ["idb"], ["r8"])
+    lin("V", T.m9[:], T.idb[:, 9:10], -4.0, 0.0, ["idb"], ["m9"])
+    lin("V", T.ka[:], T.idb[:, 9:10], 0.0625, 0.0, ["idb"], ["ka"])
+    lin("V", T.kb[:], T.idb[:, 8:9], 2048.0, T.ka[:], ["idb", "ka"], ["kb"])
     lin("S", T.kb0[:], T.ub[:, 8:9], 1025.0 - 511.5 / 1024, T.kb[:], ["ub", "kb"], ["kb0"])
-    lin("S", T.hc[:], T.idb[:, 8:9], 504.5, T.m9[:], ["idb", "m9"], ["hc"])
-    lin("S", T.idh[:], T.idb[:], 1.0, 0.0, ["idb"], ["idh"], 128)
-    lin("S", T.n2[:], T.idb[:], -2048.0, 0.0, ["idb"], ["n2"], 128)
-    lin("V", T.p2[:], T.idb[:], 2048.0, 0.0, ["idb"], ["p2"])
-    ms(T.cs0[:, 8:16], 0.0, ["wm0"])
-    lin("S", T.cs0[:, 0:8], T.bm[:, 0::16], T.wf[:], 0.0, ["bm", "wf"], ["wm"])
-    lin("S", T.k1[0:16, :], T.ci[0:16, :], T.r8[0:16, :], T.m9[0:16, :], ["ci", "r8", "m9"], ["k1"], 128)
+    lin("V", T.hc[:], T.idb[:, 8:9], 496.5, T.m9[:], ["idb", "m9"], ["hc"])
+    lin("V", T.idh[:], T.idb[:], 1.0, 0.0, ["idb"], ["idh"])
+    lin("V", T.n2[:], T.idb[:], -4096.0, 0.0, ["idb"], ["n2"])
+    lin("V", T.p2[:], T.idb[:], 4096.0, 0.0, ["idb"], ["p2"])
+    ms(T.cs[:, :, 8:16], 0.0, ["wm0"])
+    lin("S", T.cs[:, 0, 0:8], T.bm[:, 0::16], T.wf[:], 0.0, ["bm", "wf"], ["wm"])
+    eb = T.pa3[:, 320:448]
+    mm([(eb[:, 16 * i:16 * i + 16], T.am[:], T.emt[:], i == 0, i == 7) for i in range(8)], ["am", "emb"], ["eb0"], "a3")
+    tt(T.em0[:, 2064:], eb, T.bm[:], A.mult, ["eb0", "bm"], ["eb"], 128, ["a3"])
+    ci = T.pa2[0:16, 320:448]
+    mm([(ci, T.ob[:, 0:16], T.ub[:], True, True)], ["ob", "ub"], ["ci"], "a2")
     sm = T.pa0[:, 320:448]
     mm([(sm, T.p2[:], T.ub[:], True, False), (sm, T.n2[:], T.idb[:], False, False),
         (sm[:, 16::32], T.p2[:], T.bm[:, 0::32], False, False), (sm[:, 0::32], T.p2[:], T.bm[:, 16::32], False, True)],
        ["p2", "ub", "n2", "idb", "bm"], ["sm"], "a0")
     for e, c in enumerate(("even", "odd")):
         km = T["km%d" % e]
-        aff(km[0:16, :], T.k1[0:16, :], [[0, 4], [1, 2], [0, 16]], A.is_equal, -e, 0, ["k1"], [("km", e)])
+        lin("S", km[0:16, :], ci, T.r8[0:16, :], T.m9[0:16, :], ["ci", "r8", "m9"], [("km", e)], 128, ["a2"])
         lin("S", km[0:16, 16 - 16 * e::32], T.idb[0:16, e:8:2], -1024.0, T.hc[0:16, :], ["idb", "hc", ("km", e)], [("km", e)])
         lin("S", T["ih%d" % e][:], T.idb[:], T[c][:], 0.0, ["idb", c], [("ih", e)], 128)
         lin("S", T["sm%d" % e][:], sm, T[c][:], 0.0, ["sm", c], [("sm", e)], 128, ["a0"])
     ms(T.wx0[:], 0.0, [("wx", 0)], 128)
     for k in range(1, NR):
         op("G", 670, lambda k=k: g.iota(T["wx%d" % k][:], [[0, 256]], 0, 0, allow_small_or_imprecise_dtypes=True), (), [("wx", k)])
-    gcp(T.cl0[:, 1024:1025], T.cl0[:, 0:1], 1, ["cl"], ["clx"])
+    lin("S", T.cl0[:, 1024:1031], T.cl0[:, 0:7], 1.0, 0.0, ["cl"], ["clx"])
+    lin("S", T.cl0[:, 1031:1032], T.thf[:], 1.0, 0.0, ["th", "cl"], ["clt"])
     gcp(T.key0[:, 2048:2064], T.key0[:, 0:16], 16, ["key"], ["keyx"])
     gcp(T.em0[:, 2048:2064], T.em0[:, 0:16], 16, ["em"], ["emx"])
-    own = {"cs": ["wm", "wm0", "emb"], "key": ["key", "keyx"], "cl": ["cl", "clx"], "em": ["em", "emx"],
-           "cu": ["cu%d" % i for i in range(4)]}
+    own = {"cs": ["wm"], "key": ["key", "keyx"], "cl": ["cl", "clx", "clt"], "em": ["em", "emx", "eb"], "cu": ["cu0", "cu1"]}
 
     def tab(n, k):
-        return own[n] if k == 0 else [(n, k, c) for c in range(0, 1032, 258)] if n == "cl" else [(n, k)]
+        if k and n == "cl":
+            return [(n, k, c) for c in range(0, 1032, 258)] if form("cu", k, rank) == "cu" else [("cu", k)]
+        return [(n, k)] if k else own[n]
 
-    def send(ways, R, name, first=False):
+    def use(n, t, k):
+        return tab(n, k) + [("due", "cu" if n == "cl" else n)] * (k == 1) if t else [n]
+
+    def send(ways, R, name, first=False, free=False):
         def f():
             return g.remote_dma_fused([
                 RemoteDMATransfer(dst_ids=[DstId(rid=topo.addr(c, core)[0], pnc=topo.addr(c, core)[1])],
                                   dma_engine_mask=sum(1 << e for e in es), remote_sem=T.sem[sem], src=src, dst=dst)
                 for c, dst, src, sem, es in ways], local_sem=T.sem.sent)
-        op("G", CFG["iss"] + CFG["first"] * (name == "akey1"), f, R + ["LG"], ["LG", ("snd", name)], sem="sent",
-           val=sum(len(w[4]) for w in ways), bias=-2000 if first else 0)
+        op("G", CFG["iss"] + CFG["first"] * (name == "a%s1" % CFG["own"][0][1]), f, R + ["LG"] * (not free),
+           ["LF" if free else "LG", ("snd", name)], sem="sent", val=sum(len(w[4]) for w in ways))
 
-    def pass_on(d, dst, src, sem, R, W):
-        send([(at(rank + d), dst, src, sem, topo.engines(core, at(rank + d)))], R, sem)
+    def pass_on(d, dst, src, sem, R, W, free=True):
+        send([(at(rank + d), dst, src, sem, topo.engines(core, at(rank + d)))], R + ["acs"] * free, sem, free=free)
         op("N", 0, None, [("snd", sem)], W, sem=sem, val=len(topo.engines(at(rank - d), core)))
 
     def hand_on(k, n):
         for r in range(rank - NR + 1, rank):
             if (giver(k, r) - rank) % NR == 0:
                 mine = (r + k - rank) % NR
-                dst, src, sem, es = T["%s%d" % (n, k)], T["%s%d" % (n, mine)], "a%s%d" % (n, k), topo.engines(core, at(r))
+                sem, es, m = "a%s%d" % (n, k), topo.engines(core, at(r)), form(n, k, r)
                 if near(rank, r):
-                    send([(at(r), dst[:], src[:], sem, es)], tab(n, mine), sem, k == 1)
-                else:
+                    send([(at(r), tile(m, k), tile(m, mine), sem, es)], tab(m, mine), sem, k == 1)
+                elif not aside(n, k, r):
                     a, b = parts(n, k)
                     rest = [e for e in topo.engines(core, helper(rank)) if e not in es]
-                    send([(c, dst[:, cols], src[:, cols], s, e)
+                    send([(c, tile(m, k, cols), tile(m, mine, cols), s, e)
                           for c, cols, s, e in ((at(r), a, sem, es), (helper(rank), b, "h%s%d" % (n, k), rest)) if some(cols)],
-                         tab(n, mine), sem, k == 1)
+                         tab(m, mine), sem, k == 1)
 
     def unpack(k, n):
         G = ["LG"]
         if n == "cs":
             for e in range(2):
-                gcp(T["wx%d" % k][:, 16 + 112 * e:128 + 128 * e:32], T["cs%d" % k][:, e:8:2], 4,
-                    [("cs", k) if k else "wm", ("wx", k)] + G, [("wx", k, e)] + G)
-        if n == "eb":
-            gcp(T.e0[:, 0:16], T["cs%d" % k][:, 16:32], 16, tab("cs", k) + G, ["e0"] + G)
-            for w in (16, 32, 64):
-                gcp(T.e0[:, w:2 * w], T.e0[:, 0:w], w, ["e0"] + G, ["e0"] + G)
-            inside(T["eb%d" % k][:], "e1", T.e0[:], ["e0"] + G, [("eb", k)] + G)
+                dst, src, R = T["wx%d" % k][:, 16 + 112 * e:128 + 128 * e:32], T.cs[:, k, e:8:2], tab("cs", k) + [("wx", k)]
+                if k:
+                    gcp(dst, src, 4, R + [("sg", NB - 2)], [("wx", k, e)])
+                else:
+                    lin("S", dst, src, 1.0, 0.0, R, [("wx", k, e)])
         if n == "cu":
-            for c in range(0, 1032, 258):
+            m = form(n, k, rank)
+            for c in range(0, 1032 * (m == "cu"), 258):
                 gcp(T["cl%d" % k][:, c:c + 258], T["cu%d" % k][:, c:c + 258], 258, [("cu", k)] + G, [("cl", k, c)] + G)
-            lin("S", T["th%d" % k][:], T["cu%d" % k][:, 1031:1032], -1.0, 0.5, [("cu", k)], [("th", k)])
+        if n == "th":
+            lin("S", T["th%d" % k][:], T[form("cu", k, rank) + str(k)][:, 1031:1032], -256.0, 128.0, [("cu", k), ("sg", NB - 1)],
+                [("th", k)])
 
     def store(dst, src, sem, R):
         op("Y", 80, lambda: Y.dma_start(dst, src), R, (), sem=sem, val=16, lat=1500)
 
-    def repeat(b, i):
-        xr, xs, c, R = T["xr%d" % b], T["xs%d" % i], CUT, [("xs", i), "m16"]
-        scan(xr[:, 0:c], T.m16[:, 0:c], xs[:, 0:c], A.mult, A.add, R, [("xr", b, 0)], c // 2)
-        if seq[0] < CFG["gx"]:
+    def repeat(b, n):
+        xr, xs, c, R = T["xr%d" % b], T[n], CUT, [n, "m16"]
+        for h in range(2):
+            e = slice(c // 2 * h, c // 2 * (h + 1))
+            scan(xr[:, e], T.m16[:, e], xs[:, e], A.mult, A.add, R, [("xr", b, 2 * h)], c // 4)
+        if seq[0] < GX:
             scan(xr[:, c:], T.m16[:, 0:1024 - c], xs[:, c:], A.mult, A.add, R, [("xr", b, 1), ("xo", b)], (1024 - c) // 2)
         else:
             scan(xr[:, c::2], T.m16[:, 0:1024 - c:2], xs[:, c::2], A.mult, A.add, R, [("xr", b, 1)], (1024 - c) // 4)
             gcp(xr[:, c + 1::2], xr[:, c::2], (1024 - c) // 2, [("xr", b, 1)], [("xo", b)])
+
+    def whose(t):
+        return max(t - 1, 0) if CFG["move"] else t % NR
+
+    def tokens(t, TK):
+        return ([(TK, T.wk[:, 3 - i:131 - i], T.oh[:, LB * (NB * t + i):LB * (NB * t + i + 1)], i == 0, i == NB - 1) for i in range(NB)],
+                [("oh", NB * t + i) for i in range(NB)] + ["wk"])
+
+    def tokens_out(t, TK, bank):
+        c, k = slice(LB * t, LB * t + LB), whose(t)
+        act(T.ytb[:, c], TK, F.Copy, ["TK"], [("yt", t)], 64, [bank])
+        if k:
+            pass_on(k, T.ytl[:, c], T.ytb[:, c], "ay%d" % t, [("yt", t)], [("yl", t)])
+        store(T.yt[:, 256 * t:256 * t + 256], T["ytl" if k else "ytb"][0:32, c], "oy%d" % t, [("yl" if k else "yt", t)])
 
     def arrivals(k):
         for i, n in enumerate(PIECES):
@@ -296,27 +368,50 @@ def rank_program(g, core, T, topo):
             val = len(topo.engines(at(frm), core))
             if not near(frm, rank):
                 val = val * some(parts(n, k)[0]) + len(topo.engines(helper(frm), core)) * some(parts(n, k)[1])
-            op("N", 0, None, [("snd", "a%s%d" % (n, k))] * (k == 1), [(n, k)], sem="a%s%d" % (n, k), val=val,
-               lat=CFG["way"][n] if k == 1 else CFG["tab"][k - 2] + CFG["piece"] * i)
+            op("N", 0, None, (), [(n, k)], sem="a%s%d" % (n, k), val=val,
+               lat=CFG["tab"][near(frm, rank)][k - 1] + CFG["piece"] * i)
+            if k == 1:
+                op("N", 0, None, [("snd", "a%s1" % n)], [("due", n)], lat=CFG["way"][n] * (CFG["close"] if near(rank, rank - 1) else 1))
 
-    for h in range(2):
-        lin("S", T.cu0[:, 512 * h:512 * h + 512], T.cl0[:, 512 * h:512 * h + 512], 1.0, 0.0, ["cl"], ["cu%d" % h], 512)
-    lin("S", T.cu0[:, 1024:1031], T.cl0[:, 0:7], 1.0, 0.0, ["cl"], ["cu2"])
-    lin("S", T.cu0[:, 1031:1032], T.thf[:], 1.0, 0.0, ["th"], ["cu3"])
+    for h in range(2 * (form("cu", 1, rank - 1) == "cu")):
+        lin("S", T.cu0[:, 516 * h:516 * h + 516], T.cl0[:, 516 * h:516 * h + 516], 1.0, 0.0, own["cl"][:1 + 2 * h], ["cu%d" % h], 516)
     for k in range(NR):
         if k:
             arrivals(k)
         for what, n in CFG["own" if k == 0 else "other"]:
+            if k and n == "cu" and form(n, k + 1, rank - 1) == "cl":
+                what = {"on": "lay", "lay": "on"}[what]
             if what == "lay":
                 unpack(k, n)
             elif k < NR - 1:
                 hand_on(k + 1, n)
+        for n in CFG["mate"] * (k == 0):
+            if aside(n, 2, rank - 2):
+                m, c = form(n, 2, rank - 2), mate(rank - 2)
+                for h, cols in enumerate(halves(n)):
+                    send([(c, tile(m, 2, cols), tile(m, 0, cols), "m%s%d" % (n, h), topo.engines(core, c))], tab(m, 0), "m")
 
+    for b in range(NB):
+        seq[0], pl, bl = b, "pl%d" % (b > 0), slice(LB * b, LB * b + LB)
+        lin("S" if b else "V", T.LU[:, bl], T.plb[:, bl], 1.0, 0.0, [pl], [("LU", b)])
+        lin("S" if b else "V", T.SP[:, bl], T.plb[:, bl], 1.0, 0.0, [pl], [("LP", b), ("SP", b)])
+        lin("V" if b < 2 else "S", T.xs0[:, 0::16], T.qb[:, bl], 1.0, 0.0, ["q"], [("XS", b), "xs0"])
+        repeat(b, "xs0")
     wrap = False
     for t in range(NT):
-        k = t % NR
+        k, seq[0] = whose(t), None
+        if k:
+            unpack(k, "cs")
+            unpack(k, "th")
         came, wrap = wrap, (rank + k) % NR == NR - 1
-        key, emt, clb, cs, wx, eb = [T["%s%d" % (n, k)] for n in ("key", "em", "cl", "cs", "wx", "eb")]
+        goes, moved = CFG["move"] and t == 0, CFG["move"] and t == 1
+        if moved:
+            came = rank == 0
+            for b in range(NB):
+                seq[0] = NB + b
+                lin("S", T.xs0[:, 0::16], T.MR[:, 128 * b + 64:128 * b + 128], 1.0, 0.0, [("MR", b)], [("XS", b), "xs0"])
+                repeat(b, "xs0")
+        key, emt, clb, wx = [T["%s%d" % (n, k)] for n in ("key", "em", "cl", "wx")]
         for b in range(NB):
             seq[0] = j = t * NB + b
             bA, bB = "a%d" % b, "b%d" % b
@@ -328,92 +423,121 @@ def rank_program(g, core, T, topo):
             sg, cm, LU, SU, SX, vt, sc, eq = [T[n][:, bl] for n in ("sg", "cm", "LU", "SU", "SX", "vt", "sc", "eq")]
             kk, pt, cc = T.kk[0:16, bl], T.at[:, 128 * b:128 * b + 128], T.cc[:, 4 * b:4 * b + 4]
             LP, oh = T.SP[:, LB * j:LB * j + LB], T.oh[:, LB * j:LB * j + LB]
-            x, XR, kP = xr[:, 0::16], [("xr", b, 0), ("xr", b, 1)], ("SP", j)
-            lu = "LU" if t == 0 or came else "SU"
-            if t == 0:
-                pl = "pl%d" % (b > 0)
-                lin("S" if b else "V", LU, T.plb[:, bl], 1.0, 0.0, [pl], [("LU", b)])
-                lin("S" if b else "V", LP, T.plb[:, bl], 1.0, -2048.0, [pl], [("LP", j), kP])
-                lin("S", T.xs0[:, 0::16], T.qb[:, bl], 1.0, 0.0, ["q"], [("xs", 0)])
-                repeat(b, 0)
-            elif came:
-                lin("S", LU, SU, 1.0, 1.0, [("SU", b)], [("LU", b)])
+            x, XR, kP, EG = xr[:, 0::16], [("xr", b, i) for i in range(3)], ("SP", j), [("eg", b, h) for h in range(2)]
+            ptr, lu = (T.MR[:, 128 * b:128 * b + 64], "MR") if moved else (SU, "SU")
+            if goes:
+                SU = T.MV[:, 128 * b:128 * b + 64]
+            if came:
+                lin("S", LU, ptr, 1.0, 1.0, [(lu, b)], [("LU", b)])
+            if t == 0 or came:
+                ptr, lu = LU, "LU"
+            if t:
+                copy(LP, ptr, 64, [(lu, b)], [("LP", j)] * moved + [kP])
             win = key[:, 0:2049] if t else key[:, 0:2048]
-            for h, e in enumerate((slice(0, CUT), slice(CUT, 1024))):
-                off = T[lu][:, LB * b + e.start // 16:LB * b + e.stop // 16]
-                tt(df[:, e], win.indirect(off), xr[:, e], A.subtract,
-                   (tab("key", k) if t else ["key"]) + [(lu, b), XR[h]] + [("xo", b)] * h, [("df", b, h)], (60, e.stop - e.start))
-                act(ad[:, e], df[:, e], F.Abs, [("df", b, h)], [("ad", b, h)], e.stop - e.start)
-            mm([(H, cs[:, 0:16], x, True, True)], XR + (tab("cs", k) if k else ["wm", "wm0"]), [("H", b)], bB)
+            c, R, ahead = CFG["keys"], use("key", t, k) + [(lu, b)], j >= CFG["ahead"]
+            for h, e in enumerate((slice(c[0], c[1]), slice(c[1], c[2]), slice(c[2], c[4]))):
+                X = [XR[1], ("xo", b)] if h else XR[0::2]
+                if h == 2 and ahead:
+                    kg = T.kg[:, 256 * b:256 * b + c[4] - c[2]]
+                    for i in (2, 3):
+                        ts(kg[:, c[i] - c[2]:c[i + 1] - c[2]], win.indirect(ptr[:, c[i] // 16:c[i + 1] // 16]), 256.0, A.add,
+                           R, [("kg", b, i)], (60, c[i + 1] - c[i]))
+                    scan(df[:, e], xr[:, e], kg, A.max, A.subtract, X + [("kg", b, 2), ("kg", b, 3)], [("df", b, h)], (c[4] - c[2]) // 2)
+                else:
+                    tt(df[:, e], win.indirect(ptr[:, e.start // 16:e.stop // 16]), xr[:, e], A.subtract, R + X, [("df", b, h)],
+                       (60, e.stop - e.start))
+            for i in range(4):
+                act(ad[:, c[i]:c[i + 1]], df[:, c[i]:c[i + 1]], F.Abs, [("df", b, min(i, 2))], [("ad", b, i)], c[i + 1] - c[i],
+                    bias=256.0 * (i > 1 and ahead))
+            mm([(H, T.cs[:, k, :], x, True, True)], XR + tab("cs", k) + ["wm0"], [("H", b)], bB)
             lin("S", kk, H, T.ksc[0:16, :], T.kb0[0:16, :], [("H", b), "ksc", "kb0"], [("kk", b)], banks=[bB])
             half = [PA[:, :, 16 * e:16 * e + 16] for e in range(2)]
             for e in range(2):
                 mm([(half[e], T["ih%d" % e][:], LP, e == 0, False), (half[e], wx[:, 128 * e:128 * e + 128], x, False, False),
                     (half[e], T["km%d" % e][0:16, :], kk, False, False)],
                    XR + [kP, ("kk", b), ("ih", e), ("km", e), ("wx", k, e)], [("PA", b)], bB)
-            for h in range(4):
-                mm([(D, T.wd[:, 15 - i:143 - i], ad[:, i::16], i == 0, i == 15) for i in range(4 * h, 4 * h + 4)],
-                   [("ad", b, 0), ("ad", b, 1), "wd"], [("D", b)], bA)
-            act(sg, D, F.Sign, [("D", b), ("th", k)], [("sg", b)], 64, [bA], T["th%d" % k][:])
+            for h in range(8):
+                mm([(D, T.wd[:, 15 - i:143 - i], ad[:, i::16], i == 0, i == 15) for i in (2 * h, 2 * h + 1)],
+                   [("ad", b, i) for i in range(4)] + ["wd"], [("D", b)], bA)
+            act(sg, D, F.Sigmoid, [("D", b), ("th", k)], [("sg", b)], 64, [bA], T["th%d" % k][:], 256.0)
             mm([(half[e], T["sm%d" % e][:], sg, False, e == 1) for e in range(2)], [("sg", b), ("sm", 0), ("sm", 1)], [("PA", b)], bB)
-            mm([(Q, T.idh[:], LP, True, False), (Q, T.n2[:], sg, False, True)], [kP, ("sg", b), "idh", "n2"], [("Q", b)], bA)
-            turn(pt, PA, [("PA", b)], [("at", b)], 128, [bB])
-            unit("V", 256, [lambda i=i, cc=cc, pt=pt: V.tensor_reduce(cc[:, i:i + 1], pt[:, 32 * i:32 * i + 32], AxisListType.X, A.max)
-                            for i in range(4)], [("at", b)], [("cc", b)])
+            tk, R = tokens(t - 1, TK) if t and b == 2 else ([], [])
+            mm([(Q, T.idh[:], LP, True, False), (Q, T.n2[:], sg, False, True)] + tk, [kP, ("sg", b), "idh", "n2"] + R,
+               [("Q", b)] + ["TK"] * bool(tk), bA)
+            for h in range(2):
+                turn(pt[:, 64 * h:64 * h + 64], PA[:, 2 * h:2 * h + 2, :], [("PA", b)], [("at", b, h)], 64, [bB])
+            for h in range(2):
+                unit("V", 128, [lambda i=i, cc=cc, pt=pt: V.tensor_reduce(cc[:, i:i + 1], pt[:, 32 * i:32 * i + 32], AxisListType.X, A.max)
+                                for i in (2 * h, 2 * h + 1)], [("at", b, h)], [("cc", b, h)])
             clw = clb[:, 0:1025] if t else clb[:, 0:1024]
-            tt(cm, clw.indirect(cc), sg, A.mult, [("cc", b), ("sg", b)] + (tab("cl", k) if t else ["cl"]), [("cm", b)], (60, 64))
+            tt(cm, clw.indirect(cc), sg, A.mult, [("cc", b, 0), ("cc", b, 1), ("sg", b)] + use("cl", t, k), [("cm", b)], (60, 64))
             tt(SU, cm, Q, A.max, [("cm", b), ("Q", b)], [("SU", b)], banks=[bA])
-            if t < NT - 1:
-                lin("S", T.SP[:, LB * (j + NB):LB * (j + NB + 1)], SU, 1.0, wrap - 2048.0, [("SU", b)], [("SP", j + NB)])
+            if tk:
+                tokens_out(t - 1, TK, bA)
             mm([(E, T.idb[:], x, True, False)], XR + ["idb"], [("E", b)], bA)
-            emw = emt[:, 0:2049] if t else emt[:, 0:2048]
-            both = j >= NB * NT - CFG["both"]
-            c = 512 if both else CFG["votes"]
-            for h, e in enumerate((slice(0, c), slice(c, 1024))):
-                off = T.SU[:, LB * b + e.start // 16:LB * b + e.stop // 16]
-                R = [("SU", b)] + (tab("em", k) if t else ["em"])
-                if h and both:
-                    cp(eg[:, e], emw.indirect(off), R, [("eg", b, h)], (60, e.stop - e.start))
-                else:
-                    act(eg[:, e], emw.indirect(off), F.Copy, R, [("eg", b, h)], (78, e.stop - e.start))
+            emw, R = emt[:, 0:2049] if t else emt[:, 0:2048], [("SU", b)] + use("em", t, k)
+            both = j >= CFG["both"]
+            if both:
+                act(eg[:, 0:512], emw.indirect(SU[:, 0:32]), F.Copy, R, EG[:1], (78, 512))
+                cp(eg[:, 512:], emw.indirect(SU[:, 32:64]), R, EG[1:], (60, 512))
+            else:
+                c = CFG["votes"]
+                act(eg[:, 0:c], emw.indirect(SU[:, 0:c // 16]), F.Copy, R, EG[:1], (78, c))
+                act(eg[:, c:], emw.indirect(SU[:, c // 16:64]), F.Copy, R, EG[1:], (78, 1024 - c))
             if t == NT - 1:
                 lin("S", T.ip[:, bl], SU, 1.0, float(wrap), [("SU", b)], [("SP", j + NB)])
                 if b % 2:
                     c = slice(LB * (b - 1), LB * (b + 1))
                     ts(T.iq[:, c], T.ip[:, c], 2047, A.bitwise_and, [("SP", j + NB - 1), ("SP", j + NB)], [("iq", b)], 128)
                     gcp(T.SYP[:, c], T.iq[:, c], 2 * LB, [("iq", b)], [("SYP", b)])
-                if b == NB - 1:
+                if b == NB - 1 and CFG["move"]:
+                    store(T.yp[:], T.SYP[:], "op", [("SYP", i) for i in range(1, NB, 2)])
+                elif b == NB - 1:
                     pass_on(1, T.FYP[:], T.SYP[:], "ap", [("SYP", i) for i in range(1, NB, 2)], ["FYP"])
                     store(T.yp[:], T.FYP[:], "op", ["FYP"])
-            for h in range(4):
-                mm([(VT, T.idb[:], eg[:, i::16], i == 0, i == 15) for i in range(4 * h, 4 * h + 4)],
-                   [("eg", b, 0), ("eg", b, 1), "idb"], [("VT", b)], bB)
+            rows, vs, VS = [eg[:, i::16] for i in range(16)], T.vs[:, 512 * (b % 2):512 * (b % 2) + 512], [("vs", b % 2, h) for h in range(2)]
+            if j >= CFG["sum"][1]:
+                for h in range(2):
+                    scan(vs[:, 256 * h:256 * h + 256], T.m16[:, 0:512:2], eg[:, 512 * h + 1:512 * h + 512:2], A.mult, A.add,
+                         [EG[h], "m16"], [VS[h]], 128)
+                rows = rows[0::2] + [vs[:, 7::8]]
+            elif j >= CFG["sum"][0] and j % CFG["every"] == 0:
+                unit("V", 128, [lambda c=c, vs=vs, eg=eg: V.tensor_tensor_scan(
+                    vs[:, c:c + 128], T.m16[:, 0:512:4], eg[:, 4 * c + 3:4 * c + 512:4], 0.0, A.mult, A.add) for c in (0, 128)],
+                    EG + ["m16"], VS)
+                rows = [rows[i] for i in range(16) if i % 4 < 3] + [vs[:, 3:256:4]]
+            for h in range(8):
+                mm([(VT, T.idh[:], rows[i], i == 0, i == len(rows) - 1) for i in range(len(rows) * h // 8, len(rows) * (h + 1) // 8)],
+                   EG + ["idh"] + VS * (h == 7 and len(rows) < 16), [("VT", b)], bB)
             turn(vt, VT, [("VT", b)], [("vt", b)], 64, [bB])
-            scan(sc, T.up[:], vt, A.add, A.max, [("vt", b), "up"], [("sc", b)], 64)
-            scan(SC[:, ::-1], T.dn[:], sc[:, ::-1], A.add, A.max, [("sc", b), "dn"], [("SC", b)], 64, [bA])
-            tt(eq, vt, SC, A.is_equal, [("vt", b), ("SC", b)], [("eq", b)], banks=[bA])
+            scan(sc, T.m16[:, 0:64], vt, A.mult, A.max, [("vt", b), "m16"], [("sc", b)], 64)
+            scan(SC[:, ::-1], T.m16[:, 0:64], vt[:, ::-1], A.mult, A.max, [("vt", b), "m16"], [("SC", b)], 64, [bA])
+            tt(eq, sc, SC, A.is_ge, [("sc", b), ("SC", b)], [("eq", b)], banks=[bA])
             turn(oh, eq, [("eq", b)], [("oh", j)], 64)
-            mm([(E, eb[:], oh, False, True)], [("oh", j), ("eb", k)], [("E", b)], bA)
-            if t < NT - 1:
-                lin("S", T.xs1[:, 0::16], E, 0.5, -0.25, [("E", b)], [("SX", b), ("xs", 1)], banks=[bA])
+            mm([(E, emt[:, 2064:], oh, False, True)], [("oh", j)] + tab("em", k), [("E", b)], bA)
+            if goes:
+                c = slice(128 * b, 128 * b + 128)
+                lin("S", T.MV[:, 128 * b + 64:128 * b + 128], E, 0.5, -0.25, [("E", b)], [("SX", b)], banks=[bA])
+                pass_on(1, T.MR[:, c], T.MV[:, c], "am%d" % b, [("SX", b), ("SU", b)], [("MR", b)], True)
+            elif t < NT - 1:
+                n = "xs%d" % (1 - b % 2)
+                lin("S", T[n][:, 0::16], E, 0.5, -0.25, [("E", b)], [("SX", b), n], banks=[bA])
                 seq[0] = j + NB
-                repeat(b, 1)
+                repeat(b, n)
                 seq[0] = j
             else:
                 lin("S", SX, E, 0.5, XO - 0.25, [("E", b)], [("SX", b)], banks=[bA])
                 lin("S", T.SYQ[:, bl], SX, 1.0, -XO, [("SX", b)], [("SYQ", b)])
                 if b % 2:
                     c, i = slice(LB * (b - 1), LB * (b + 1)), b // 2
-                    pass_on(1, T.FYQ[:, c], T.SYQ[:, c], "aq%d" % i, [("SYQ", b - 1), ("SYQ", b)], [("FYQ", i)])
-                    store(T.yq[:, c], T.FYQ[:, c], "oq%d" % i, [("FYQ", i)])
-            if b == NB - 1:
-                mm([(TK, T.wk[:, 3 - i:131 - i], T.oh[:, LB * (NB * t + i):LB * (NB * t + i + 1)], i == 0, i == NB - 1)
-                    for i in range(NB)], [("oh", NB * t + i) for i in range(NB)] + ["wk"], ["TK"], bA)
-                c = slice(LB * t, LB * t + LB)
-                act(T.ytb[:, c], TK, F.Copy, ["TK"], [("yt", t)], 64, [bA])
-                if k:
-                    pass_on(k, T.ytl[:, c], T.ytb[:, c], "ay%d" % t, [("yt", t)], [("yl", t)])
-                store(T.yt[:, 256 * t:256 * t + 256], T["ytl" if k else "ytb"][0:32, c], "oy%d" % t, [("yl" if k else "yt", t)])
+                    if CFG["move"]:
+                        store(T.yq[:, c], T.SYQ[:, c], "oq%d" % i, [("SYQ", b - 1), ("SYQ", b)])
+                    else:
+                        pass_on(1, T.FYQ[:, c], T.SYQ[:, c], "aq%d" % i, [("SYQ", b - 1), ("SYQ", b)], [("FYQ", i)])
+                        store(T.yq[:, c], T.FYQ[:, c], "oq%d" % i, [("FYQ", i)])
+            if j == NB * NT - 1:
+                mm(*tokens(t, TK), ["TK"], bA)
+                tokens_out(t, TK, bA)
 
     schedule(ops)
     emit_all(ops, {"V": V, "S": S, "P": P, "G": g, "Y": Y}, T, g)
@@ -422,11 +546,19 @@ def rank_program(g, core, T, topo):
 CNT_SEM = {"V": "cv", "S": "cs", "P": "ct", "G": "cg"}
 
 
+def gap(d, o, hop, dma=1.0, soon=1.0):
+    if d["i"] in o["O"]:
+        return 0.0
+    if d["q"] == "N":
+        return d["lat"] * soon + CFG["link"]
+    return dma * d["lat"] + hop[1 if d["q"] == o["q"] else 2 if "G" in (d["q"], o["q"]) else 0]
+
+
 def place(ops, order):
     slots = {q: [] for q in "VSPGY"}
     for i in order:
         o = ops[i]
-        st = max([ops[d]["st"] + ops[d]["dur"] + (0.0 if d in o["O"] else ops[d]["after"]) for d in o["D"]] + [0.0])
+        st = max([ops[d]["st"] + ops[d]["dur"] + gap(ops[d], o, CFG["hop"]) for d in o["D"]] + [0.0])
         if o["q"] != "N":
             sl = slots[o["q"]]
             at, hi = 0, len(sl)
@@ -452,35 +584,34 @@ def schedule(ops):
                 (order if k in ("LG", "LY", "LS") else d).add(lastw[k])
             readers.setdefault(k, []).append(o["i"])
         for k in o["W"]:
-            if k not in ("LG", "LY", "LS"):
+            if k not in ("LG", "LY", "LS", "LF"):
                 if k in lastw:
                     d.add(lastw[k])
                 d.update(readers.get(k, []))
             lastw[k], readers[k] = o["i"], []
         for k in o["banks"]:
-            for q, i in bank.setdefault(k, {}).items():
-                if q != o["q"] or q == "P":
-                    d.add(i)
-            bank[k][o["q"]] = o["i"]
+            q, before, now = bank.get(k, (None, [], []))
+            if q != o["q"]:
+                before, now = now, []
+            d.update(before + now[-1:] * (q == "P"))
+            bank[k] = (o["q"], before, now + [o["i"]])
         d.discard(o["i"])
         if o["q"] == "P":
             order = {i for i in d if ops[i]["q"] == "P"}
         else:
             order -= d
         o["D"], o["O"] = d | order, order
-        o["after"] = o["lat"] + (CFG["link"] if o["q"] == "N" else CFG["hop"])
+        o["after"] = o["lat"] + (CFG["link"] if o["q"] == "N" else CFG["hop"][0])
     n, soft = len(ops), []
-    key = [-o["bias"] if o["bias"] else 1e9 for o in ops]
     for q, turn in CFG["round"].items():
         spot = {kind: lag + at / len(turn) for at, (kind, lag) in enumerate(turn)}
         mine = sorted((o["seq"] + spot[o["kind"]], o["i"]) for o in ops if o["q"] == q and o["kind"] in spot)
-        for (_, a), (_, b) in zip(mine, mine[1:]):
+        mine = [i for v, i in mine if CFG["full"][0] <= v < CFG["full"][1]]
+        for a, b in zip(mine, mine[1:]):
             if a not in ops[b]["D"]:
                 ops[b]["D"].add(a)
                 ops[b]["O"].add(a)
                 soft.append((a, b))
-        for v, i in mine:
-            key[i] = v
     succ, left = [[] for _ in ops], [len(o["D"]) for o in ops]
     for o in ops:
         for d in o["D"]:
@@ -493,9 +624,11 @@ def schedule(ops):
             if not left[s]:
                 todo.append(s)
     assert len(order) == n, "the rounds ask for a call before what it needs"
+    way = [0.0] * n
     for i in reversed(order):
-        key[i] = min([key[i]] + [key[s] - 1e-4 for s in succ[i]])
-    place(ops, sorted(range(n), key=lambda i: key[i]))
+        o = ops[i]
+        way[i] = 1 + o["bias"] + o["dur"] + max([o["after"]] + [way[s] + gap(o, ops[s], CFG["hop"]) for s in succ[i]])
+    place(ops, sorted(range(n), key=lambda i: -way[i]))
     for a, b in soft:
         ops[b]["D"].discard(a)
         ops[b]["O"].discard(a)
@@ -510,8 +643,7 @@ def shorten(ops):
     cases = []
     for f, gam, hop, dma in CFG["cases"]:
         cases.append(([(o["cyc"] + gam * o["gat"]) * (0.83 * f if o["sem"] is None else 1) for o in ops],
-                      [[(d, 0.0 if d in o["O"] else lat[d] + CFG["link"] if q[d] == "N" else dma * lat[d] + hop)
-                        for d in o["D"]] for o in ops]))
+                      [[(d, gap(ops[d], o, hop, dma, CFG["soon"])) for d in o["D"]] for o in ops]))
 
     def times(order, frm, old):
         seen, new = {}, []
@@ -580,6 +712,9 @@ def emit_all(ops, queues, T, g):
     for o in sorted(ops, key=lambda o: (o["st"], o["i"])):
         q = o["q"]
         kn = known[q]
+        if q == "N" and o["sem"] is None:
+            o["tok"] = ("sent", 0)
+            continue
         if q == "N":
             clock[o["i"]] = {o["sem"]: o["val"]}
             total[o["sem"]] = o["val"]

import math
from concourse.mybir import AluOpType, ActivationFunctionType, AxisListType
from concourse.bass import DstId, RemoteDMATransfer

NR, NB, LB, NT = 4, 4, 64, 5
CORES = 256
XO = 1536.0
CFG = {
    "keys": [0, 512, 832, 928, 1024], "ahead": 6,
    "cut": 512, "votes": 704,
    "gx": 4,
    "sum": [99, 18],
    "both": 18,
    "move": False, "pack": [1, 2], "close": 0.6, "every": 1, "late": 2, "mate": [],
    "help": [],
    "round": {
        "V": [("at1", 2), ("df2", 1), ("cc0", 2), ("cc1", 2), ("kg0", -1), ("cm0", 2), ("kg1", -1), ("SU0", 2), ("xr2", 0), ("xr0", 0),
              ("vt0", 3), ("xr1", 0), ("sc0", 3), ("SC0", 3), ("df0", 0), ("eq0", 3), ("df1", 0), ("at0", 1), ("oh0", 3)],
        "S": [("eg0", 2), ("LU0", -2), ("yt0", 2), ("sg0", 1), ("eg1", 2), ("ad0", 0), ("kk0", 0), ("ad1", 0), ("ad2", 0), ("SX0", 3),
              ("ad3", 0)],
        "P": [("VT6", 3), ("VT7", 3), ("D0", 1), ("D1", 1), ("D2", 1), ("D3", 1), ("D4", 1), ("D5", 1), ("D6", 1), ("D7", 1), ("H0", 0),
              ("PA0", 1), ("PA1", 1), ("E0", 2), ("PA2", 1), ("Q0", 1), ("VT0", 2), ("VT1", 2), ("VT2", 2), ("E1", 3), ("VT3", 2),
              ("VT4", 2), ("VT5", 2)],
        "G": [("xo0", 0), ("SP0", 0)]},
    "own": [("on", "cs"), ("lay", "cs"), ("on", "key"), ("on", "cu"), ("on", "em")],
    "other": [("on", "key"), ("on", "cs"), ("on", "cu"), ("lay", "cu"), ("on", "em")],
    "f": 1.05, "gam": 1.56, "hop": [245, 205, 250], "link": 2600, "iss": 700, "first": 2800, "piece": 1000,
    "tab": [[12000, 22000, 0], [7500, 21000, 32000]],
    "way": {"key": 8500, "cs": 3500, "cu": 8000, "em": 10500},
    "cases": [(1.0, 1.56, [250, 200, 250], 1.0), (1.1, 1.2, [250, 210, 260], 1.3), (1.4, 1.9, [240, 200, 250], 1.1),
              (1.2, 1.5, [220, 190, 260], 1.5)],
    "full": [3, 21], "ends": [0.4, 0.78], "tries": 9000, "heat": 40, "soon": 0.85}

SCRATCH = {
    "plb": ("sbuf", [128, 256], "int32"), "qb": ("sbuf", [128, 256], "bfloat16"),
    "wb": ("sbuf", [128, 1], "bfloat16"), "thf": ("sbuf", [128, 1], "float32"),
    "LU": ("sbuf", [128, 256], "uint16"), "SU": ("sbuf", [128, 256], "uint16"),
    "SP": ("sbuf", [128, 1280], "float16"), "SX": ("sbuf", [128, 256], "float16"),
    "SYP": ("sbuf", [128, 256], "float32"), "SYQ": ("sbuf", [128, 256], "bfloat16"),
    "FYP": ("sbuf", [128, 256], "float32"), "FYQ": ("sbuf", [128, 256], "bfloat16"),
    "ip": ("sbuf", [128, 256], "int32"), "iq": ("sbuf", [128, 256], "int32"),
    "xs0": ("sbuf", [128, 1024], "uint16"), "xs1": ("sbuf", [128, 1024], "uint16"),
    "MV": ("sbuf", [128, 512], "uint16"), "MR": ("sbuf", [128, 512], "uint16"), "kg": ("sbuf", [128, 1024], "float16"),
    "ob": ("sbuf", [128, 144], "bfloat16"), "m16": ("sbuf", [128, 640], "bfloat16"), "cs": ("sbuf", [128, NR, 16], "bfloat16"), "emt": ("sbuf", [128, 16], "bfloat16"),
    "vs": ("sbuf", [128, 1024], "float16"),
    "wd": ("sbuf", [128, 144], "bfloat16"), "wk": ("sbuf", [128, 132], "bfloat16"),
    "junk": ("sbuf", [128, 8], "float32"),
    "oh": ("sbuf", [128, 1280], "bfloat16"), "ytb": ("sbuf", [128, 320], "float32"), "ytl": ("sbuf", [128, 320], "float32"),
}
for _k in range(NR):
    SCRATCH.update({"key%d" % _k: ("sbuf", [128, 2064], "bfloat16"), "em%d" % _k: ("sbuf", [128, 2192], "bfloat16"),
                    "cl%d" % _k: ("sbuf", [128, 1032], "int32"), "cu%d" % _k: ("sbuf", [128, 1032], "uint16"),
                    "wx%d" % _k: ("sbuf", [128, 256], "bfloat16"), "th%d" % _k: ("sbuf", [128, 1], "float32")})
for _n in ("m32", "bm0", "bm", "idb", "ub", "p2", "n2", "am", "sm0", "sm1"):
    SCRATCH[_n] = ("sbuf", [128, 128], "bfloat16")
for _n in ("idh", "ih0", "ih1", "km0", "km1"):
    SCRATCH[_n] = ("sbuf", [128, 128], "float16")
for _n in ("kc", "odd", "even", "ksc", "ka", "kb", "kb0", "r8", "m9", "hc", "wf"):
    SCRATCH[_n] = ("sbuf", [128, 1], "float32")
for _n, _s, _d in (("kk", [128, 256], "float16"), ("sg", [128, 256], "bfloat16"),
                   ("at", [128, 512], "float32"), ("cc", [128, 16], "uint16"), ("cm", [128, 256], "float16"),
                   ("vt", [128, 256], "float32"), ("sc", [128, 256], "float32"), ("eq", [128, 256], "bfloat16")):
    SCRATCH[_n] = ("sbuf", _s, _d)
for _b in range(NB):
    SCRATCH.update({
        "xr%d" % _b: ("sbuf", [128, 1024], "bfloat16"), "df%d" % _b: ("sbuf", [128, 1024], "float16"),
        "ad%d" % _b: ("sbuf", [128, 1024], "bfloat16"), "eg%d" % _b: ("sbuf", [128, 1024], "float16"),
        "pa%d" % _b: ("psum", [128, 512], "float32"), "pb%d" % _b: ("psum", [128, 16, 32], "float32"),
    })
PIECES = {"key": 2064, "cs": 8, "cu": 1032, "em": 2192}
STRAIGHT = {("key", 1): 1, ("cu", 1): 0, ("cs", 2): 1}
LOADS = ["pl0", "q", "key", "pl1", "w", "th", "cl", "emb", "em"]
SEMAPHORES = (["cv", "cs", "ct", "cg", "sent"] + ["ld_" + n for n in LOADS]
              + ["%s%s%d" % (a, n, k) for a in "ah" for n in PIECES for k in range(1, NR)]
              + ["op", "oq0", "oq1", "ap", "aq0", "aq1"] + ["oy%d" % t for t in range(NT)] + ["ay%d" % t for t in range(NT)]
              + ["am%d" % b for b in range(NB)] + ["m%s%d" % (n, h) for n in PIECES for h in range(2)])


def rank_program(g, core, T, topo):
    rank = T.rank_of(core)

    def at(r):
        return T.cores[r % NR]

    def near(a, b):
        return at(b) in topo.cores_of(at(a))

    def helper(r):
        return [c for c in topo.cores_of(at(r))
                if topo.die(c) != topo.die(at(r)) and T.rank_of(c) is None and topo.may_write(c, at(r - 1))][0]

    def giver(k, r):
        return r + k if near(r, r + k) else r + 1

    def parts(n, k):
        cut = int(PIECES[n] * STRAIGHT.get((n, k), 0.5))
        return slice(0, cut), slice(cut, PIECES[n])

    def some(c):
        return c.stop > c.start

    def form(n, k, r):
        def far(k, r):
            return k in CFG["pack"] and not near(giver(k, r), r)
        return "cl" if n == "cu" and not (far(k, r) or (giver(k + 1, r - 1) - r) % NR == 0 and far(k + 1, r - 1)) else n

    def tile(n, k, cols=None):
        cols = cols or slice(0, PIECES[n if n != "cl" else "cu"])
        return T.cs[:, k, cols] if n == "cs" else T["%s%d" % (n, k)][:, cols]

    def aside(n, k, r):
        return n in CFG["mate"] and k == 2 and not near(r, r + 1)

    def mate(r):
        return [c for c in range(CORES) if topo.mates(c, at(r)) and topo.die(c) == topo.die(at(r))
                and topo.may_write(at(r + 2), c) and topo.may_write(c, at(r))][0]

    def halves(n):
        return [slice(PIECES[n] // 2 * h, PIECES[n] // 2 * (h + 1)) for h in range(2)]

    if rank is None:
        for r in range(NR):
            if CFG["mate"] and not near(r, r + 1) and core == mate(r):
                rid, pid = topo.addr(at(r), core)
                for n in CFG["mate"]:
                    for h, cols in enumerate(halves(n)):
                        part = tile(form(n, 2, r), 2, cols)
                        g.wait_ge(T.sem["m%s%d" % (n, h)], len(topo.engines(at(r + 2), core)))
                        g.remote_dma(part, part, T.sem["a%s2" % n], T.sem.sent, pid, rid, topo.mask(core, at(r)))
                g.wait_ge(T.sem.sent, 2 * len(CFG["mate"]) * len(topo.engines(core, at(r))))
            if not near(r, r - 1) and core == helper(r):
                rid, pid = topo.addr(at(r - 1), core)
                came = len(topo.engines(at(r), core)) - len(topo.engines(at(r), at(r - 1)))
                far = [(k, n) for k in range(1, NR) for n in PIECES
                       if not near(r - 1, r - 1 + k) and some(parts(n, k)[1]) and not aside(n, k, r - 1)]
                for k, n in far:
                    part = tile(form(n, k, r - 1), k, parts(n, k)[1])
                    g.wait_ge(T.sem["h%s%d" % (n, k)], came)
                    g.remote_dma(part, part, T.sem["a%s%d" % (n, k)], T.sem.sent, pid, rid, topo.mask(core, at(r - 1)))
                g.wait_ge(T.sem.sent, len(far) * len(topo.engines(core, at(r - 1))))
        return
    A, F = AluOpType, ActivationFunctionType
    V, S, P, Y = g.vector, g.scalar, g.tensor, g.sync
    ops, seq, seen, CUT = [], [None], {}, CFG["cut"]
    GX = CFG["gx"] + CFG["late"] * (form("cu", 1, rank) == "cu")

    def op(q, dur, emit, R=(), W=(), banks=(), sem=None, val=1, lat=0, bias=0):
        kind = None
        if seq[0] is not None and q in "VSPG" and not isinstance(W[0], str):
            seen[seq[0], W[0][0]] = seen.get((seq[0], W[0][0]), 0) + 1
            kind = "%s%d" % (W[0][0], seen[seq[0], W[0][0]] - 1)
        cyc, gat = dur if isinstance(dur, tuple) else (dur, 0)
        ops.append({"q": q, "cyc": cyc, "gat": gat, "dur": (cyc + CFG["gam"] * gat) * (0.83 * CFG["f"] if q in "VSP" else 1),
                    "emit": emit, "R": list(R), "W": list(W), "banks": list(banks), "sem": sem, "val": val, "lat": lat,
                    "i": len(ops), "bias": bias, "seq": seq[0], "kind": kind})

    def load(q, name, out, src, done):
        op(q, 80, lambda: (S if q == "S" else Y).dma_start(out, src), ["L" + q], [name, "L" + q], sem="ld_" + name, val=16, lat=done,
           bias=1e7)

    def ts(out, i, s1, a, R, W, n=64):
        op("V", n, lambda: V.tensor_scalar(out, i, s1, None, a), R, W)

    def tt(out, a, b, o, R, W, n=64, banks=()):
        op("V", n, lambda: V.tensor_tensor(out, a, b, o), R, W, banks)

    def cp(out, i, R, W, n=64):
        op("V", n, lambda: V.tensor_copy(out, i), R, W)

    def ms(out, c, W, n=64):
        op("V", n, lambda: V.memset(out, c), (), W)

    def lin(q, out, i, mul, add, R, W, n=64, banks=()):
        if q == "V":
            op("V", n, lambda: V.tensor_scalar(out, i, mul, add, A.mult, A.add), R, W, banks)
        else:
            op("S", n, lambda: S.activation(out, i, F.Identity, bias=add, scale=mul), R, W, banks)

    def scan(out, d0, d1, o0, o1, R, W, n, banks=()):
        op("V", n, lambda: V.tensor_tensor_scan(out, d0, d1, 0.0, o0, o1), R, W, banks)

    def turn(out, i, R, W, n, banks=()):
        op("V", n, lambda: V.transpose(out, i), R, W, banks)

    def act(out, i, f, R, W, n, banks=(), bias=0.0, scale=1.0):
        op("S", n, lambda: S.activation(out, i, f, bias=bias, scale=scale), R, W, banks)

    def unit(q, n, calls, R, W, banks=()):
        def f():
            last = None
            for c in calls:
                last = c()
            return last
        op(q, n, f, R, W, banks)

    def mm(ms_, R, W, bank):
        unit("P", 64 * len(ms_), [lambda m=m: P.matmul(*m) for m in ms_], R, W, [bank])

    def aff(out, src, pat, cmp, base, cm, R, W, n=128, fill=0.0):
        op("G", 205 + 2 * n, lambda: g.affine_select(out, src, pat, cmp, fill, base, cm), R, W)

    def gcp(out, src, n, R, W):
        aff(out, src, [[0, n]], A.is_ge, 0, 0, R, W, n)

    def copy(out, src, n, R, W):
        if seq[0] >= GX:
            gcp(out, src, n, R, W)
        else:
            lin("S", out, src, 1.0, 0.0, R, W)

    def inside(out, tmp, src, R, W):
        aff(T[tmp][:], src, [[-16, 8], [0, 16]], A.is_ge, 0, 1, R, [tmp])
        aff(out, T[tmp][:], [[16, 8], [0, 16]], A.is_ge, 15, -1, [tmp] + [r for r in R if r == "LG"], W)

    load("S", "q", T.qb[:], T.q[:], 1200)
    load("Y", "pl0", T.plb[:, 0:LB], T.pl[:, 0:LB], 1300)
    load("Y", "key", T.key0[:, 0:2048], T.key[:], 2600)
    load("S", "w", T.wb[:], T.w[:], 1600)
    load("Y", "pl1", T.plb[:, LB:], T.pl[:, LB:], 3000)
    load("Y", "th", T.thf[:], T.th[:], 3100)
    load("Y", "emb", T.emt[:], T.emb[:], 3200)
    load("Y", "cl", T.cl0[:, 0:1024], T.cl[:], 4400)
    load("Y", "em", T.em0[:, 0:2048], T.em[:], 5700)

    ms(T.ob[:], 1.0, ["ob"])
    op("S", 1600, lambda: S.activation(T.wd[:], T.ob[:], F.Sigmoid, scale=-256.0), ["ob", "LS"], ["wd"], bias=1e6)
    aff(T.idb[:], T.ob[:, 0:128], [[-1, 128]], A.is_equal, 0, 1, ["ob"], ["idb", "LG"])
    inside(T.bm[:], "bm0", T.ob[:, 0:128], ["ob", "LG"], ["bm", "LG"])
    aff(T.ub[:], T.bm[:], [[1, 128]], A.is_ge, -1, -1, ["bm", "LG"], ["ub", "LG"])
    ms(T.m16[:], 1.0, ["m16"], 320)
    ms(T.m16[:, 0::16], 0.0, ["m16"])
    ms(T.xs0[:], 0, ["xs0"], 512)
    for h in range(2):
        ms(T.xs1[:, 512 * h:512 * h + 512], 0, ["xs1"], 256)
    aff(T.am[:], T.idb[:], [[-1, 128]], A.not_equal, -1, 1, ["idb"], ["am"], fill=-1.0)
    gcp(T.am[:, 15::16], T.idb[:, 15::16], 8, ["idb", "am"], ["am"])

    def total(n, src, mul, add, R):
        op("S", 90, lambda: S.activation(T.junk[:, 0:src.shape[1]], src, F.Identity, bias=add, scale=mul, accum_out=T[n][:]), R, [n, "junk"])

    total("kc", T.idb[:, 15::16], 16.0, -0.125, ["idb"])
    total("even", T.bm[:, 0::32], 0.5, 0.0, ["bm"])
    lin("S", T.odd[:], T.even[:], -1.0, 0.5, ["even"], ["odd"])
    lin("S", T.th0[:], T.thf[:], -256.0, 128.0, ["th"], [("th", 0)])
    lin("S", T.wf[:], T.wb[:], 1.0, 0.0, ["w"], ["wf"])
    cp(T.wd[:, 15:128:16], T.bm[:, 0::16], ["bm"], ["wd"])
    ms(T.wk[:], 0.0, ["wk"], 66)
    lin("S", T.wk[:, 3:35:4], T.bm[:, 0::16], T.kc[:], 0.0, ["bm", "kc"], ["wk"])
    lin("S", T.ksc[:], T.ub[:, 8:9], 2.0 ** -10, 0.0, ["ub"], ["ksc"])
    lin("V", T.r8[:], T.idb[:, 8:9], -1.0, 0.0, ["idb"], ["r8"])
    lin("V", T.m9[:], T.idb[:, 9:10], -4.0, 0.0, ["idb"], ["m9"])
    lin("V", T.ka[:], T.idb[:, 9:10], 0.0625, 0.0, ["idb"], ["ka"])
    lin("V", T.kb[:], T.idb[:, 8:9], 2048.0, T.ka[:], ["idb", "ka"], ["kb"])
    lin("S", T.kb0[:], T.ub[:, 8:9], 1025.0 - 511.5 / 1024, T.kb[:], ["ub", "kb"], ["kb0"])
    lin("V", T.hc[:], T.idb[:, 8:9], 496.5, T.m9[:], ["idb", "m9"], ["hc"])
    lin("V", T.idh[:], T.idb[:], 1.0, 0.0, ["idb"], ["idh"])
    lin("V", T.n2[:], T.idb[:], -4096.0, 0.0, ["idb"], ["n2"])
    lin("V", T.p2[:], T.idb[:], 4096.0, 0.0, ["idb"], ["p2"])
    ms(T.cs[:, :, 8:16], 0.0, ["wm0"])
    lin("S", T.cs[:, 0, 0:8], T.bm[:, 0::16], T.wf[:], 0.0, ["bm", "wf"], ["wm"])
    eb = T.pa3[:, 320:448]
    mm([(eb[:, 16 * i:16 * i + 16], T.am[:], T.emt[:], i == 0, i == 7) for i in range(8)], ["am", "emb"], ["eb0"], "a3")
    tt(T.em0[:, 2064:], eb, T.bm[:], A.mult, ["eb0", "bm"], ["eb"], 128, ["a3"])
    ci = T.pa2[0:16, 320:448]
    mm([(ci, T.ob[:, 0:16], T.ub[:], True, True)], ["ob", "ub"], ["ci"], "a2")
    sm = T.pa0[:, 320:448]
    mm([(sm, T.p2[:], T.ub[:], True, False), (sm, T.n2[:], T.idb[:], False, False),
        (sm[:, 16::32], T.p2[:], T.bm[:, 0::32], False, False), (sm[:, 0::32], T.p2[:], T.bm[:, 16::32], False, True)],
       ["p2", "ub", "n2", "idb", "bm"], ["sm"], "a0")
    for e, c in enumerate(("even", "odd")):
        km = T["km%d" % e]
        lin("S", km[0:16, :], ci, T.r8[0:16, :], T.m9[0:16, :], ["ci", "r8", "m9"], [("km", e)], 128, ["a2"])
        lin("S", km[0:16, 16 - 16 * e::32], T.idb[0:16, e:8:2], -1024.0, T.hc[0:16, :], ["idb", "hc", ("km", e)], [("km", e)])
        lin("S", T["ih%d" % e][:], T.idb[:], T[c][:], 0.0, ["idb", c], [("ih", e)], 128)
        lin("S", T["sm%d" % e][:], sm, T[c][:], 0.0, ["sm", c], [("sm", e)], 128, ["a0"])
    ms(T.wx0[:], 0.0, [("wx", 0)], 128)
    for k in range(1, NR):
        op("G", 670, lambda k=k: g.iota(T["wx%d" % k][:], [[0, 256]], 0, 0, allow_small_or_imprecise_dtypes=True), (), [("wx", k)])
    lin("S", T.cl0[:, 1024:1031], T.cl0[:, 0:7], 1.0, 0.0, ["cl"], ["clx"])
    lin("S", T.cl0[:, 1031:1032], T.thf[:], 1.0, 0.0, ["th", "cl"], ["clt"])
    gcp(T.key0[:, 2048:2064], T.key0[:, 0:16], 16, ["key"], ["keyx"])
    gcp(T.em0[:, 2048:2064], T.em0[:, 0:16], 16, ["em"], ["emx"])
    own = {"cs": ["wm"], "key": ["key", "keyx"], "cl": ["cl", "clx", "clt"], "em": ["em", "emx", "eb"], "cu": ["cu0", "cu1"]}

    def tab(n, k):
        if k and n == "cl":
            return [(n, k, c) for c in range(0, 1032, 258)] if form("cu", k, rank) == "cu" else [("cu", k)]
        return [(n, k)] if k else own[n]

    def use(n, t, k):
        return tab(n, k) + [("due", "cu" if n == "cl" else n)] * (k == 1) if t else [n]

    def send(ways, R, name, first=False, free=False):
        def f():
            return g.remote_dma_fused([
                RemoteDMATransfer(dst_ids=[DstId(rid=topo.addr(c, core)[0], pnc=topo.addr(c, core)[1])],
                                  dma_engine_mask=sum(1 << e for e in es), remote_sem=T.sem[sem], src=src, dst=dst)
                for c, dst, src, sem, es in ways], local_sem=T.sem.sent)
        op("G", CFG["iss"] + CFG["first"] * (name == "a%s1" % CFG["own"][0][1]), f, R + ["LG"] * (not free),
           ["LF" if free else "LG", ("snd", name)], sem="sent", val=sum(len(w[4]) for w in ways))

    def pass_on(d, dst, src, sem, R, W, free=True):
        send([(at(rank + d), dst, src, sem, topo.engines(core, at(rank + d)))], R + ["acs"] * free, sem, free=free)
        op("N", 0, None, [("snd", sem)], W, sem=sem, val=len(topo.engines(at(rank - d), core)))

    def hand_on(k, n):
        for r in range(rank - NR + 1, rank):
            if (giver(k, r) - rank) % NR == 0:
                mine = (r + k - rank) % NR
                sem, es, m = "a%s%d" % (n, k), topo.engines(core, at(r)), form(n, k, r)
                if near(rank, r):
                    send([(at(r), tile(m, k), tile(m, mine), sem, es)], tab(m, mine), sem, k == 1)
                elif not aside(n, k, r):
                    a, b = parts(n, k)
                    rest = [e for e in topo.engines(core, helper(rank)) if e not in es]
                    send([(c, tile(m, k, cols), tile(m, mine, cols), s, e)
                          for c, cols, s, e in ((at(r), a, sem, es), (helper(rank), b, "h%s%d" % (n, k), rest)) if some(cols)],
                         tab(m, mine), sem, k == 1)

    def unpack(k, n):
        G = ["LG"]
        if n == "cs":
            for e in range(2):
                dst, src, R = T["wx%d" % k][:, 16 + 112 * e:128 + 128 * e:32], T.cs[:, k, e:8:2], tab("cs", k) + [("wx", k)]
                if k:
                    gcp(dst, src, 4, R + [("sg", NB - 2)], [("wx", k, e)])
                else:
                    lin("S", dst, src, 1.0, 0.0, R, [("wx", k, e)])
        if n == "cu":
            m = form(n, k, rank)
            for c in range(0, 1032 * (m == "cu"), 258):
                gcp(T["cl%d" % k][:, c:c + 258], T["cu%d" % k][:, c:c + 258], 258, [("cu", k)] + G, [("cl", k, c)] + G)
        if n == "th":
            lin("S", T["th%d" % k][:], T[form("cu", k, rank) + str(k)][:, 1031:1032], -256.0, 128.0, [("cu", k), ("sg", NB - 1)],
                [("th", k)])

    def store(dst, src, sem, R):
        op("Y", 80, lambda: Y.dma_start(dst, src), R, (), sem=sem, val=16, lat=1500)

    def repeat(b, n):
        xr, xs, c, R = T["xr%d" % b], T[n], CUT, [n, "m16"]
        for h in range(2):
            e = slice(c // 2 * h, c // 2 * (h + 1))
            scan(xr[:, e], T.m16[:, e], xs[:, e], A.mult, A.add, R, [("xr", b, 2 * h)], c // 4)
        if seq[0] < GX:
            scan(xr[:, c:], T.m16[:, 0:1024 - c], xs[:, c:], A.mult, A.add, R, [("xr", b, 1), ("xo", b)], (1024 - c) // 2)
        else:
            scan(xr[:, c::2], T.m16[:, 0:1024 - c:2], xs[:, c::2], A.mult, A.add, R, [("xr", b, 1)], (1024 - c) // 4)
            gcp(xr[:, c + 1::2], xr[:, c::2], (1024 - c) // 2, [("xr", b, 1)], [("xo", b)])

    def whose(t):
        return max(t - 1, 0) if CFG["move"] else t % NR

    def tokens(t, TK):
        return ([(TK, T.wk[:, 3 - i:131 - i], T.oh[:, LB * (NB * t + i):LB * (NB * t + i + 1)], i == 0, i == NB - 1) for i in range(NB)],
                [("oh", NB * t + i) for i in range(NB)] + ["wk"])

    def tokens_out(t, TK, bank):
        c, k = slice(LB * t, LB * t + LB), whose(t)
        act(T.ytb[:, c], TK, F.Copy, ["TK"], [("yt", t)], 64, [bank])
        if k:
            pass_on(k, T.ytl[:, c], T.ytb[:, c], "ay%d" % t, [("yt", t)], [("yl", t)])
        store(T.yt[:, 256 * t:256 * t + 256], T["ytl" if k else "ytb"][0:32, c], "oy%d" % t, [("yl" if k else "yt", t)])

    def arrivals(k):
        for i, n in enumerate(PIECES):
            frm = giver(k, rank)
            val = len(topo.engines(at(frm), core))
            if not near(frm, rank):
                val = val * some(parts(n, k)[0]) + len(topo.engines(helper(frm), core)) * some(parts(n, k)[1])
            op("N", 0, None, (), [(n, k)], sem="a%s%d" % (n, k), val=val,
               lat=CFG["tab"][near(frm, rank)][k - 1] + CFG["piece"] * i)
            if k == 1:
                op("N", 0, None, [("snd", "a%s1" % n)], [("due", n)], lat=CFG["way"][n] * (CFG["close"] if near(rank, rank - 1) else 1))

    for h in range(2 * (form("cu", 1, rank - 1) == "cu")):
        lin("S", T.cu0[:, 516 * h:516 * h + 516], T.cl0[:, 516 * h:516 * h + 516], 1.0, 0.0, own["cl"][:1 + 2 * h], ["cu%d" % h], 516)
    for k in range(NR):
        if k:
            arrivals(k)
        for what, n in CFG["own" if k == 0 else "other"]:
            if k and n == "cu" and form(n, k + 1, rank - 1) == "cl":
                what = {"on": "lay", "lay": "on"}[what]
            if what == "lay":
                unpack(k, n)
            elif k < NR - 1:
                hand_on(k + 1, n)
        for n in CFG["mate"] * (k == 0):
            if aside(n, 2, rank - 2):
                m, c = form(n, 2, rank - 2), mate(rank - 2)
                for h, cols in enumerate(halves(n)):
                    send([(c, tile(m, 2, cols), tile(m, 0, cols), "m%s%d" % (n, h), topo.engines(core, c))], tab(m, 0), "m")

    for b in range(NB):
        seq[0], pl, bl = b, "pl%d" % (b > 0), slice(LB * b, LB * b + LB)
        lin("S" if b else "V", T.LU[:, bl], T.plb[:, bl], 1.0, 0.0, [pl], [("LU", b)])
        lin("S" if b else "V", T.SP[:, bl], T.plb[:, bl], 1.0, 0.0, [pl], [("LP", b), ("SP", b)])
        lin("V" if b < 2 else "S", T.xs0[:, 0::16], T.qb[:, bl], 1.0, 0.0, ["q"], [("XS", b), "xs0"])
        repeat(b, "xs0")
    wrap = False
    for t in range(NT):
        k, seq[0] = whose(t), None
        if k:
            unpack(k, "cs")
            unpack(k, "th")
        came, wrap = wrap, (rank + k) % NR == NR - 1
        goes, moved = CFG["move"] and t == 0, CFG["move"] and t == 1
        if moved:
            came = rank == 0
            for b in range(NB):
                seq[0] = NB + b
                lin("S", T.xs0[:, 0::16], T.MR[:, 128 * b + 64:128 * b + 128], 1.0, 0.0, [("MR", b)], [("XS", b), "xs0"])
                repeat(b, "xs0")
        key, emt, clb, wx = [T["%s%d" % (n, k)] for n in ("key", "em", "cl", "wx")]
        for b in range(NB):
            seq[0] = j = t * NB + b
            bA, bB = "a%d" % b, "b%d" % b
            pa, pb = T["pa%d" % b], T["pb%d" % b]
            D, Q, E, TK, SC = [pa[:, 64 * i:64 * i + 64] for i in range(5)]
            H, PA, VT = pb[0:16, 0:2, :], pb[:, 2:6, :], pb[:, 6:8, :]
            xr, df, ad, eg = [T["%s%d" % (n, b)] for n in ("xr", "df", "ad", "eg")]
            bl = slice(LB * b, LB * b + LB)
            sg, cm, LU, SU, SX, vt, sc, eq = [T[n][:, bl] for n in ("sg", "cm", "LU", "SU", "SX", "vt", "sc", "eq")]
            kk, pt, cc = T.kk[0:16, bl], T.at[:, 128 * b:128 * b + 128], T.cc[:, 4 * b:4 * b + 4]
            LP, oh = T.SP[:, LB * j:LB * j + LB], T.oh[:, LB * j:LB * j + LB]
            x, XR, kP, EG = xr[:, 0::16], [("xr", b, i) for i in range(3)], ("SP", j), [("eg", b, h) for h in range(2)]
            ptr, lu = (T.MR[:, 128 * b:128 * b + 64], "MR") if moved else (SU, "SU")
            if goes:
                SU = T.MV[:, 128 * b:128 * b + 64]
            if came:
                lin("S", LU, ptr, 1.0, 1.0, [(lu, b)], [("LU", b)])
            if t == 0 or came:
                ptr, lu = LU, "LU"
            if t:
                copy(LP, ptr, 64, [(lu, b)], [("LP", j)] * moved + [kP])
            win = key[:, 0:2049] if t else key[:, 0:2048]
            c, R, ahead = CFG["keys"], use("key", t, k) + [(lu, b)], j >= CFG["ahead"]
            for h, e in enumerate((slice(c[0], c[1]), slice(c[1], c[2]), slice(c[2], c[4]))):
                X = [XR[1], ("xo", b)] if h else XR[0::2]
                if h == 2 and ahead:
                    kg = T.kg[:, 256 * b:256 * b + c[4] - c[2]]
                    for i in (2, 3):
                        ts(kg[:, c[i] - c[2]:c[i + 1] - c[2]], win.indirect(ptr[:, c[i] // 16:c[i + 1] // 16]), 256.0, A.add,
                           R, [("kg", b, i)], (60, c[i + 1] - c[i]))
                    scan(df[:, e], xr[:, e], kg, A.max, A.subtract, X + [("kg", b, 2), ("kg", b, 3)], [("df", b, h)], (c[4] - c[2]) // 2)
                else:
                    tt(df[:, e], win.indirect(ptr[:, e.start // 16:e.stop // 16]), xr[:, e], A.subtract, R + X, [("df", b, h)],
                       (60, e.stop - e.start))
            for i in range(4):
                act(ad[:, c[i]:c[i + 1]], df[:, c[i]:c[i + 1]], F.Abs, [("df", b, min(i, 2))], [("ad", b, i)], c[i + 1] - c[i],
                    bias=256.0 * (i > 1 and ahead))
            mm([(H, T.cs[:, k, :], x, True, True)], XR + tab("cs", k) + ["wm0"], [("H", b)], bB)
            lin("S", kk, H, T.ksc[0:16, :], T.kb0[0:16, :], [("H", b), "ksc", "kb0"], [("kk", b)], banks=[bB])
            half = [PA[:, :, 16 * e:16 * e + 16] for e in range(2)]
            for e in range(2):
                mm([(half[e], T["ih%d" % e][:], LP, e == 0, False), (half[e], wx[:, 128 * e:128 * e + 128], x, False, False),
                    (half[e], T["km%d" % e][0:16, :], kk, False, False)],
                   XR + [kP, ("kk", b), ("ih", e), ("km", e), ("wx", k, e)], [("PA", b)], bB)
            for h in range(8):
                mm([(D, T.wd[:, 15 - i:143 - i], ad[:, i::16], i == 0, i == 15) for i in (2 * h, 2 * h + 1)],
                   [("ad", b, i) for i in range(4)] + ["wd"], [("D", b)], bA)
            act(sg, D, F.Sigmoid, [("D", b), ("th", k)], [("sg", b)], 64, [bA], T["th%d" % k][:], 256.0)
            mm([(half[e], T["sm%d" % e][:], sg, False, e == 1) for e in range(2)], [("sg", b), ("sm", 0), ("sm", 1)], [("PA", b)], bB)
            tk, R = tokens(t - 1, TK) if t and b == 2 else ([], [])
            mm([(Q, T.idh[:], LP, True, False), (Q, T.n2[:], sg, False, True)] + tk, [kP, ("sg", b), "idh", "n2"] + R,
               [("Q", b)] + ["TK"] * bool(tk), bA)
            for h in range(2):
                turn(pt[:, 64 * h:64 * h + 64], PA[:, 2 * h:2 * h + 2, :], [("PA", b)], [("at", b, h)], 64, [bB])
            for h in range(2):
                unit("V", 128, [lambda i=i, cc=cc, pt=pt: V.tensor_reduce(cc[:, i:i + 1], pt[:, 32 * i:32 * i + 32], AxisListType.X, A.max)
                                for i in (2 * h, 2 * h + 1)], [("at", b, h)], [("cc", b, h)])
            clw = clb[:, 0:1025] if t else clb[:, 0:1024]
            tt(cm, clw.indirect(cc), sg, A.mult, [("cc", b, 0), ("cc", b, 1), ("sg", b)] + use("cl", t, k), [("cm", b)], (60, 64))
            tt(SU, cm, Q, A.max, [("cm", b), ("Q", b)], [("SU", b)], banks=[bA])
            if tk:
                tokens_out(t - 1, TK, bA)
            mm([(E, T.idb[:], x, True, False)], XR + ["idb"], [("E", b)], bA)
            emw, R = emt[:, 0:2049] if t else emt[:, 0:2048], [("SU", b)] + use("em", t, k)
            both = j >= CFG["both"]
            if both:
                act(eg[:, 0:512], emw.indirect(SU[:, 0:32]), F.Copy, R, EG[:1], (78, 512))
                cp(eg[:, 512:], emw.indirect(SU[:, 32:64]), R, EG[1:], (60, 512))
            else:
                c = CFG["votes"]
                act(eg[:, 0:c], emw.indirect(SU[:, 0:c // 16]), F.Copy, R, EG[:1], (78, c))
                act(eg[:, c:], emw.indirect(SU[:, c // 16:64]), F.Copy, R, EG[1:], (78, 1024 - c))
            if t == NT - 1:
                lin("S", T.ip[:, bl], SU, 1.0, float(wrap), [("SU", b)], [("SP", j + NB)])
                if b % 2:
                    c = slice(LB * (b - 1), LB * (b + 1))
                    ts(T.iq[:, c], T.ip[:, c], 2047, A.bitwise_and, [("SP", j + NB - 1), ("SP", j + NB)], [("iq", b)], 128)
                    gcp(T.SYP[:, c], T.iq[:, c], 2 * LB, [("iq", b)], [("SYP", b)])
                if b == NB - 1 and CFG["move"]:
                    store(T.yp[:], T.SYP[:], "op", [("SYP", i) for i in range(1, NB, 2)])
                elif b == NB - 1:
                    pass_on(1, T.FYP[:], T.SYP[:], "ap", [("SYP", i) for i in range(1, NB, 2)], ["FYP"])
                    store(T.yp[:], T.FYP[:], "op", ["FYP"])
            rows, vs, VS = [eg[:, i::16] for i in range(16)], T.vs[:, 512 * (b % 2):512 * (b % 2) + 512], [("vs", b % 2, h) for h in range(2)]
            if j >= CFG["sum"][1]:
                for h in range(2):
                    scan(vs[:, 256 * h:256 * h + 256], T.m16[:, 0:512:2], eg[:, 512 * h + 1:512 * h + 512:2], A.mult, A.add,
                         [EG[h], "m16"], [VS[h]], 128)
                rows = rows[0::2] + [vs[:, 7::8]]
            elif j >= CFG["sum"][0] and j % CFG["every"] == 0:
                unit("V", 128, [lambda c=c, vs=vs, eg=eg: V.tensor_tensor_scan(
                    vs[:, c:c + 128], T.m16[:, 0:512:4], eg[:, 4 * c + 3:4 * c + 512:4], 0.0, A.mult, A.add) for c in (0, 128)],
                    EG + ["m16"], VS)
                rows = [rows[i] for i in range(16) if i % 4 < 3] + [vs[:, 3:256:4]]
            for h in range(8):
                mm([(VT, T.idh[:], rows[i], i == 0, i == len(rows) - 1) for i in range(len(rows) * h // 8, len(rows) * (h + 1) // 8)],
                   EG + ["idh"] + VS * (h == 7 and len(rows) < 16), [("VT", b)], bB)
            turn(vt, VT, [("VT", b)], [("vt", b)], 64, [bB])
            scan(sc, T.m16[:, 0:64], vt, A.mult, A.max, [("vt", b), "m16"], [("sc", b)], 64)
            scan(SC[:, ::-1], T.m16[:, 0:64], vt[:, ::-1], A.mult, A.max, [("vt", b), "m16"], [("SC", b)], 64, [bA])
            tt(eq, sc, SC, A.is_ge, [("sc", b), ("SC", b)], [("eq", b)], banks=[bA])
            turn(oh, eq, [("eq", b)], [("oh", j)], 64)
            mm([(E, emt[:, 2064:], oh, False, True)], [("oh", j)] + tab("em", k), [("E", b)], bA)
            if goes:
                c = slice(128 * b, 128 * b + 128)
                lin("S", T.MV[:, 128 * b + 64:128 * b + 128], E, 0.5, -0.25, [("E", b)], [("SX", b)], banks=[bA])
                pass_on(1, T.MR[:, c], T.MV[:, c], "am%d" % b, [("SX", b), ("SU", b)], [("MR", b)], True)
            elif t < NT - 1:
                n = "xs%d" % (1 - b % 2)
                lin("S", T[n][:, 0::16], E, 0.5, -0.25, [("E", b)], [("SX", b), n], banks=[bA])
                seq[0] = j + NB
                repeat(b, n)
                seq[0] = j
            else:
                lin("S", SX, E, 0.5, XO - 0.25, [("E", b)], [("SX", b)], banks=[bA])
                lin("S", T.SYQ[:, bl], SX, 1.0, -XO, [("SX", b)], [("SYQ", b)])
                if b % 2:
                    c, i = slice(LB * (b - 1), LB * (b + 1)), b // 2
                    if CFG["move"]:
                        store(T.yq[:, c], T.SYQ[:, c], "oq%d" % i, [("SYQ", b - 1), ("SYQ", b)])
                    else:
                        pass_on(1, T.FYQ[:, c], T.SYQ[:, c], "aq%d" % i, [("SYQ", b - 1), ("SYQ", b)], [("FYQ", i)])
                        store(T.yq[:, c], T.FYQ[:, c], "oq%d" % i, [("FYQ", i)])
            if j == NB * NT - 1:
                mm(*tokens(t, TK), ["TK"], bA)
                tokens_out(t, TK, bA)

    schedule(ops)
    emit_all(ops, {"V": V, "S": S, "P": P, "G": g, "Y": Y}, T, g)


CNT_SEM = {"V": "cv", "S": "cs", "P": "ct", "G": "cg"}


def gap(d, o, hop, dma=1.0, soon=1.0):
    if d["i"] in o["O"]:
        return 0.0
    if d["q"] == "N":
        return d["lat"] * soon + CFG["link"]
    return dma * d["lat"] + hop[1 if d["q"] == o["q"] else 2 if "G" in (d["q"], o["q"]) else 0]


def place(ops, order):
    slots = {q: [] for q in "VSPGY"}
    for i in order:
        o = ops[i]
        st = max([ops[d]["st"] + ops[d]["dur"] + gap(ops[d], o, CFG["hop"]) for d in o["D"]] + [0.0])
        if o["q"] != "N":
            sl = slots[o["q"]]
            at, hi = 0, len(sl)
            while at < hi:
                mid = (at + hi) // 2
                if sl[mid][1] > st:
                    hi = mid
                else:
                    at = mid + 1
            while at < len(sl) and sl[at][0] < st + o["dur"]:
                st = max(st, sl[at][1])
                at += 1
            sl.insert(at, (st, st + o["dur"]))
        o["st"], o["end"] = st, st + o["dur"] + o["after"]


def schedule(ops):
    lastw, readers, bank = {}, {}, {}
    for o in ops:
        d, order = set(), set()
        for k in o["R"]:
            if k in lastw:
                (order if k in ("LG", "LY", "LS") else d).add(lastw[k])
            readers.setdefault(k, []).append(o["i"])
        for k in o["W"]:
            if k not in ("LG", "LY", "LS", "LF"):
                if k in lastw:
                    d.add(lastw[k])
                d.update(readers.get(k, []))
            lastw[k], readers[k] = o["i"], []
        for k in o["banks"]:
            q, before, now = bank.get(k, (None, [], []))
            if q != o["q"]:
                before, now = now, []
            d.update(before + now[-1:] * (q == "P"))
            bank[k] = (o["q"], before, now + [o["i"]])
        d.discard(o["i"])
        if o["q"] == "P":
            order = {i for i in d if ops[i]["q"] == "P"}
        else:
            order -= d
        o["D"], o["O"] = d | order, order
        o["after"] = o["lat"] + (CFG["link"] if o["q"] == "N" else CFG["hop"][0])
    n, soft = len(ops), []
    for q, turn in CFG["round"].items():
        spot = {kind: lag + at / len(turn) for at, (kind, lag) in enumerate(turn)}
        mine = sorted((o["seq"] + spot[o["kind"]], o["i"]) for o in ops if o["q"] == q and o["kind"] in spot)
        mine = [i for v, i in mine if CFG["full"][0] <= v < CFG["full"][1]]
        for a, b in zip(mine, mine[1:]):
            if a not in ops[b]["D"]:
                ops[b]["D"].add(a)
                ops[b]["O"].add(a)
                soft.append((a, b))
    succ, left = [[] for _ in ops], [len(o["D"]) for o in ops]
    for o in ops:
        for d in o["D"]:
            succ[d].append(o["i"])
    order, todo = [], [i for i in range(n) if not left[i]]
    while todo:
        order.append(todo.pop())
        for s in succ[order[-1]]:
            left[s] -= 1
            if not left[s]:
                todo.append(s)
    assert len(order) == n, "the rounds ask for a call before what it needs"
    way = [0.0] * n
    for i in reversed(order):
        o = ops[i]
        way[i] = 1 + o["bias"] + o["dur"] + max([o["after"]] + [way[s] + gap(o, ops[s], CFG["hop"]) for s in succ[i]])
    place(ops, sorted(range(n), key=lambda i: -way[i]))
    for a, b in soft:
        ops[b]["D"].discard(a)
        ops[b]["O"].discard(a)
    if CFG["tries"]:
        shorten(ops)


def shorten(ops):
    n = len(ops)
    q, need = [o["q"] for o in ops], [o["D"] for o in ops]
    lat = [o["lat"] * (CFG["soon"] if o["q"] == "N" else 1) for o in ops]
    cases = []
    for f, gam, hop, dma in CFG["cases"]:
        cases.append(([(o["cyc"] + gam * o["gat"]) * (0.83 * f if o["sem"] is None else 1) for o in ops],
                      [[(d, gap(ops[d], o, hop, dma, CFG["soon"])) for d in o["D"]] for o in ops]))

    def times(order, frm, old):
        seen, new = {}, []
        for i in reversed(order[:frm]):
            if q[i] not in seen:
                seen[q[i]] = i
                if len(seen) == 6:
                    break
        rest = order[frm:]
        for (dur, pred), (_, end, why) in zip(cases, old):
            end, why, last = end[:], why[:], dict(seen)
            for i in rest:
                p = last.get(q[i], -1) if q[i] != "N" else -1
                st, w = (end[p], -2 - p) if p >= 0 else (0.0, -1)
                for d, gap in pred[i]:
                    if end[d] + gap > st:
                        st, w = end[d] + gap, d
                end[i], why[i], last[q[i]] = st + dur[i], w, i
            new.append((max((end[i] + lat[i], i) for i in final), end, why))
        return new

    final = [i for i in range(n) if q[i] == "Y"]
    order = [o["i"] for o in sorted(ops, key=lambda o: (o["st"], o["i"]))]
    now = times(order, 0, [(0, [0.0] * n, [-1] * n)] * len(cases))
    weight = [now[0][0][0] / c[0][0] / len(cases) for c in now]

    def total(got):
        return sum(w * c[0][0] for w, c in zip(weight, got))

    best, x, pairs = (total(now), now), 12345, None
    for turn in range(CFG["tries"]):
        if pairs is None:
            pairs = []
            for (_, i), end, why in now:
                while i >= 0:
                    if why[i] <= -2 and not CFG["ends"][0] < end[i] / end[final[-1]] < CFG["ends"][1]:
                        pairs.append((-2 - why[i], i))
                    i = -2 - why[i] if why[i] <= -2 else why[i]
        x = (x * 1103515245 + 12345) % 2 ** 31
        a, b = pairs[(x >> 8) % len(pairs)]
        ia, ib = order.index(a), order.index(b)
        front, rest, qs = [b], [], {q[b]}
        for i in reversed(order[ia:ib]):
            if (q[i] in qs and q[i] != "N" and i != a) or any(i in need[j] for j in front):
                front.append(i)
                qs.add(q[i])
            else:
                rest.append(i)
        if front[-1] == a:
            continue
        new = order[:ia] + front[::-1] + rest[::-1] + order[ib + 1:]
        got = times(new, ia, now)
        x = (x * 1103515245 + 12345) % 2 ** 31
        heat = CFG["heat"] * (1 - turn / CFG["tries"]) + 1
        if total(got) - total(now) <= -heat * math.log((x + 1) / 2 ** 31):
            order, now, pairs = new, got, None
            if total(now) < best[0]:
                best = (total(now), now)
    for o in ops:
        o["st"] = best[1][0][1][o["i"]] - cases[0][0][o["i"]]
        o["end"] = best[1][0][1][o["i"]] + o["after"]


def emit_all(ops, queues, T, g):
    count, known, total, clock = {}, {q: {} for q in "VSPGYN"}, {}, {}
    for o in sorted(ops, key=lambda o: (o["st"], o["i"])):
        q = o["q"]
        kn = known[q]
        if q == "N" and o["sem"] is None:
            o["tok"] = ("sent", 0)
            continue
        if q == "N":
            clock[o["i"]] = {o["sem"]: o["val"]}
            total[o["sem"]] = o["val"]
            o["tok"] = (o["sem"], o["val"])
            continue
        eng = queues[q]
        for d in sorted((ops[i] for i in o["D"] - o["O"]), key=lambda x: -x["end"]):
            s, v = d["tok"]
            if kn.get(s, 0) >= v:
                continue
            eng.wait_ge(T.sem[s], v)
            for a, w in clock[d["i"]].items():
                if kn.get(a, 0) < w:
                    kn[a] = w
        ins = o["emit"]()
        if o["sem"] == "sent":
            total["sent"] = total.get("sent", 0) + o["val"]
            o["tok"] = ("sent", 0)
            clock[o["i"]] = {}
            continue
        if o["sem"] is not None:
            ins.then_inc(T.sem[o["sem"]], o["val"])
            s, v = o["sem"], o["val"]
        else:
            s = CNT_SEM[q]
            count[s] = count.get(s, 0) + 1
            v = count[s]
            ins.then_inc(T.sem[s], 1)
        total[s] = v
        o["tok"] = (s, v)
        ck = dict(kn)
        ck[s] = v
        clock[o["i"]] = ck
    for s, v in sorted(total.items()):
        g.wait_ge(T.sem[s], v)
